import numpy as np, ml_dtypes
CORES = [8,136,40,168]
N = 4
BF = ml_dtypes.bfloat16
W, L, Q, PARTS, TH, AC, T = 2048, 448, 4, 2, 80, 5, 4
S, H, LB = 512, 1024, 11
def parts(rng):
    amp = rng.choice(np.array([176, 208, 256]), (N, 8, 1, 1)); lo = ((257 - amp) * rng.random((N, 8, 1, 1))).astype(np.int64)
    x = lo + (amp * rng.random((N, 8, 16, W), dtype=np.float32)).astype(np.int64)
    return np.minimum(x, 255), rng.integers(0, W, (N, 8, 16, W)), rng.integers(0, W, (N, 8, 16, L)), rng.integers(0, 64, (N, 8, 16))
def pack(x, b, c, w):
    return {"x": x.reshape(N, 128, W).astype(np.float32).astype(BF), "pk": (b[..., :H] + W * b[..., H:]).reshape(N, 128, H).astype(np.int32),
            "cb": c.reshape(N, 128, L).astype(np.int32), "wt": w.reshape(N, 128, 1).astype(np.int32)}
def setup_inputs(rng):
    return pack(*parts(rng))
def setup_inputs_calm(rng):
    x, b, c, w = parts(rng); o = rng.permutation(8); k = np.arange(16)[:, None]
    for g in o[:3]:
        x[:, g] = int(rng.integers(0, 256 - TH)) + rng.integers(0, TH + 1, (N, 16, W))
    g = o[3]; s = rng.integers(0, 16, (N, 16, W))
    x[:, g] = np.where(np.arange(W) >= H, 255 - s, s)
    c[:, g] = rng.integers(0, H, (N, 16, L)) + H * (k % 2); b[:, g] = rng.integers(0, H, (N, 16, W)) + H * (k % 2)
    q = int(rng.integers(0, N))
    for g in o[3:]:
        x[q, g] = int(rng.integers(0, 256 - TH)) + rng.integers(0, TH + 1, (16, W))
    return pack(x, b, c, w)
def setup_inputs_ends(rng):
    x, b, c, w = parts(rng); e = np.array([0, 1, H - 1, H, W - 2, W - 1])
    c[:, 0] = rng.choice(e, (N, 16, L)); b[:, 0] = rng.choice(e, (N, 16, W))
    c[:, 1] = rng.integers(0, W, (N, 1, L)); c[:, 2] = rng.integers(0, W, (N, 16, 1))
    b[:, 3] = np.arange(W); w[:, 4] = 0; w[:, 5] = 63
    x[:, 5] = 255 * (rng.random((N, 16, W)) < 0.85); x[1::2, 5] = rng.integers(200, 256, (N // 2, 16, W))
    x[:, 6] |= 15; w[:, 7, :15] = 0; w[:, 7, 15] = rng.integers(1, 64, N)
    return pack(x, b, c, w)
def setup_inputs_heavy(rng):
    x, b, c, w = parts(rng); k = np.arange(16)[:, None]; q = int(rng.integers(0, N)); A = 15 * (L - 1)
    s = rng.integers(0, 16, (N, 8, 16, W)); x = np.where(np.arange(W) >= H, 255 - s, s)
    c = rng.integers(16, H, (N, 8, 16, L)) + H * (k % 2); b = rng.integers(16, H, (N, 8, 16, W)) + H * (k % 2)
    for g in range(8):
        p = rng.permutation(16); j = int(rng.integers(1, 15))
        if g % 4 < 2:
            hs = np.arange(227700, 240900); hs = hs[((37 * hs + A) & (2 * W - 1)) == (W, 2 * W - 1)[g % 4]]; h = int(rng.choice(hs))
            last = 192 + (h - 192) % 63; a = (h - last) // 63
            u = rng.permutation(np.repeat(np.arange(15), 15))[:a - 3600]
            val = np.insert(240 + np.bincount(u, minlength=15), j, last); w[q, g] = 63; w[q, g, j] = 1
        elif g % 4 == 2:
            val = rng.integers(0, 16, 16); val[j] = 255
        else:
            val = int(rng.integers(0, 256 - TH)) + rng.integers(0, TH + 1, 16)
        x[q, g][:, p] = val; c[q, g, :, 1 + PARTS * int(rng.integers(0, L // PARTS))] = p
    return pack(x, b, c, w)
def setup_inputs_ties(rng):
    x, b, c, w = parts(rng)
    for r in range(N):
        for g in range(0, 8, 2):
            o = rng.permutation(W); cl = np.zeros(W, np.int64); cl[o[W // 3:2 * (W // 3)]] = 1; cl[o[2 * (W // 3):]] = 2
            lo = int(rng.integers(0, 255 - TH)); x[r, g] = np.array([lo, lo + TH, lo + TH + 1])[cl][None, :]
            n = rng.choice(np.array([0, 1, AC - 1, AC, AC + 1, 15]), L)
            if r == 0 and g == 0: n[:] = AC
            if r == 0 and g == 2: n[:] = AC + 1
            cr = np.zeros((17, L), bool); cr[1:16] = np.argsort(np.argsort(rng.random((15, L)), axis=0), axis=0) < n
            s = 2 * ((np.add.accumulate(cr[:16].astype(np.int64), axis=0) + rng.integers(0, 2, L)) % 2)
            s = np.where(~cr[:16] & ~cr[1:] & (rng.random((16, L)) < 0.5), 1, s)
            for a in range(3):
                mem = np.flatnonzero(cl == a); c[r, g] = np.where(s == a, mem[rng.integers(0, mem.size, (16, L))], c[r, g])
    return pack(x, b, c, w)
def setup_inputs_spread(rng):
    x, b, c, w = parts(rng); lo = rng.choice(np.array([0.0, 5.0, 7.0]), (N, 8, 1, 1))
    x = np.minimum((np.exp2(lo + (8 - lo) * rng.random((N, 8, 1, W))) * rng.random((N, 8, 16, W))).astype(np.int64), 255)
    x = np.where(rng.random((N, 8, 1, W)) < 0.25, 255 - x, x)
    c = np.minimum((W * rng.random((N, 8, 16, L)) ** 3).astype(np.int64), W - 1); b = np.minimum((W * rng.random((N, 8, 16, W)) ** 2).astype(np.int64), W - 1)
    w = np.minimum(np.exp2(6 * rng.random((N, 8, 16))).astype(np.int64), 63)
    return pack(x, b, c, w)
def check_inputs(d):
    bad = []
    for k, hi in (("x", 255), ("pk", W * W - 1), ("cb", W - 1), ("wt", 63)):
        a = np.asarray(d[k]).astype(np.float64)
        if not np.all((a >= 0) & (a <= hi) & (a == np.floor(a))): bad.append("range of " + k)
    return bad
def reference(x, pk, cb, wt):
    X = x.astype(np.float32).astype(np.int64).reshape(N, 8, 16, W); p = pk.astype(np.int64).reshape(N, 8, 16, H)
    B = np.concatenate([p & (W - 1), p >> LB], axis=3)
    c = cb.astype(np.int64).reshape(N, 8, 16, L); w = wt.astype(np.int64).reshape(N, 8, 16, 1)
    lane = np.arange(L); rr = np.arange(N)[:, None, None, None]; gg = np.arange(8)[None, :, None, None]
    for t in range(T):
        e = np.take_along_axis(X, c, 3)
        z = np.concatenate([np.zeros((N, 8, 1, L), np.int64), e[:, :, :15] & 15], axis=2)
        v = X[rr, gg, z, c]
        cr = np.concatenate([np.zeros((N, 8, 1, L), bool), np.abs(v[:, :, 1:] - v[:, :, :15]) > TH], axis=2)
        n = np.add.reduce(cr.astype(np.int64), axis=2); A = np.add.reduce(n, axis=2)[:, :, None]; h = np.add.reduce(w * v, axis=2)
        ok = n <= AC; place = S * ((h + A) & (Q - 1)) + lane; nxt = (37 * h + A) & (W - 1)
        mend = np.where(cr, np.take_along_axis(B, c, 3), c)
        X, B = np.array(X), np.array(B)
        for r in range(N):
            for m in range(PARTS):
                q = r if m == 0 else (r + 1 + (t + m - 1) % (N - 1)) % N
                for g in range(8):
                    i = lane[m::PARTS]; i = i[ok[r, g, i]]
                    X[q, g][:, place[r, g, i]] = v[r, g][:, i]; B[q, g][:, place[r, g, i]] = c[r, g][:, i]
        new = np.take_along_axis(B, np.repeat(nxt[:, :, None, :], 16, axis=2), 3)
        c = np.where(ok[:, :, None, :], new, mend)
    return {"yx": X.reshape(N, 128, W).astype(np.float32).astype(BF), "yc": c.reshape(N, 128, L).astype(np.float32)}

@@ -1,0 +1,489 @@
+from concourse.mybir import AluOpType as OP, AxisListType, ActivationFunctionType as AF
+
+N, NT = 4, 4
+L, HB, W = 448, 224, 2048
+CHUNKS = [(0, 96), (96, 128), (224, 128), (352, 96)]
+PIECE = 64
+MEND, BTAB = 0, 448
+BW, XW = 448 + 4096, 4096
+PLAN = {'x0': 'xsxxxxsx', 'x1': 'svvsxvss', 'r0': 'sssvssssxxssxs', 'r1': 'vxsssxsxssxxxs',
+        'adj': {'BG': -31.6, 'v': -16.3, 'XG': -14.6, 'm2': 68.5, 'BX': -100.8, 'relu': 7.5, 'U': -34.2, 'E': 49.3, 'v0': 42.2,
+                'abs': -28.5, 'copy': 7.2, 'A': 9.5, 'ZL': 17.7, 'relu@1': -14.9, 'd': 16.1, 'sign@1': -10.3, 'EL': -11.1,
+                'v@1': 33.3, 'S16': 10.7, 'rej': -17.6, 'v@0': 10.2, 'abs@2': 35.9, 't2': -21.6, 'relu@2': 7.5, 'BX@2': -6.0,
+                'BG@3': -27.0, 'BX@1': -6.5}, 'delta': 0.06, 'wf': 0.11}
+
+F32, B16, I32, U16, H16 = "float32", "bfloat16", "int32", "uint16", "float16"
+SCRATCH = {}
+for _n, _w, _d in (
+        ("X", XW, B16), ("B", BW, F32), ("pki", 1024, I32), ("tlo", 1024, I32), ("thi", 1024, I32), ("cbi", L, I32), ("wti", 8, I32),
+        ("C0", L, U16), ("C1", L, U16), ("CF0", L, H16), ("CF1", L, H16), ("G", 16 * L, B16), ("GB", 16 * L, H16), ("R", 15 * L, B16),
+        ("QI", L, I32), ("Y", L, B16), ("FT", 2 * L, B16), ("V0", L, B16), ("V1", L, B16), ("AB", L, B16), ("SG", L, B16),
+        ("CR", L, B16), ("VT", 8 * 128, B16), ("M2", L, H16), ("YC", L, F32), ("SUMS", 8, F32), ("SA", 8, F32), ("hbf", 32, F32),
+        ("rej", 32, F32), ("acc", 32, F32), ("t1", 32, I32), ("t2", 32, I32), ("t3", 32, F32), ("n1", 32, I32), ("n5", 32, I32),
+        ("n6", 32, I32), ("n2", 32, I32), ("n3", 32, F32), ("n4", 32, F32), ("dl", 32, F32), ("LS0", 32, U16), ("LS1", 32, U16),
+        ("NL", 32, U16), ("COL", 144, F32), ("KC", 128, F32), ("GC", 128, F32), ("M64", 128, F32), ("PI", 8, I32), ("PF", 8, F32),
+        ("KI", 8, I32), ("GI", 8, I32), ("K8I", 8, I32), ("RGI", 8, I32), ("KF", 8, F32), ("GF", 8, F32), ("K8F", 8, F32),
+        ("RGF", 8, F32), ("CFF", 8, F32), ("CBA", 8, F32), ("BIAS", 8, F32), ("P1", 8, F32), ("K2", 8, F32), ("NEG", 8, F32),
+        ("ONE", 8, F32), ("HALF", 8, F32), ("KD", 8, F32), ("KLO", 8, F32), ("IB0", 32, F32), ("IB", 32, F32), ("MC0", 32, F32),
+        ("MC", 32, F32), ("RM", 16, F32), ("RM8", 8, F32), ("ID", 128, B16), ("ID6", 128, B16), ("ID16", 128, H16),
+        ("NI16", 128, H16), ("F", 144, B16), ("BA", 128, B16), ("DA", 128, B16), ("DB", 128, B16), ("EL", 15 * 128, B16),
+        ("ZM", 128, B16), ("KV", 128, B16), ("ZB", 128, B16), ("ZL", 8 * 128, B16), ("S16", 16 * 128, H16), ("O8", 8, B16),
+        ("O80", 8, B16), ("SH", 128, B16), ("KM", 128, B16), ("DF0", 128, B16), ("DF", 128, B16), ("OB", 128, F32), ("WF", 8, F32),
+        ("FW", 144, B16)):
+    SCRATCH[_n] = ("sbuf", [128, _w], _d)
+for _t in range(NT):
+    SCRATCH["rc%d" % _t] = ("sbuf", [128, HB], U16)
+    SCRATCH["rv%d" % _t] = ("sbuf", [128, HB], B16)
+    SCRATCH["rl%d" % _t] = ("sbuf", [128, 16], U16)
+for _n in ("pE0", "pE1", "pU0", "pU1", "pU2", "pV", "pS", "pB"):
+    SCRATCH[_n] = ("psum", [128, 512], F32)
+SEMAPHORES = (["qv", "qs", "qt", "qg", "dcb", "dx", "dpk", "dwt", "oyx", "oyc"]
+              + [a + b + str(t) for a in "rl" for b in "CVL" for t in range(NT)])
+
+CY, TCY, GAM, SCA, LAT = 0.00083 * 1.15, 0.00042 * 1.15, 1.4, 3, 0.1
+
+
+def R(buf, c0, c1, step=1, p0=0, p1=128):
+    return (buf, c0, c1, step, p0, p1)
+
+
+def ap(T, a):
+    buf, c0, c1, step, p0, p1 = a
+    if step == 1:
+        return T[buf][p0:p1, c0:c1]
+    return T[buf][p0:p1, c0:c1:step]
+
+
+def val(T, s):
+    return ap(T, s) if isinstance(s, tuple) else s
+
+
+def build_ops(nsig):
+    ops, ck = [], [9]
+
+    def add(eng, fn, reads, writes, cost, tok=None, name="", after=()):
+        ops.append(dict(eng=eng, fn=fn, reads=list(reads), writes=list(writes), cost=cost, tok=tok, name=name, after=list(after), ck=ck[0]))
+        return len(ops) - 1
+
+    def ne(a):
+        return -((a[1] - a[2]) // a[3])
+
+    def vc(n):
+        return 0.06 + max(64, n) * CY
+
+    def cp(out, in_, cyc=1.0, name="copy"):
+        add("v", lambda g, T, X: g.vector.tensor_copy(ap(T, out), ap(T, in_)), [in_], [out], vc(ne(out) * cyc), name=name)
+
+    def ts(out, in0, s1, s2, op0, op1=None, cyc=1.0, name="ts"):
+        def fn(g, T, X):
+            if op1 is None:
+                return g.vector.tensor_scalar(ap(T, out), ap(T, in0), val(T, s1), None, op0)
+            return g.vector.tensor_scalar(ap(T, out), ap(T, in0), val(T, s1), val(T, s2), op0, op1)
+        add("v", fn, [in0] + [s for s in (s1, s2) if isinstance(s, tuple)], [out], vc(ne(out) * cyc), name=name)
+
+    def tt(out, a, b, op, cyc=2.0, name="tt"):
+        add("v", lambda g, T, X: g.vector.tensor_tensor(ap(T, out), ap(T, a), ap(T, b), op), [a, b], [out], vc(ne(out) * cyc), name=name)
+
+    def ms(out, x):
+        add("v", lambda g, T, X: g.vector.memset(ap(T, out), x), [], [out], vc(ne(out)), name="memset")
+
+    def act(out, in_, func, bias=0.0, scale=1.0, accum=None, name="act"):
+        def fn(g, T, X):
+            if accum is None:
+                return g.scalar.activation(ap(T, out), ap(T, in_), func, bias=val(T, bias), scale=val(T, scale))
+            return g.scalar.activation(ap(T, out), ap(T, in_), func, bias=val(T, bias), scale=val(T, scale), accum_out=ap(T, accum))
+        add("s", fn, [in_] + [s for s in (bias, scale) if isinstance(s, tuple)], [out] + ([accum] if accum else []), 0.08 + ne(out) * CY, name=name)
+
+    def gat(eng, out, win, off, name):
+        def fv(g, T, X):
+            return g.vector.tensor_copy(ap(T, out), ap(T, win).indirect(ap(T, off)))
+
+        def fs(g, T, X):
+            return g.scalar.activation(ap(T, out), ap(T, win).indirect(ap(T, off)), AF.Copy)
+        add(eng, {"v": fv, "s": fs}, [win, off], [out], 0.06 + ne(out) * GAM * CY, name=name)
+
+    def sca(win, off, in_, name):
+        add("v", lambda g, T, X: g.vector.tensor_copy(ap(T, win).indirect(ap(T, off)), ap(T, in_)), [in_, off], [win],
+            0.06 + ne(in_) * SCA * CY, name=name)
+
+    def mm(lst, name, f32=False):
+        def fn(g, T, X):
+            i = None
+            for o, l, r, a, b in lst:
+                i = g.tensor.matmul(ap(T, o), ap(T, l), ap(T, r), a, b)
+            return i
+        cost = sum(max(64, ne(r)) for _o, _l, r, _a, _b in lst) * TCY * (4 if f32 else 1)
+        add("t", fn, [x for m in lst for x in (m[1], m[2])], [m[0] for m in lst], 0.05 + cost, name=name)
+
+    def iota(out, pat, base, cm, f32=True):
+        def fn(g, T, X):
+            if f32:
+                return g.iota(ap(T, out), pat, base, cm, allow_small_or_imprecise_dtypes=True)
+            return g.iota(ap(T, out), pat, base, cm)
+        add("g", fn, [], [out], 0.15 + 2 * ne(out) * CY, name="iota")
+
+    def c1(b):
+        return R(b, 0, 1)
+
+    def whole(b):
+        return R(b, 0, SCRATCH[b][1][1])
+
+    def scaled(o, base, col, name):
+        def fv(g, T, X):
+            return g.vector.tensor_scalar(ap(T, o), ap(T, base), ap(T, col), None, OP.mult)
+
+        def fs(g, T, X):
+            return g.scalar.activation(ap(T, o), ap(T, base), AF.Copy, scale=ap(T, col))
+        add("vs", {"v": fv, "s": fs}, [base, col], [o], 0.12, name=name)
+
+    add("y", lambda g, T, X: g.sync.dma_start(T.cbi[:, :], T.cb[:, :]), [], [R("cbi", 0, L)], 2.5, ("dcb", 16), "ld cb")
+    add("sd", lambda g, T, X: g.scalar.dma_start(T.X[:, 0:W], T.x[:, :]), [], [R("X", 0, W)], 4.5, ("dx", 16), "ld x")
+    add("y", lambda g, T, X: g.sync.dma_start(T.wti[:, 0:1], T.wt[:, :]), [], [c1("wti")], 2.0, ("dwt", 16), "ld wt")
+    add("y", lambda g, T, X: g.sync.dma_start(T.pki[:, :], T.pk[:, :]), [], [R("pki", 0, 1024)], 4.5, ("dpk", 16), "ld pk")
+    iota(c1("PI"), [[1, 1]], 0, 1, False)
+    iota(c1("PF"), [[1, 1]], 0, 1)
+    iota(R("M64", 0, 128), [[0, 2], [1, 64]], 0, 0)
+    iota(R("COL", 0, 144), [[1, 144]], 0, 0)
+    iota(R("GC", 0, 128), [[1, 8], [0, 16]], 0, 0)
+    iota(R("KC", 0, 128), [[0, 8], [1, 16]], 0, 0)
+    iota(R("IB0", 0, 14), [[32, 14]], 1, 0)
+    iota(R("IB0", 14, 28), [[32, 14]], 0, 0)
+    iota(R("MC0", 0, 28), [[16, 28]], -448, 0)
+    ts(c1("KI"), c1("PI"), 15, None, OP.bitwise_and)
+    ts(c1("GI"), c1("PI"), 4, None, OP.logical_shift_right)
+    ts(c1("K8I"), c1("PI"), 7, None, OP.bitwise_and)
+    ts(c1("RGI"), c1("PI"), 63, 3, OP.bitwise_and, OP.logical_shift_right)
+    cp(c1("KF"), c1("KI"))
+    cp(c1("GF"), c1("GI"))
+    cp(c1("K8F"), c1("K8I"))
+    cp(c1("RGF"), c1("RGI"))
+    cp(R("C0", 0, HB), R("cbi", 1, L, 2), name="c16")
+    cp(R("C0", HB, L), R("cbi", 0, L, 2), name="c16")
+    ts(c1("CBA"), c1("GF"), 8.0, c1("K8F"), OP.mult, OP.add)
+    ts(whole("ID6"), R("COL", 0, 128), c1("PF"), 0.0625, OP.is_equal, OP.mult)
+    ts(whole("BA"), whole("M64"), c1("CBA"), None, OP.is_equal)
+    ts(R("RM", 0, 16), R("COL", 0, 16), c1("KF"), None, OP.is_equal)
+    for k in range(15):
+        scaled(R("EL", 128 * k, 128 * k + 128), whole("ID6"), R("RM", k, k + 1), "EL")
+    ts(whole("ID"), R("COL", 0, 128), c1("PF"), None, OP.is_equal)
+    ts(c1("KLO"), c1("KF"), 7.5, None, OP.is_lt)
+    ts(c1("KD"), c1("KF"), 7.5, None, OP.is_gt)
+    scaled(whole("DA"), whole("BA"), c1("KLO"), "DA")
+    scaled(whole("DB"), whole("BA"), c1("KD"), "DA")
+    ms(R("HALF", 0, 1, 1, 0, 64), 0.0)
+    ms(R("HALF", 0, 1, 1, 64, 128), -0.5)
+    ts(R("RM8", 0, 8), R("COL", 0, 8), c1("K8F"), None, OP.is_equal)
+    ts(whole("ZM"), whole("GC"), c1("RGF"), None, OP.is_equal)
+    ts(R("KV", 0, 128, 1, 0, 64), R("KC", 0, 128, 1, 0, 64), 8192.0, -65536.0, OP.mult, OP.add)
+    ts(R("KV", 0, 128, 1, 64, 128), R("KC", 0, 128, 1, 64, 128), -8192.0, None, OP.mult)
+    tt(whole("ZB"), whole("ZM"), whole("KV"), OP.mult)
+    for s in range(8):
+        scaled(R("ZL", 128 * s, 128 * s + 128), whole("ZB"), R("RM8", s, s + 1), "ZL")
+    ts(c1("K2"), c1("KF"), -256.0, 2048.0, OP.mult, OP.add)
+    tt(c1("BIAS"), c1("KF"), c1("K2"), OP.mult)
+    ts(c1("CFF"), c1("GF"), 16.0, 15.0, OP.mult, OP.add)
+    ts(whole("F"), whole("COL"), c1("CFF"), None, OP.is_equal)
+    ts(R("O8", 0, 8), R("COL", 0, 8), c1("GF"), None, OP.is_equal)
+    ts(R("O80", 0, 8), R("O8", 0, 8), R("RM", 0, 1), None, OP.mult)
+    ts(c1("P1"), c1("PF"), 1.0, None, OP.add)
+    ts(whole("SH"), R("COL", 0, 128), c1("P1"), None, OP.is_equal)
+    tt(whole("DF0"), whole("ID"), whole("SH"), OP.subtract)
+    ts(whole("KM"), whole("KC"), 0.0, None, OP.is_gt)
+    tt(whole("DF"), whole("DF0"), whole("KM"), OP.mult)
+    ms(c1("NEG"), -80.5)
+    ms(c1("ONE"), 1.0)
+    ms(c1("SUMS"), 448.0)
+    cp(c1("WF"), c1("wti"))
+    scaled(whole("FW"), whole("F"), c1("WF"), "FW")
+    ts(whole("OB"), whole("GC"), c1("GF"), 0.5, OP.is_equal, OP.mult)
+    ts(c1("K2"), c1("KF"), 2.0, None, OP.mult)
+    ts(R("IB", 0, 28), R("IB0", 0, 28), c1("K2"), 1.0 / 512, OP.add, OP.mult)
+    ts(R("MC", 0, 28), R("MC0", 0, 28), c1("KF"), 1.0 / 2048, OP.add, OP.mult)
+    ts(whole("ID16"), R("COL", 0, 128), c1("PF"), None, OP.is_equal)
+    ts(whole("NI16"), whole("ID16"), -1.0, None, OP.mult)
+    for k in range(1, 16):
+        ts(R("S16", 128 * k, 128 * k + 128), whole("ID16"), R("RM", k, k + 1), None, OP.mult, cyc=0.5, name="S16")
+    ts(whole("tlo"), whole("pki"), W - 1, None, OP.bitwise_and)
+    cp(R("B", BTAB, BTAB + 1024), whole("tlo"))
+    ts(whole("thi"), whole("pki"), 11, None, OP.logical_shift_right)
+    cp(R("B", BTAB + 1024, BTAB + 2048), whole("thi"))
+    cp(whole("CF0"), whole("C0"), 0.5)
+
+    xw, bw = R("X", 0, W), R("B", BTAB, BTAB + W)
+    ub, un = ["pU0", "pU1", "pU2"], 0
+    nc = len(CHUNKS)
+
+    for t in range(NT):
+        C, CF, V, LS = "C%d" % (t % 2), "CF%d" % (t % 2), "V%d" % (t % 2), "LS%d" % (t % 2)
+
+        def send(what, src, dst, t=t):
+            def fn(g, T, X):
+                rid, pid, m = X[t]
+                return g.remote_dma(ap(T, dst), ap(T, src), T.sem["r%s%d" % (what, t)], T.sem["l%s%d" % (what, t)], pid, rid, m)
+            i = add("g", fn, [src], [], 0.6, ("l%s%d" % (what, t), nsig), "send " + what)
+            add("x", None, [], [dst], 2.2, ("r%s%d" % (what, t), nsig), "recv " + what, [i])
+
+        send("C", R(C, 0, HB), R("rc%d" % t, 0, HB))
+        for c, (i0, n) in enumerate(CHUNKS):
+            i1, g0, ck[0] = i0 + n, 16 * i0, c
+            for j in range(i0, i1, PIECE):
+                e = min(j + PIECE, i1)
+                gat("vs", R("G", 16 * j, 16 * e), xw, R(C, j, e), "XG")
+            pe = "pE%d" % (c % 2)
+            mm([(R(pe, 0, n), R("EL", 128 * k, 128 * k + 128), R("G", g0 + k, 16 * i1, 16), k == 0, k == 14) for k in range(15)], "E")
+            q, y = R("QI", i0, i1), R("Y", i0, i1)
+            ts(q, R(pe, 0, n), 0.46875, None, OP.subtract, name="q")
+            tt(y, R(pe, 0, n), q, OP.subtract, 1.0, name="y")
+            mm([(R(pe, 256, 256 + n), whole("DA"), y, True, True), (R(pe, 256 + n, 256 + 2 * n), whole("DB"), y, True, True)], "yy")
+            act(R("FT", 2 * i0, 2 * i1), R(pe, 256, 256 + 2 * n), AF.Square, bias=c1("HALF"), name="sq")
+            mm([(R("pV", 0, 128, 16, 0, n), R("G", g0, 16 * i1, 16), R("O80", 0, 8), True, True)], "v0")
+            per = 512 // n
+            for b in range(0, 15, per):
+                kk = list(range(1, 16))[b:b + per]
+                u = ub[un % 3]
+                un += 1
+                lst = []
+                for x, k in enumerate(kk):
+                    o, s, h = R(u, x * n, x * n + n), (k - 1) % 8, (k - 1) // 8
+                    lst.append((o, whole("ID"), R("G", g0 + k, 16 * i1, 16), True, False))
+                    lst.append((o, R("ZL", 128 * s, 128 * s + 128), R("FT", 2 * i0 + h * n, 2 * i0 + h * n + n), False, True))
+                mm(lst, "U")
+                r0 = 15 * i0 + b * n
+                ro, ui = R("R", r0, r0 + len(kk) * n), R(u, 0, len(kk) * n)
+
+                def fv(g, T, X, ro=ro, ui=ui):
+                    return g.vector.tensor_scalar(ap(T, ro), ap(T, ui), T.BIAS[:, 0:1], 0.0, OP.add, OP.max)
+
+                def fs(g, T, X, ro=ro, ui=ui):
+                    return g.scalar.activation(ap(T, ro), ap(T, ui), AF.Relu, bias=T.BIAS[:, 0:1])
+                add("vs", {"v": fv, "s": fs}, [ui, c1("BIAS")], [ro], 0.08 + len(kk) * n * CY, name="relu")
+                mm([(R("pV", k, 128, 16, 0, n), R("R", 15 * i0 + (k - 1) * n, 15 * i0 + k * n), R("O8", 0, 8), True, True) for k in kk], "v")
+            vv, vt = R(V, i0, i1), R("VT", 128 * c, 128 * c + 128, 1, 0, n)
+            act(vt, R("pV", 0, 128, 1, 0, n), AF.Copy, name="vt")
+            mm([(R("pS", 128, 128 + n), vt, R("ID", 0, n, 1, 0, n), True, True)], "vn")
+            act(vv, R("pS", 128, 128 + n), AF.Copy, name="vcopy")
+            mm([(R("pS", 0, n), whole("DF"), vv, True, True)], "d")
+            act(R("AB", i0, i1), R("pS", 0, n), AF.Abs, name="abs")
+            act(R("SG", i0, i1), R("AB", i0, i1), AF.Sign, bias=c1("NEG"), accum=R("SUMS", c + 1, c + 2), name="sign")
+            act(R("CR", i0, i1), R("SG", i0, i1), AF.Relu, name="cr")
+            if i1 == HB:
+                send("V", R(V, 0, HB), R("rv%d" % t, 0, HB))
+        for c, (i0, n) in enumerate(CHUNKS):
+            i1, g0, ck[0], pb = i0 + n, 16 * i0, c, ("pB", "pV", "pE1", "pS")[c]
+            for j in range(i0, i1, PIECE):
+                e = min(j + PIECE, i1)
+                gat("v", R("GB", 16 * j, 16 * e), bw, R(C, j, e), "BG")
+            bl = ([(R(pb, 0, n), R("S16", 128 * k, 128 * k + 128), R("GB", g0 + k, 16 * i1, 16), k == 1, False) for k in range(1, 16)]
+                  + [(R(pb, 0, n), whole("NI16"), R(CF, i0, i1), False, True)])
+            for j in range(0, 16, 4):
+                mm(bl[j:j + 4], "BX")
+            tt(R("M2", i0, i1), R(pb, 0, n), R("CR", i0, i1), OP.mult, 1.0, name="m2")
+            mm([(R(pb, 256, 256 + n), whole("ID16"), R("M2", i0, i1), True, False),
+                (R(pb, 256, 256 + n), whole("ID16"), R(CF, i0, i1), False, True)], "mend")
+            act(R("B", MEND + i0, MEND + i1), R(pb, 256, 256 + n), AF.Copy, name="mend")
+        ck[0] = 9
+
+        def wrap(bank, lh, src, name):
+            mm([(R(bank, 0, 28), R(lh, 15 - b, 143 - b), R(src, b, L, 16), b == 0, b == 15) for b in range(16)], name)
+        wrap("pU0", "FW", V, "h")
+        cp(R("n1", 0, 28), R("pU0", 0, 28), name="h1")
+        ts(R("n2", 0, 28), R("n1", 0, 28), 2047, None, OP.bitwise_and, name="h2")
+        tt(R("hbf", 0, 28), R("n2", 0, 28), R("IB", 0, 28), OP.add, name="hb")
+        sa, su, sl = c1("SA"), R("SUMS", 0, nc), R("SUMS", nc, nc + 1)
+        add("v", lambda g, T, X, sa=sa, su=su: g.vector.tensor_reduce(ap(T, sa), ap(T, su), AxisListType.X, OP.add), [su], [sa], vc(4), name="SA")
+        mm([(R("pU2", 0, 1), whole("OB"), sa, True, False), (R("pU2", 0, 1), whole("OB"), sl, False, True)], "A", True)
+        wrap("pU1", "F", "SG", "n")
+        ts(R("rej", 0, 28), R("pU1", 0, 28), -5.0, 2048.0, OP.is_gt, OP.mult, name="rej")
+        act(R("acc", 0, 28), R("rej", 0, 28), AF.Identity, bias=c1("ONE"), scale=-1.0 / 2048, name="acc")
+        ts(R("t1", 0, 28), R("hbf", 0, 28), R("pU2", 0, 1), 512.0, OP.add, OP.mult, name="t1")
+        ts(R("t2", 0, 28), R("t1", 0, 28), 2047, None, OP.bitwise_and, name="t2")
+        tt(R("t3", 0, 28), R("t2", 0, 28), R("rej", 0, 28), OP.add, name="t3")
+        cp(R(LS, 0, 28), R("t3", 0, 28), name="list")
+        send("L", R(LS, 0, 14), R("rl%d" % t, 0, 14))
+        ts(R("n5", 0, 28), R("n2", 0, 28), 37.0, R("pU2", 0, 1), OP.mult, OP.add, name="n1")
+        ts(R("n6", 0, 28), R("n5", 0, 28), 2047, None, OP.bitwise_and, name="n2")
+        tt(R("n3", 0, 28), R("n6", 0, 28), R("acc", 0, 28), OP.mult, name="n3")
+        tt(R("dl", 0, 28), R("rej", 0, 28), R("MC", 0, 28), OP.mult, name="dl")
+        tt(R("n4", 0, 28), R("n3", 0, 28), R("dl", 0, 28), OP.add, name="n4")
+        ts(R("NL", 0, 28), R("n4", 0, 28), 448.0, None, OP.add, name="NL")
+        xs, bs = R("X", 0, XW), R("B", BTAB, BW)
+        ls, rl = R(LS, 14, 28), R("rl%d" % t, 0, 14)
+        sca(xs, ls, R(V, HB, L), "XS even")
+        sca(bs, ls, R(C, HB, L), "BS even")
+        last = t == NT - 1
+        rest = [(xs, R("rv%d" % t, 0, HB), "XS odd"), (bs, R("rc%d" % t, 0, HB), "BS odd")]
+        for w, s, nm in (rest if last else rest[::-1]):
+            sca(w, rl, s, nm)
+        bn = R("B", 0, BTAB + W)
+        if last:
+            add("y", lambda g, T, X: g.sync.dma_start(T.yx[:, :], T.X[:, 0:W]), [R("X", 0, W)], [], 4.0, ("oyx", 16), "st x")
+            gat("v", R("YC", 1, L, 2), bn, R("NL", 0, 14), "nxt")
+            gat("s", R("YC", 0, L, 2), bn, R("NL", 14, 28), "nxt")
+            add("y", lambda g, T, X: g.sync.dma_start(T.yc[:, :], T.YC[:, :]), [R("YC", 0, L)], [], 2.5, ("oyc", 16), "st c")
+        else:
+            D, DF_ = "C%d" % ((t + 1) % 2), "CF%d" % ((t + 1) % 2)
+            gat("v", R(D, 0, HB), bn, R("NL", 0, 14), "nxt")
+            gat("v", R(D, HB, L), bn, R("NL", 14, 28), "nxt")
+            cp(whole(DF_), whole(D), 0.5, name="cf")
+    return ops
+
+
+def hit(a, b):
+    return a[0] == b[0] and a[1] < b[2] and b[1] < a[2] and a[4] < b[5] and b[4] < a[5]
+
+
+def depend(ops):
+    hist, deps = {}, []
+    for i, o in enumerate(ops):
+        d = {a: True for a in o["after"]}
+        acc = [(r, False) for r in o["reads"]] + [(w, True) for w in o["writes"]]
+        for r, wr in acc:
+            ps = SCRATCH[r[0]][0] == "psum"
+            for j, q, qw in hist.get(r[0], []):
+                if j == i:
+                    continue
+                same = ops[j]["eng"] == o["eng"] and o["eng"] in ("t", "v", "s", "g")
+                over = hit(r, q) and (wr or qw)
+                if same and o["eng"] == "t":
+                    if over:
+                        d[j] = d.get(j, False)
+                elif over or (ps and not same):
+                    d[j] = True
+        deps.append(d)
+        for r, wr in acc:
+            h = hist.setdefault(r[0], [])
+            if wr and SCRATCH[r[0]][0] != "psum" and r[3] == 1:
+                h[:] = [e for e in h if e[0] == i or not (e[1][1] >= r[1] and e[1][2] <= r[2] and e[1][4] >= r[4] and e[1][5] <= r[5])]
+            h.append((i, r, wr))
+            if SCRATCH[r[0]][0] == "psum":
+                del h[:-80]
+    return deps
+
+
+def force(ops):
+    f, k = {}, {"XG": 0, "relu": 0}
+    tot = {z: sum(o["name"] == z for o in ops) // NT for z in k}
+    for i, o in enumerate(ops):
+        z = o["name"]
+        if z in k:
+            f[i] = PLAN[("x" if z == "XG" else "r") + ("0" if k[z] < tot[z] else "1")][k[z] % tot[z]]
+            k[z] += 1
+    return {i: ("vs" if v == "x" else v) for i, v in f.items()}
+
+
+def schedule(ops, deps):
+    n = len(ops)
+    fc, adj, dl, wf = force(ops), PLAN["adj"], PLAN["delta"], PLAN["wf"]
+    succ = [[] for _ in range(n)]
+    for i in range(n):
+        for j in deps[i]:
+            succ[j].append(i)
+    pri = [0.0] * n
+    for i in range(n - 1, -1, -1):
+        pri[i] = ops[i]["cost"] + max([pri[s] + LAT for s in succ[i]] or [0.0])
+    pa = [pri[i] + adj.get(ops[i]["name"], 0.0) + adj.get("%s@%d" % (ops[i]["name"], ops[i]["ck"]), 0.0) for i in range(n)]
+    left = [len(d) for d in deps]
+    ready = {i: 0.0 for i in range(n) if left[i] == 0}
+    free = {"v": 0.0, "s": 0.0, "t": 0.0, "g": 0.0, "y": 0.0}
+    fin, order = [0.0] * n, []
+    while ready:
+        best, heads = None, {}
+        for i, r in ready.items():
+            e = ops[i]["eng"]
+            if e == "x":
+                best = (r, "x", i)
+                break
+            if e == "vs":
+                e = fc.get(i, "vs")
+            for q in ("v", "s") if e == "vs" else (("s",) if e == "sd" else (e,)):
+                heads.setdefault(q, []).append((max(free[q], r), i))
+        if best is None:
+            for q, c in heads.items():
+                t0 = min(c)[0]
+                if best is not None and t0 >= best[0]:
+                    continue
+                a = max((pa[i], -i) for st, i in c if st <= t0 + dl)
+                lim = t0 + max(dl, wf * ops[-a[1]]["cost"])
+                a = max((pa[i], -i, st) for st, i in c if st <= lim)
+                if best is None or a[2] < best[0]:
+                    best = (a[2], q, -a[1])
+        st, q, i = best
+        del ready[i]
+        o = ops[i]
+        if q == "x":
+            fin[i] = st + o["cost"]
+        elif o["eng"] in ("y", "sd"):
+            free[q] = st + 0.1
+            fin[i] = st + o["cost"]
+        else:
+            free[q] = fin[i] = st + o["cost"]
+        order.append((i, q))
+        for s in succ[i]:
+            left[s] -= 1
+            if left[s] == 0:
+                ready[s] = max(fin[j] + (LAT if w else 0.0) for j, w in deps[s].items())
+    return order, max(fin)
+
+
+_plan = {}
+
+
+def plan(nsig):
+    if nsig in _plan:
+        return _plan[nsig]
+    ops = build_ops(nsig)
+    deps = depend(ops)
+    order, span = schedule(ops, deps)
+    sem = {"v": "qv", "s": "qs", "t": "qt", "g": "qg"}
+    cnt, known, tok, snap, out = {}, {q: {} for q in "vstgy"}, {}, {}, []
+    for i, q in order:
+        o = ops[i]
+        if q == "x":
+            tok[i] = o["tok"]
+            cnt[o["tok"][0]] = o["tok"][1]
+            snap[i] = {o["tok"][0]: o["tok"][1]}
+            continue
+        kn, top = known[q], {}
+        for j in sorted((j for j, w in deps[i].items() if w), reverse=True):
+            s, v = tok[j]
+            if kn.get(s, 0) < v:
+                top[s] = max(top.get(s, 0), v)
+                for a, b in snap[j].items():
+                    if kn.get(a, 0) < b:
+                        kn[a] = b
+        if o["tok"]:
+            tok[i] = o["tok"]
+            cnt[o["tok"][0]] = o["tok"][1]
+        else:
+            s = sem[q]
+            cnt[s] = cnt.get(s, 0) + 1
+            tok[i] = (s, cnt[s])
+        snap[i] = dict(kn)
+        snap[i][tok[i][0]] = tok[i][1]
+        out.append((q, o, sorted(top.items()), tok[i]))
+    _plan[nsig] = (out, cnt, span)
+    return _plan[nsig]
+
+
+def rank_program(g, core, T, topo):
+    rank = T.rank_of(core)
+    if rank is None:
+        return
+    X = []
+    for t in range(NT):
+        d = T.cores[(rank + 1 + t % (N - 1)) % N]
+        rid, pid = topo.addr(d, core)
+        X.append((rid, pid, topo.mask(core, d)))
+    out, cnt, _span = plan(len(topo.engines(core, T.cores[(rank + 1) % N])))
+    queue = {"v": g.vector, "s": g.scalar, "t": g.tensor, "g": g, "y": g.sync}
+    for q, o, waits, tk in out:
+        for s, v in waits:
+            queue[q].wait_ge(T.sem[s], v)
+        fn = o["fn"][q] if isinstance(o["fn"], dict) else o["fn"]
+        ins = fn(g, T, X)
+        if o["tok"] is None:
+            ins.then_inc(T.sem[tk[0]], 1)
+        elif o["name"][:4] != "send":
+            ins.then_inc(T.sem[tk[0]], tk[1])
+    for s, v in sorted(cnt.items()):
+        g.wait_ge(T.sem[s], v)

@@ -2,45 +2,39 @@ from concourse.mybir import AluOpType as OP, AxisListType, ActivationFunctionTyp
 
 N, NT = 4, 4
 L, HB, W = 448, 224, 2048
-CHUNKS = [(0, 96), (96, 128), (224, 128), (352, 96)]
-PIECE = 64
-MEND, BTAB = 0, 448
-BW, XW = 448 + 4096, 4096
-PLAN = {'x0': 'xsxxxxsx', 'x1': 'svvsxvss', 'r0': 'sssvssssxxssxs', 'r1': 'vxsssxsxssxxxs',
-        'adj': {'BG': -31.6, 'v': -16.3, 'XG': -14.6, 'm2': 68.5, 'BX': -100.8, 'relu': 7.5, 'U': -34.2, 'E': 49.3, 'v0': 42.2,
-                'abs': -28.5, 'copy': 7.2, 'A': 9.5, 'ZL': 17.7, 'relu@1': -14.9, 'd': 16.1, 'sign@1': -10.3, 'EL': -11.1,
-                'v@1': 33.3, 'S16': 10.7, 'rej': -17.6, 'v@0': 10.2, 'abs@2': 35.9, 't2': -21.6, 'relu@2': 7.5, 'BX@2': -6.0,
-                'BG@3': -27.0, 'BX@1': -6.5}, 'delta': 0.06, 'wf': 0.11}
+CHUNKS = [(0, 128), (128, 128), (256, 128), (384, 64)]
+BCHUNKS = [(0, 224), (224, 224)]
+MEND = 4096
+BW, XW = MEND + L, 4096
+PLAN = {'eng': {'XG': 'xxxxsss', 'BG': 'sxxssxx', 'mendc': 'sss', 'cr': 'vss'}, 'xp': 64, 'bp': 64,
+        'adj': {'BG': -9.8, 'unpk': 47.2, 'S16': -2.7, 's': 8.6, 'd': 1.0, 'back@1': 1.7, 'EL': -2.5, 'tt@3': 4.2, 'XS even': 6.9, 'PW': -1.5, 'h37': 1.1, 'E@2': -5.0, 'y': 3.3, 'and@0': 0.6, 'n6': 0.1, 'tt@0': -0.4, 'send C': 3.9, 'dl': -0.1, 'BS even': -0.3, 'd@3': -0.3, 'n': -0.7, 'q@2': 7.8, 'rej': -2.5, 's@3': 2.4, 'NL': -3.1, 'pen@1': -0.6, 't1': 2.1, 'n7': 3.4},
+        'delta': 0.0, 'wf': 0.17, 'bc': [(0, 128), (128, 128), (256, 192)], 'nx': [(0, 128), (128, 448)]}
 
 F32, B16, I32, U16, H16 = "float32", "bfloat16", "int32", "uint16", "float16"
 SCRATCH = {}
 for _n, _w, _d in (
         ("X", XW, B16), ("B", BW, F32), ("pki", 1024, I32), ("tlo", 1024, I32), ("thi", 1024, I32), ("cbi", L, I32), ("wti", 8, I32),
-        ("C0", L, U16), ("C1", L, U16), ("CF0", L, H16), ("CF1", L, H16), ("G", 16 * L, B16), ("GB", 16 * L, H16), ("R", 15 * L, B16),
-        ("QI", L, I32), ("Y", L, B16), ("FT", 2 * L, B16), ("V0", L, B16), ("V1", L, B16), ("AB", L, B16), ("SG", L, B16),
-        ("CR", L, B16), ("VT", 8 * 128, B16), ("M2", L, H16), ("YC", L, F32), ("SUMS", 8, F32), ("SA", 8, F32), ("hbf", 32, F32),
-        ("rej", 32, F32), ("acc", 32, F32), ("t1", 32, I32), ("t2", 32, I32), ("t3", 32, F32), ("n1", 32, I32), ("n5", 32, I32),
-        ("n6", 32, I32), ("n2", 32, I32), ("n3", 32, F32), ("n4", 32, F32), ("dl", 32, F32), ("LS0", 32, U16), ("LS1", 32, U16),
-        ("NL", 32, U16), ("COL", 144, F32), ("KC", 128, F32), ("GC", 128, F32), ("M64", 128, F32), ("PI", 8, I32), ("PF", 8, F32),
-        ("KI", 8, I32), ("GI", 8, I32), ("K8I", 8, I32), ("RGI", 8, I32), ("KF", 8, F32), ("GF", 8, F32), ("K8F", 8, F32),
-        ("RGF", 8, F32), ("CFF", 8, F32), ("CBA", 8, F32), ("BIAS", 8, F32), ("P1", 8, F32), ("K2", 8, F32), ("NEG", 8, F32),
-        ("ONE", 8, F32), ("HALF", 8, F32), ("KD", 8, F32), ("KLO", 8, F32), ("IB0", 32, F32), ("IB", 32, F32), ("MC0", 32, F32),
-        ("MC", 32, F32), ("RM", 16, F32), ("RM8", 8, F32), ("ID", 128, B16), ("ID6", 128, B16), ("ID16", 128, H16),
-        ("NI16", 128, H16), ("F", 144, B16), ("BA", 128, B16), ("DA", 128, B16), ("DB", 128, B16), ("EL", 15 * 128, B16),
-        ("ZM", 128, B16), ("KV", 128, B16), ("ZB", 128, B16), ("ZL", 8 * 128, B16), ("S16", 16 * 128, H16), ("O8", 8, B16),
-        ("O80", 8, B16), ("SH", 128, B16), ("KM", 128, B16), ("DF0", 128, B16), ("DF", 128, B16), ("OB", 128, F32), ("WF", 8, F32),
-        ("FW", 144, B16)):
+        ("C0", L, U16), ("C1", L, U16), ("CF0", L, H16), ("CF1", L, H16), ("G", 16 * L, H16), ("GB", 16 * L, H16), ("SO", 3584, F32),
+        ("QI", L, I32), ("Y", L, B16), ("BT", L, I32), ("S", L, B16), ("TI", L, I32), ("A8", L, I32), ("VK", L, H16),
+        ("V0", L, B16), ("V1", L, B16), ("AB", L, B16), ("SG", L, B16), ("M2", L, H16), ("YC", L, F32), ("SUMS", 8, F32), ("SA", 8, F32),
+        ("rej", 32, F32), ("t1", 32, I32), ("t2", 32, I32), ("t3", 32, F32), ("n5", 32, I32), ("n6", 32, I32), ("n7", 32, F32),
+        ("dl", 32, F32), ("LS0", 32, U16), ("LS1", 32, U16), ("NL", 32, U16),
+        ("II", 8, I32), ("FF", 8, F32), ("CC", 16, F32), ("WI", 8, I32), ("W2", 8, H16), ("COL", 160, F32), ("GC", 128, F32),
+        ("DZ", 512, F32), ("IB0", 32, F32), ("IB", 32, H16), ("MC0", 32, F32), ("MC", 32, F32), ("RM", 16, F32),
+        ("EB", 144, H16), ("EL", 15 * 128, H16), ("XP", 64, H16), ("I64", 64, B16), ("PW", 512, B16), ("IDF", 128, F32),
+        ("PM", 128, H16), ("PK", 128, H16), ("SH", 128, H16), ("DF", 128, H16), ("F", 144, B16), ("FK", 144, H16), ("F4", 144, H16),
+        ("F37", 144, H16), ("OB", 128, F32), ("ID16", 128, H16), ("CR", L, B16), ("NI16", 128, H16), ("S16", 15 * 128, H16)):
     SCRATCH[_n] = ("sbuf", [128, _w], _d)
 for _t in range(NT):
     SCRATCH["rc%d" % _t] = ("sbuf", [128, HB], U16)
     SCRATCH["rv%d" % _t] = ("sbuf", [128, HB], B16)
     SCRATCH["rl%d" % _t] = ("sbuf", [128, 16], U16)
-for _n in ("pE0", "pE1", "pU0", "pU1", "pU2", "pV", "pS", "pB"):
+for _n in ("pE0", "pE1", "pU0", "pU1", "pU2", "pT", "pD", "pW"):
     SCRATCH[_n] = ("psum", [128, 512], F32)
 SEMAPHORES = (["qv", "qs", "qt", "qg", "dcb", "dx", "dpk", "dwt", "oyx", "oyc"]
               + [a + b + str(t) for a in "rl" for b in "CVL" for t in range(NT)])
 
-CY, TCY, GAM, SCA, LAT = 0.00083 * 1.15, 0.00042 * 1.15, 1.4, 3, 0.1
+CY, TCY, GAM, SCA, LAT = 0.00083 * 1.1, 0.00042 * 1.1, 1.45, 3.5, 0.1
 
 
 def R(buf, c0, c1, step=1, p0=0, p1=128):
@@ -58,53 +52,62 @@ def val(T, s):
     return ap(T, s) if isinstance(s, tuple) else s
 
 
+def cost_of(el):
+    kind, n = el
+    return {"plain": 0.06 + max(64, n) * CY, "gat": 0.06 + n * GAM * CY, "sca": 0.06 + n * SCA * CY, "pe": 0.03 + n * TCY,
+            "pool": 0.15 + 2 * n * CY, "fixed": n}[kind]
+
+
 def build_ops(nsig):
     ops, ck = [], [9]
 
-    def add(eng, fn, reads, writes, cost, tok=None, name="", after=()):
-        ops.append(dict(eng=eng, fn=fn, reads=list(reads), writes=list(writes), cost=cost, tok=tok, name=name, after=list(after), ck=ck[0]))
+    def add(eng, fn, reads, writes, el, tok=None, name="", after=()):
+        ops.append(dict(eng=eng, fn=fn, reads=list(reads), writes=list(writes), el=el, cost=cost_of(el), tok=tok, name=name,
+                        after=list(after), ck=ck[0]))
         return len(ops) - 1
 
     def ne(a):
         return -((a[1] - a[2]) // a[3])
 
-    def vc(n):
-        return 0.06 + max(64, n) * CY
-
     def cp(out, in_, cyc=1.0, name="copy"):
-        add("v", lambda g, T, X: g.vector.tensor_copy(ap(T, out), ap(T, in_)), [in_], [out], vc(ne(out) * cyc), name=name)
+        add("v", lambda g, T, X: g.vector.tensor_copy(ap(T, out), ap(T, in_)), [in_], [out], ("plain", ne(out) * cyc), name=name)
 
     def ts(out, in0, s1, s2, op0, op1=None, cyc=1.0, name="ts"):
         def fn(g, T, X):
             if op1 is None:
                 return g.vector.tensor_scalar(ap(T, out), ap(T, in0), val(T, s1), None, op0)
             return g.vector.tensor_scalar(ap(T, out), ap(T, in0), val(T, s1), val(T, s2), op0, op1)
-        add("v", fn, [in0] + [s for s in (s1, s2) if isinstance(s, tuple)], [out], vc(ne(out) * cyc), name=name)
+        add("v", fn, [in0] + [s for s in (s1, s2) if isinstance(s, tuple)], [out], ("plain", ne(out) * cyc), name=name)
 
     def tt(out, a, b, op, cyc=2.0, name="tt"):
-        add("v", lambda g, T, X: g.vector.tensor_tensor(ap(T, out), ap(T, a), ap(T, b), op), [a, b], [out], vc(ne(out) * cyc), name=name)
+        add("v", lambda g, T, X: g.vector.tensor_tensor(ap(T, out), ap(T, a), ap(T, b), op), [a, b], [out], ("plain", ne(out) * cyc), name=name)
 
     def ms(out, x):
-        add("v", lambda g, T, X: g.vector.memset(ap(T, out), x), [], [out], vc(ne(out)), name="memset")
+        add("v", lambda g, T, X: g.vector.memset(ap(T, out), x), [], [out], ("plain", ne(out)), name="memset")
 
     def act(out, in_, func, bias=0.0, scale=1.0, accum=None, name="act"):
         def fn(g, T, X):
             if accum is None:
                 return g.scalar.activation(ap(T, out), ap(T, in_), func, bias=val(T, bias), scale=val(T, scale))
             return g.scalar.activation(ap(T, out), ap(T, in_), func, bias=val(T, bias), scale=val(T, scale), accum_out=ap(T, accum))
-        add("s", fn, [in_] + [s for s in (bias, scale) if isinstance(s, tuple)], [out] + ([accum] if accum else []), 0.08 + ne(out) * CY, name=name)
+        add("s", fn, [in_] + [s for s in (bias, scale) if isinstance(s, tuple)], [out] + ([accum] if accum else []), ("plain", ne(out)), name=name)
+
+    def move(out, in_, name):
+        add("vs", {"v": lambda g, T, X: g.vector.tensor_copy(ap(T, out), ap(T, in_)),
+                   "s": lambda g, T, X: g.scalar.activation(ap(T, out), ap(T, in_), AF.Copy)}, [in_], [out], ("plain", ne(out)), name=name)
+
+    def scaled(o, base, by, name):
+        add("vs", {"v": lambda g, T, X: g.vector.tensor_scalar(ap(T, o), ap(T, base), val(T, by), None, OP.mult),
+                   "s": lambda g, T, X: g.scalar.activation(ap(T, o), ap(T, base), AF.Copy, scale=val(T, by))},
+            [base] + ([by] if isinstance(by, tuple) else []), [o], ("plain", ne(o) * 0.75), name=name)
 
     def gat(eng, out, win, off, name):
-        def fv(g, T, X):
-            return g.vector.tensor_copy(ap(T, out), ap(T, win).indirect(ap(T, off)))
-
-        def fs(g, T, X):
-            return g.scalar.activation(ap(T, out), ap(T, win).indirect(ap(T, off)), AF.Copy)
-        add(eng, {"v": fv, "s": fs}, [win, off], [out], 0.06 + ne(out) * GAM * CY, name=name)
+        add(eng, {"v": lambda g, T, X: g.vector.tensor_copy(ap(T, out), ap(T, win).indirect(ap(T, off))),
+                  "s": lambda g, T, X: g.scalar.activation(ap(T, out), ap(T, win).indirect(ap(T, off)), AF.Copy)},
+            [win, off], [out], ("gat", ne(out)), name=name)
 
     def sca(win, off, in_, name):
-        add("v", lambda g, T, X: g.vector.tensor_copy(ap(T, win).indirect(ap(T, off)), ap(T, in_)), [in_, off], [win],
-            0.06 + ne(in_) * SCA * CY, name=name)
+        add("v", lambda g, T, X: g.vector.tensor_copy(ap(T, win).indirect(ap(T, off)), ap(T, in_)), [in_, off], [win], ("sca", ne(in_)), name=name)
 
     def mm(lst, name, f32=False):
         def fn(g, T, X):
@@ -112,201 +115,203 @@ def build_ops(nsig):
             for o, l, r, a, b in lst:
                 i = g.tensor.matmul(ap(T, o), ap(T, l), ap(T, r), a, b)
             return i
-        cost = sum(max(64, ne(r)) for _o, _l, r, _a, _b in lst) * TCY * (4 if f32 else 1)
-        add("t", fn, [x for m in lst for x in (m[1], m[2])], [m[0] for m in lst], 0.05 + cost, name=name)
+        cyc = sum(max(min(64, ne(l)), ne(r)) for _o, l, r, _a, _b in lst) * (4 if f32 else 1)
+        add("t", fn, [x for m in lst for x in (m[1], m[2])], [m[0] for m in lst], ("pe", cyc), name=name)
 
     def iota(out, pat, base, cm, f32=True):
         def fn(g, T, X):
             if f32:
                 return g.iota(ap(T, out), pat, base, cm, allow_small_or_imprecise_dtypes=True)
             return g.iota(ap(T, out), pat, base, cm)
-        add("g", fn, [], [out], 0.15 + 2 * ne(out) * CY, name="iota")
+        add("g", fn, [], [out], ("pool", ne(out)), name="iota")
 
-    def c1(b):
-        return R(b, 0, 1)
+    def col(b, j=0):
+        return R(b, j, j + 1)
 
     def whole(b):
         return R(b, 0, SCRATCH[b][1][1])
 
-    def scaled(o, base, col, name):
-        def fv(g, T, X):
-            return g.vector.tensor_scalar(ap(T, o), ap(T, base), ap(T, col), None, OP.mult)
-
-        def fs(g, T, X):
-            return g.scalar.activation(ap(T, o), ap(T, base), AF.Copy, scale=ap(T, col))
-        add("vs", {"v": fv, "s": fs}, [base, col], [o], 0.12, name=name)
-
-    add("y", lambda g, T, X: g.sync.dma_start(T.cbi[:, :], T.cb[:, :]), [], [R("cbi", 0, L)], 2.5, ("dcb", 16), "ld cb")
-    add("sd", lambda g, T, X: g.scalar.dma_start(T.X[:, 0:W], T.x[:, :]), [], [R("X", 0, W)], 4.5, ("dx", 16), "ld x")
-    add("y", lambda g, T, X: g.sync.dma_start(T.wti[:, 0:1], T.wt[:, :]), [], [c1("wti")], 2.0, ("dwt", 16), "ld wt")
-    add("y", lambda g, T, X: g.sync.dma_start(T.pki[:, :], T.pk[:, :]), [], [R("pki", 0, 1024)], 4.5, ("dpk", 16), "ld pk")
-    iota(c1("PI"), [[1, 1]], 0, 1, False)
-    iota(c1("PF"), [[1, 1]], 0, 1)
-    iota(R("M64", 0, 128), [[0, 2], [1, 64]], 0, 0)
-    iota(R("COL", 0, 144), [[1, 144]], 0, 0)
-    iota(R("GC", 0, 128), [[1, 8], [0, 16]], 0, 0)
-    iota(R("KC", 0, 128), [[0, 8], [1, 16]], 0, 0)
+    add("y", lambda g, T, X: g.sync.dma_start(T.cbi[:, :], T.cb[:, :]), [], [R("cbi", 0, L)], ("fixed", 2.5), ("dcb", 16), "ld cb")
+    add("sd", lambda g, T, X: g.scalar.dma_start(T.X[:, 0:W], T.x[:, :]), [], [R("X", 0, W)], ("fixed", 4.5), ("dx", 16), "ld x")
+    add("y", lambda g, T, X: g.sync.dma_start(T.wti[:, 0:1], T.wt[:, :]), [], [col("wti")], ("fixed", 2.0), ("dwt", 16), "ld wt")
+    add("y", lambda g, T, X: g.sync.dma_start(T.pki[:, :], T.pk[:, :]), [], [R("pki", 0, 1024)], ("fixed", 5.0), ("dpk", 16), "ld pk")
+    iota(col("II", 0), [[1, 1]], 0, 1, False)
+    iota(R("COL", 0, 152), [[1, 152]], -8, 0)
+    iota(whole("DZ"), [[0, 64], [16384, 8]], -8192, 0)
+    iota(whole("GC"), [[1, 8], [0, 16]], 0, 0)
     iota(R("IB0", 0, 14), [[32, 14]], 1, 0)
     iota(R("IB0", 14, 28), [[32, 14]], 0, 0)
-    iota(R("MC0", 0, 28), [[16, 28]], -448, 0)
-    ts(c1("KI"), c1("PI"), 15, None, OP.bitwise_and)
-    ts(c1("GI"), c1("PI"), 4, None, OP.logical_shift_right)
-    ts(c1("K8I"), c1("PI"), 7, None, OP.bitwise_and)
-    ts(c1("RGI"), c1("PI"), 63, 3, OP.bitwise_and, OP.logical_shift_right)
-    cp(c1("KF"), c1("KI"))
-    cp(c1("GF"), c1("GI"))
-    cp(c1("K8F"), c1("K8I"))
-    cp(c1("RGF"), c1("RGI"))
+    iota(R("MC0", 0, 28), [[16, 28]], MEND, 0)
+    for j, (s, op) in enumerate(((15, OP.bitwise_and), (4, OP.logical_shift_right), (7, OP.bitwise_and), (3, OP.logical_shift_right),
+                                 (63, OP.bitwise_and))):
+        ts(col("II", j + 1), col("II", 0), s, None, op)
+    cp(R("FF", 0, 6), R("II", 0, 6))
+    pf, kf, gf, k8, k2, p64 = (col("FF", j) for j in range(6))
+
+    def cols(a, n):
+        return R("COL", 8 + a, 8 + a + n)
     cp(R("C0", 0, HB), R("cbi", 1, L, 2), name="c16")
     cp(R("C0", HB, L), R("cbi", 0, L, 2), name="c16")
-    ts(c1("CBA"), c1("GF"), 8.0, c1("K8F"), OP.mult, OP.add)
-    ts(whole("ID6"), R("COL", 0, 128), c1("PF"), 0.0625, OP.is_equal, OP.mult)
-    ts(whole("BA"), whole("M64"), c1("CBA"), None, OP.is_equal)
-    ts(R("RM", 0, 16), R("COL", 0, 16), c1("KF"), None, OP.is_equal)
+    ts(col("CC", 0), kf, 8.0, gf, OP.mult, OP.add)
+    ts(R("EB", 0, 136), cols(-8, 136), col("CC", 0), 0.125, OP.is_equal, OP.mult)
+    ts(R("RM", 0, 16), cols(0, 16), kf, None, OP.is_equal)
     for k in range(15):
-        scaled(R("EL", 128 * k, 128 * k + 128), whole("ID6"), R("RM", k, k + 1), "EL")
-    ts(whole("ID"), R("COL", 0, 128), c1("PF"), None, OP.is_equal)
-    ts(c1("KLO"), c1("KF"), 7.5, None, OP.is_lt)
-    ts(c1("KD"), c1("KF"), 7.5, None, OP.is_gt)
-    scaled(whole("DA"), whole("BA"), c1("KLO"), "DA")
-    scaled(whole("DB"), whole("BA"), c1("KD"), "DA")
-    ms(R("HALF", 0, 1, 1, 0, 64), 0.0)
-    ms(R("HALF", 0, 1, 1, 64, 128), -0.5)
-    ts(R("RM8", 0, 8), R("COL", 0, 8), c1("K8F"), None, OP.is_equal)
-    ts(whole("ZM"), whole("GC"), c1("RGF"), None, OP.is_equal)
-    ts(R("KV", 0, 128, 1, 0, 64), R("KC", 0, 128, 1, 0, 64), 8192.0, -65536.0, OP.mult, OP.add)
-    ts(R("KV", 0, 128, 1, 64, 128), R("KC", 0, 128, 1, 64, 128), -8192.0, None, OP.mult)
-    tt(whole("ZB"), whole("ZM"), whole("KV"), OP.mult)
-    for s in range(8):
-        scaled(R("ZL", 128 * s, 128 * s + 128), whole("ZB"), R("RM8", s, s + 1), "ZL")
-    ts(c1("K2"), c1("KF"), -256.0, 2048.0, OP.mult, OP.add)
-    tt(c1("BIAS"), c1("KF"), c1("K2"), OP.mult)
-    ts(c1("CFF"), c1("GF"), 16.0, 15.0, OP.mult, OP.add)
-    ts(whole("F"), whole("COL"), c1("CFF"), None, OP.is_equal)
-    ts(R("O8", 0, 8), R("COL", 0, 8), c1("GF"), None, OP.is_equal)
-    ts(R("O80", 0, 8), R("O8", 0, 8), R("RM", 0, 1), None, OP.mult)
-    ts(c1("P1"), c1("PF"), 1.0, None, OP.add)
-    ts(whole("SH"), R("COL", 0, 128), c1("P1"), None, OP.is_equal)
-    tt(whole("DF0"), whole("ID"), whole("SH"), OP.subtract)
-    ts(whole("KM"), whole("KC"), 0.0, None, OP.is_gt)
-    tt(whole("DF"), whole("DF0"), whole("KM"), OP.mult)
-    ms(c1("NEG"), -80.5)
-    ms(c1("ONE"), 1.0)
-    ms(c1("SUMS"), 448.0)
-    cp(c1("WF"), c1("wti"))
-    scaled(whole("FW"), whole("F"), c1("WF"), "FW")
-    ts(whole("OB"), whole("GC"), c1("GF"), 0.5, OP.is_equal, OP.mult)
-    ts(c1("K2"), c1("KF"), 2.0, None, OP.mult)
-    ts(R("IB", 0, 28), R("IB0", 0, 28), c1("K2"), 1.0 / 512, OP.add, OP.mult)
-    ts(R("MC", 0, 28), R("MC0", 0, 28), c1("KF"), 1.0 / 2048, OP.add, OP.mult)
-    ts(whole("ID16"), R("COL", 0, 128), c1("PF"), None, OP.is_equal)
-    ts(whole("NI16"), whole("ID16"), -1.0, None, OP.mult)
+        scaled(R("EL", 128 * k, 128 * k + 128), R("EB", 0, 128), col("RM", k), "EL")
+    ts(col("CC", 1), gf, 8.0, k8, OP.mult, OP.add)
+    ts(col("CC", 2), kf, 7.5, 32.0, OP.is_gt, OP.mult)
+    ts(col("CC", 3), col("CC", 2), 0.125, None, OP.max)
+    ts(whole("XP"), cols(0, 64), col("CC", 1), col("CC", 3), OP.is_equal, OP.mult)
+    ts(whole("I64"), cols(0, 64), p64, None, OP.is_equal)
+    for j in range(8):
+        scaled(R("PW", j, 512, 8), whole("I64"), float(j * 2 ** 17), "PW")
+    ms(R("DZ", 0, 512, 8), -float(2 ** 24))
+    ts(whole("IDF"), cols(0, 128), pf, None, OP.is_equal)
+    ts(col("CC", 4), k8, 16.0, k2, OP.mult, OP.add)
+    ts(col("CC", 5), k2, 0.5, None, OP.is_gt)
+    ts(col("CC", 6), k2, 14.5, None, OP.is_lt)
+    ts(whole("PM"), cols(0, 128), col("CC", 4), None, OP.is_equal)
+    ts(whole("PK"), cols(0, 128), col("CC", 4), col("CC", 5), OP.is_equal, OP.mult)
+    ts(whole("SH"), cols(-1, 128), col("CC", 4), col("CC", 6), OP.is_equal, OP.mult)
+    tt(whole("DF"), whole("PK"), whole("SH"), OP.subtract)
+    ms(col("CC", 7), -80.5)
+    ms(col("SUMS"), 448.0)
+    ts(col("CC", 8), gf, 16.0, 15.0, OP.mult, OP.add)
+    ts(whole("F"), cols(0, 144), col("CC", 8), None, OP.is_equal)
+    ts(col("CC", 9), k8, 16.0, 15.0, OP.mult, OP.add)
+    ts(whole("FK"), cols(0, 144), col("CC", 9), 8.0, OP.is_equal, OP.mult)
+    ts(col("WI", 0), col("wti"), 3, None, OP.bitwise_and)
+    ts(col("WI", 2), col("wti"), 37.0, None, OP.mult)
+    ts(col("WI", 1), col("WI", 2), W - 1, None, OP.bitwise_and)
+    cp(R("W2", 0, 2), R("WI", 0, 2))
+    mm([(R("pW", 0, 2), R("EB", 8, 136), R("W2", 0, 2), True, True)], "w")
+    ts(whole("F4"), whole("FK"), col("pW", 0), None, OP.mult)
+    ts(whole("F37"), whole("FK"), col("pW", 1), None, OP.mult)
+    ts(whole("OB"), whole("GC"), gf, 0.5, OP.is_equal, OP.mult)
+    ts(col("CC", 10), kf, 2.0, None, OP.mult)
+    ts(R("IB", 0, 28), R("IB0", 0, 28), col("CC", 10), 1.0 / 512, OP.add, OP.mult)
+    ts(R("MC", 0, 28), R("MC0", 0, 28), kf, 1.0 / 2048, OP.add, OP.mult)
+    ts(whole("ID16"), cols(0, 128), pf, None, OP.is_equal)
+    scaled(whole("NI16"), whole("ID16"), -1.0, "NI")
     for k in range(1, 16):
-        ts(R("S16", 128 * k, 128 * k + 128), whole("ID16"), R("RM", k, k + 1), None, OP.mult, cyc=0.5, name="S16")
-    ts(whole("tlo"), whole("pki"), W - 1, None, OP.bitwise_and)
-    cp(R("B", BTAB, BTAB + 1024), whole("tlo"))
-    ts(whole("thi"), whole("pki"), 11, None, OP.logical_shift_right)
-    cp(R("B", BTAB + 1024, BTAB + 2048), whole("thi"))
-    cp(whole("CF0"), whole("C0"), 0.5)
+        scaled(R("S16", 128 * k - 128, 128 * k), whole("ID16"), col("RM", k), "S16")
+    ts(whole("tlo"), whole("pki"), W - 1, None, OP.bitwise_and, name="unpk")
+    cp(R("B", 0, 1024), whole("tlo"), name="unpk")
+    ts(whole("thi"), whole("pki"), 11, None, OP.logical_shift_right, name="unpk")
+    cp(R("B", 1024, 2048), whole("thi"), name="unpk")
+    cp(whole("CF0"), whole("C0"), 0.5, name="cf")
 
-    xw, bw = R("X", 0, W), R("B", BTAB, BTAB + W)
-    ub, un = ["pU0", "pU1", "pU2"], 0
+    xw, bw = R("X", 0, W), R("B", 0, W)
+    ub = ["pU0", "pU1", "pU2"]
     nc = len(CHUNKS)
 
     for t in range(NT):
         C, CF, V, LS = "C%d" % (t % 2), "CF%d" % (t % 2), "V%d" % (t % 2), "LS%d" % (t % 2)
+        un, so = 0, 0
 
         def send(what, src, dst, t=t):
             def fn(g, T, X):
                 rid, pid, m = X[t]
                 return g.remote_dma(ap(T, dst), ap(T, src), T.sem["r%s%d" % (what, t)], T.sem["l%s%d" % (what, t)], pid, rid, m)
-            i = add("g", fn, [src], [], 0.6, ("l%s%d" % (what, t), nsig), "send " + what)
-            add("x", None, [], [dst], 2.2, ("r%s%d" % (what, t), nsig), "recv " + what, [i])
+            i = add("g", fn, [src], [], ("fixed", 0.6), ("l%s%d" % (what, t), nsig), "send " + what)
+            add("x", None, [], [dst], ("fixed", 2.2), ("r%s%d" % (what, t), nsig), "recv " + what, [i])
+
+        def wrap(out, lh, src, a0, a1, name, first=()):
+            mm(list(first) + [(out, R(lh, 15 - b, 143 - b), R(src, 16 * a0 + b, 16 * a1, 16), b == 0 and not first, b == 15)
+                              for b in range(16)], name)
+
+        def places(ph, a0, a1):
+            ts(R("t1", a0, a1), ph, col("pW", 64), 512.0, OP.add, OP.mult, name="t1")
+            ts(R("t2", a0, a1), R("t1", a0, a1), W - 1, None, OP.bitwise_and, name="t2")
+            tt(R("t3", a0, a1), R("t2", a0, a1), R("rej", a0, a1), OP.add, name="t3")
+            cp(R(LS, a0, a1), R("t3", a0, a1), name="list")
+
+        def sums(ph, pn, a0, a1, what):
+            if what == "h":
+                wrap(ph, "F4", "VK", a0, a1, "h4", [(ph, whole("ID16"), R("IB", a0, a1), True, False)])
+            else:
+                wrap(pn, "F", "SG", a0, a1, "n")
+                ts(R("rej", a0, a1), pn, -5.0, 2048.0, OP.is_gt, OP.mult, name="rej")
 
         send("C", R(C, 0, HB), R("rc%d" % t, 0, HB))
         for c, (i0, n) in enumerate(CHUNKS):
             i1, g0, ck[0] = i0 + n, 16 * i0, c
-            for j in range(i0, i1, PIECE):
-                e = min(j + PIECE, i1)
+            for j in range(i0, i1, PLAN["xp"]):
+                e = min(j + PLAN["xp"], i1)
                 gat("vs", R("G", 16 * j, 16 * e), xw, R(C, j, e), "XG")
-            pe = "pE%d" % (c % 2)
-            mm([(R(pe, 0, n), R("EL", 128 * k, 128 * k + 128), R("G", g0 + k, 16 * i1, 16), k == 0, k == 14) for k in range(15)], "E")
-            q, y = R("QI", i0, i1), R("Y", i0, i1)
-            ts(q, R(pe, 0, n), 0.46875, None, OP.subtract, name="q")
-            tt(y, R(pe, 0, n), q, OP.subtract, 1.0, name="y")
-            mm([(R(pe, 256, 256 + n), whole("DA"), y, True, True), (R(pe, 256 + n, 256 + 2 * n), whole("DB"), y, True, True)], "yy")
-            act(R("FT", 2 * i0, 2 * i1), R(pe, 256, 256 + 2 * n), AF.Square, bias=c1("HALF"), name="sq")
-            mm([(R("pV", 0, 128, 16, 0, n), R("G", g0, 16 * i1, 16), R("O80", 0, 8), True, True)], "v0")
-            per = 512 // n
-            for b in range(0, 15, per):
-                kk = list(range(1, 16))[b:b + per]
+            pe = R("pE%d" % (c % 2), 0, n)
+            el = [(pe, R("EL", 128 * k, 128 * k + 128), R("G", g0 + k, 16 * i1, 16), k == 0, k == 14) for k in range(15)]
+            mm(el, "E")
+            q, y, bt, s = (R(b, i0, i1) for b in ("QI", "Y", "BT", "S"))
+            ts(q, pe, 0.4375, None, OP.subtract, name="q")
+            tt(y, pe, q, OP.subtract, 1.0, name="y")
+            ts(bt, q, 1, None, OP.bitwise_and, name="bit")
+            ts(s, bt, -2040.0, 2048.0, OP.mult, OP.add, name="s")
+            pt = []
+            for hs in ([(0,), (1,)] if n > 64 else [(0, 1)]):
                 u = ub[un % 3]
                 un += 1
-                lst = []
-                for x, k in enumerate(kk):
-                    o, s, h = R(u, x * n, x * n + n), (k - 1) % 8, (k - 1) // 8
-                    lst.append((o, whole("ID"), R("G", g0 + k, 16 * i1, 16), True, False))
-                    lst.append((o, R("ZL", 128 * s, 128 * s + 128), R("FT", 2 * i0 + h * n, 2 * i0 + h * n + n), False, True))
-                mm(lst, "U")
-                r0 = 15 * i0 + b * n
-                ro, ui = R("R", r0, r0 + len(kk) * n), R(u, 0, len(kk) * n)
-
-                def fv(g, T, X, ro=ro, ui=ui):
-                    return g.vector.tensor_scalar(ap(T, ro), ap(T, ui), T.BIAS[:, 0:1], 0.0, OP.add, OP.max)
-
-                def fs(g, T, X, ro=ro, ui=ui):
-                    return g.scalar.activation(ap(T, ro), ap(T, ui), AF.Relu, bias=T.BIAS[:, 0:1])
-                add("vs", {"v": fv, "s": fs}, [ui, c1("BIAS")], [ro], 0.08 + len(kk) * n * CY, name="relu")
-                mm([(R("pV", k, 128, 16, 0, n), R("R", 15 * i0 + (k - 1) * n, 15 * i0 + k * n), R("O8", 0, 8), True, True) for k in kk], "v")
-            vv, vt = R(V, i0, i1), R("VT", 128 * c, 128 * c + 128, 1, 0, n)
-            act(vt, R("pV", 0, 128, 1, 0, n), AF.Copy, name="vt")
-            mm([(R("pS", 128, 128 + n), vt, R("ID", 0, n, 1, 0, n), True, True)], "vn")
-            act(vv, R("pS", 128, 128 + n), AF.Copy, name="vcopy")
-            mm([(R("pS", 0, n), whole("DF"), vv, True, True)], "d")
-            act(R("AB", i0, i1), R("pS", 0, n), AF.Abs, name="abs")
-            act(R("SG", i0, i1), R("AB", i0, i1), AF.Sign, bias=c1("NEG"), accum=R("SUMS", c + 1, c + 2), name="sign")
-            act(R("CR", i0, i1), R("SG", i0, i1), AF.Relu, name="cr")
-            if i1 == HB:
+                xs, ps = [], []
+                for h in hs:
+                    p0 = 64 * h if len(hs) == 2 else 0
+                    xs += [(R(u, 64 * k, 64 * k + 64, 1, p0, p0 + n), R("G", g0 + 8 * h + k, 16 * i1, 16), whole("XP"), k == 0, False)
+                           for k in range(8)]
+                    ps.append((R(u, 0, 512, 1, p0, p0 + n), R("Y", i0, i1, 1, 64 * h, 64 * h + 64), R("PW", 0, 512, 1, 64 * h, 64 * h + 64),
+                               False, True))
+                    if len(hs) == 2:
+                        pt.append((R("pT", 0, n, 1, p0, p0 + 64), R("SO", so + 7, so + 512, 8, p0, p0 + n), R("IDF", p0, p0 + n, 1, p0, p0 + n), True, True))
+                mm(xs, "X")
+                mm(ps, "pen")
+                o, ui = R("SO", so, so + 512), R(u, 0, 512)
+                add("v", lambda g, T, X, o=o, ui=ui: g.vector.tensor_tensor_scan(ap(T, o), T.DZ[:, :], ap(T, ui), 0.0, OP.add, OP.max),
+                    [ui, whole("DZ")], [o], ("plain", 512), name="scan")
+                so += 512
+            mm(pt or [(R("pT", 0, n), R("SO", so - 1017, so, 8), whole("IDF"), True, True)], "back", True)
+            ti, a8, vk = (R(b, i0, i1) for b in ("TI", "A8", "VK"))
+            tt(ti, R("pT", 0, n), s, OP.mult, 1.0, name="tt")
+            ts(a8, ti, 8, 255, OP.logical_shift_right, OP.bitwise_and, name="and")
+            cp(vk, a8, name="cvt")
+            mm([(R("pD", 0, n), whole("DF"), vk, True, True), (R("pD", 128, 128 + n), whole("PM"), vk, True, True)], "d")
+            act(R("AB", i0, i1), R("pD", 0, n), AF.Abs, name="abs")
+            act(R("SG", i0, i1), R("AB", i0, i1), AF.Sign, bias=col("CC", 7), accum=col("SUMS", c + 1), name="sign")
+            act(R(V, i0, i1), R("pD", 128, 128 + n), AF.Copy, name="vcopy")
+            if i0 < HB <= i1:
                 send("V", R(V, 0, HB), R("rv%d" % t, 0, HB))
-        for c, (i0, n) in enumerate(CHUNKS):
-            i1, g0, ck[0], pb = i0 + n, 16 * i0, c, ("pB", "pV", "pE1", "pS")[c]
-            for j in range(i0, i1, PIECE):
-                e = min(j + PIECE, i1)
-                gat("v", R("GB", 16 * j, 16 * e), bw, R(C, j, e), "BG")
-            bl = ([(R(pb, 0, n), R("S16", 128 * k, 128 * k + 128), R("GB", g0 + k, 16 * i1, 16), k == 1, False) for k in range(1, 16)]
-                  + [(R(pb, 0, n), whole("NI16"), R(CF, i0, i1), False, True)])
+                sums(R("pW", 0, 14), None, 0, 14, "h")
+                sums(None, R("pW", 32, 46), 0, 14, "n")
+        ck[0] = 9
+        sa, su, sl = col("SA"), R("SUMS", 0, nc), col("SUMS", nc)
+        add("v", lambda g, T, X, sa=sa, su=su: g.vector.tensor_reduce(ap(T, sa), ap(T, su), AxisListType.X, OP.add), [su], [sa], ("plain", 4), name="SA")
+        mm([(col("pW", 64), whole("OB"), sa, True, False), (col("pW", 64), whole("OB"), sl, False, True)], "A", True)
+        places(R("pW", 0, 14), 0, 14)
+        send("L", R(LS, 0, 14), R("rl%d" % t, 0, 14))
+        ck[0] = 8
+        sums(R("pE1", 0, 14), None, 14, 28, "h")
+        sums(None, R("pT", 0, 14), 14, 28, "n")
+        places(R("pE1", 0, 14), 14, 28)
+        wrap(R("pE0", 0, 28), "F37", "VK", 0, 28, "h37")
+        ts(R("n5", 0, 28), R("pE0", 0, 28), col("pW", 64), None, OP.add, name="n5")
+        ts(R("n6", 0, 28), R("n5", 0, 28), W - 1, None, OP.bitwise_and, name="n6")
+        tt(R("dl", 0, 28), R("rej", 0, 28), R("MC", 0, 28), OP.mult, name="dl")
+        tt(R("n7", 0, 28), R("n6", 0, 28), R("dl", 0, 28), OP.max, name="n7")
+        cp(R("NL", 0, 28), R("n7", 0, 28), name="NL")
+        for c, (i0, n) in enumerate(PLAN["bc"]):
+            i1, g0, ck[0], pb = i0 + n, 16 * i0, c, R(("pU1", "pU2", "pU0", "pD")[c], 0, n)
+            for j in range(i0, i1, PLAN["bp"]):
+                e = min(j + PLAN["bp"], i1)
+                gat("vs", R("GB", 16 * j, 16 * e), bw, R(C, j, e), "BG")
+            bl = ([(pb, whole("NI16"), R(CF, i0, i1), True, False)]
+                  + [(pb, R("S16", 128 * k - 128, 128 * k), R("GB", g0 + k, 16 * i1, 16), False, k == 15) for k in range(1, 16)])
             for j in range(0, 16, 4):
                 mm(bl[j:j + 4], "BX")
-            tt(R("M2", i0, i1), R(pb, 0, n), R("CR", i0, i1), OP.mult, 1.0, name="m2")
-            mm([(R(pb, 256, 256 + n), whole("ID16"), R("M2", i0, i1), True, False),
-                (R(pb, 256, 256 + n), whole("ID16"), R(CF, i0, i1), False, True)], "mend")
-            act(R("B", MEND + i0, MEND + i1), R(pb, 256, 256 + n), AF.Copy, name="mend")
+            cr, sg, pm = R("CR", i0, i1), R("SG", i0, i1), R(pb[0], 256, 256 + n)
+            add("vs", {"v": lambda g, T, X, cr=cr, sg=sg: g.vector.tensor_scalar(ap(T, cr), ap(T, sg), 0.0, None, OP.max),
+                       "s": lambda g, T, X, cr=cr, sg=sg: g.scalar.activation(ap(T, cr), ap(T, sg), AF.Relu)},
+                [sg], [cr], ("plain", n * 0.75), name="cr")
+            tt(R("M2", i0, i1), pb, cr, OP.mult, 1.0, name="m2")
+            mm([(pm, whole("ID16"), R(CF, i0, i1), True, False), (pm, whole("ID16"), R("M2", i0, i1), False, True)], "mend")
+            move(R("B", MEND + i0, MEND + i1), pm, "mendc")
         ck[0] = 9
-
-        def wrap(bank, lh, src, name):
-            mm([(R(bank, 0, 28), R(lh, 15 - b, 143 - b), R(src, b, L, 16), b == 0, b == 15) for b in range(16)], name)
-        wrap("pU0", "FW", V, "h")
-        cp(R("n1", 0, 28), R("pU0", 0, 28), name="h1")
-        ts(R("n2", 0, 28), R("n1", 0, 28), 2047, None, OP.bitwise_and, name="h2")
-        tt(R("hbf", 0, 28), R("n2", 0, 28), R("IB", 0, 28), OP.add, name="hb")
-        sa, su, sl = c1("SA"), R("SUMS", 0, nc), R("SUMS", nc, nc + 1)
-        add("v", lambda g, T, X, sa=sa, su=su: g.vector.tensor_reduce(ap(T, sa), ap(T, su), AxisListType.X, OP.add), [su], [sa], vc(4), name="SA")
-        mm([(R("pU2", 0, 1), whole("OB"), sa, True, False), (R("pU2", 0, 1), whole("OB"), sl, False, True)], "A", True)
-        wrap("pU1", "F", "SG", "n")
-        ts(R("rej", 0, 28), R("pU1", 0, 28), -5.0, 2048.0, OP.is_gt, OP.mult, name="rej")
-        act(R("acc", 0, 28), R("rej", 0, 28), AF.Identity, bias=c1("ONE"), scale=-1.0 / 2048, name="acc")
-        ts(R("t1", 0, 28), R("hbf", 0, 28), R("pU2", 0, 1), 512.0, OP.add, OP.mult, name="t1")
-        ts(R("t2", 0, 28), R("t1", 0, 28), 2047, None, OP.bitwise_and, name="t2")
-        tt(R("t3", 0, 28), R("t2", 0, 28), R("rej", 0, 28), OP.add, name="t3")
-        cp(R(LS, 0, 28), R("t3", 0, 28), name="list")
-        send("L", R(LS, 0, 14), R("rl%d" % t, 0, 14))
-        ts(R("n5", 0, 28), R("n2", 0, 28), 37.0, R("pU2", 0, 1), OP.mult, OP.add, name="n1")
-        ts(R("n6", 0, 28), R("n5", 0, 28), 2047, None, OP.bitwise_and, name="n2")
-        tt(R("n3", 0, 28), R("n6", 0, 28), R("acc", 0, 28), OP.mult, name="n3")
-        tt(R("dl", 0, 28), R("rej", 0, 28), R("MC", 0, 28), OP.mult, name="dl")
-        tt(R("n4", 0, 28), R("n3", 0, 28), R("dl", 0, 28), OP.add, name="n4")
-        ts(R("NL", 0, 28), R("n4", 0, 28), 448.0, None, OP.add, name="NL")
-        xs, bs = R("X", 0, XW), R("B", BTAB, BW)
+        xs, bs = R("X", 0, XW), R("B", 0, MEND)
         ls, rl = R(LS, 14, 28), R("rl%d" % t, 0, 14)
         sca(xs, ls, R(V, HB, L), "XS even")
         sca(bs, ls, R(C, HB, L), "BS even")
@@ -314,16 +319,16 @@ def build_ops(nsig):
         rest = [(xs, R("rv%d" % t, 0, HB), "XS odd"), (bs, R("rc%d" % t, 0, HB), "BS odd")]
         for w, s, nm in (rest if last else rest[::-1]):
             sca(w, rl, s, nm)
-        bn = R("B", 0, BTAB + W)
+        bn = whole("B")
         if last:
-            add("y", lambda g, T, X: g.sync.dma_start(T.yx[:, :], T.X[:, 0:W]), [R("X", 0, W)], [], 4.0, ("oyx", 16), "st x")
+            add("y", lambda g, T, X: g.sync.dma_start(T.yx[:, :], T.X[:, 0:W]), [R("X", 0, W)], [], ("fixed", 4.0), ("oyx", 16), "st x")
             gat("v", R("YC", 1, L, 2), bn, R("NL", 0, 14), "nxt")
             gat("s", R("YC", 0, L, 2), bn, R("NL", 14, 28), "nxt")
-            add("y", lambda g, T, X: g.sync.dma_start(T.yc[:, :], T.YC[:, :]), [R("YC", 0, L)], [], 2.5, ("oyc", 16), "st c")
+            add("y", lambda g, T, X: g.sync.dma_start(T.yc[:, :], T.YC[:, :]), [R("YC", 0, L)], [], ("fixed", 2.5), ("oyc", 16), "st c")
         else:
             D, DF_ = "C%d" % ((t + 1) % 2), "CF%d" % ((t + 1) % 2)
-            gat("v", R(D, 0, HB), bn, R("NL", 0, 14), "nxt")
-            gat("v", R(D, HB, L), bn, R("NL", 14, 28), "nxt")
+            for i0, i1 in PLAN["nx"]:
+                gat("v", R(D, i0, i1), R("B", 0, MEND + i1), R("NL", i0 // 16, i1 // 16), "nxt")
             cp(whole(DF_), whole(D), 0.5, name="cf")
     return ops
 
@@ -345,7 +350,7 @@ def depend(ops):
                 same = ops[j]["eng"] == o["eng"] and o["eng"] in ("t", "v", "s", "g")
                 over = hit(r, q) and (wr or qw)
                 if same and o["eng"] == "t":
-                    if over:
+                    if over or ps:
                         d[j] = d.get(j, False)
                 elif over or (ps and not same):
                     d[j] = True
@@ -361,12 +366,13 @@ def depend(ops):
 
 
 def force(ops):
-    f, k = {}, {"XG": 0, "relu": 0}
-    tot = {z: sum(o["name"] == z for o in ops) // NT for z in k}
+    f, k = {}, {z: 0 for z in PLAN["eng"]}
+    tot = {z: max(1, sum(o["name"] == z for o in ops) // NT) for z in k}
     for i, o in enumerate(ops):
         z = o["name"]
         if z in k:
-            f[i] = PLAN[("x" if z == "XG" else "r") + ("0" if k[z] < tot[z] else "1")][k[z] % tot[z]]
+            p = PLAN["eng"][z]
+            f[i] = p[(k[z] % tot[z]) % len(p)]
             k[z] += 1
     return {i: ("vs" if v == "x" else v) for i, v in f.items()}
 

@@ -1,29 +1,30 @@
+import math
 from concourse.mybir import AluOpType as OP, AxisListType, ActivationFunctionType as AF
 
 N, NT = 4, 4
 L, HB, W = 448, 224, 2048
-CHUNKS = [(0, 128), (128, 128), (256, 128), (384, 64)]
-BCHUNKS = [(0, 224), (224, 224)]
 MEND = 4096
 BW, XW = MEND + L, 4096
-PLAN = {'eng': {'XG': 'xxxxsss', 'BG': 'sxxssxx', 'mendc': 'sss', 'cr': 'vss'}, 'xp': 64, 'bp': 64,
-        'adj': {'BG': -9.8, 'unpk': 47.2, 'S16': -2.7, 's': 8.6, 'd': 1.0, 'back@1': 1.7, 'EL': -2.5, 'tt@3': 4.2, 'XS even': 6.9, 'PW': -1.5, 'h37': 1.1, 'E@2': -5.0, 'y': 3.3, 'and@0': 0.6, 'n6': 0.1, 'tt@0': -0.4, 'send C': 3.9, 'dl': -0.1, 'BS even': -0.3, 'd@3': -0.3, 'n': -0.7, 'q@2': 7.8, 'rej': -2.5, 's@3': 2.4, 'NL': -3.1, 'pen@1': -0.6, 't1': 2.1, 'n7': 3.4},
-        'delta': 0.0, 'wf': 0.17, 'bc': [(0, 128), (128, 128), (256, 192)], 'nx': [(0, 128), (128, 448)]}
+PLAN = {'ch': [128, 128, 128, 64], 'xg': [32, 32] + [64] * 6, 'bg': [64, 64, 64, 64, 64, 48, 48, 32], 'bc': [128, 128, 192], 'nx': [128, 128, 192],
+        'pc': [256, 128, 64], 'sc': [256, 192], 'pool': ["cvt", "cf"], 'defer': 256, 'deferg': 448, 'ec': [64, 64, 128, 128, 64],
+        'bb': ["pU1", "pU2", "pD"]}
+ORDER = {'v': 'cb XG1 m22 XG4 unpk mendc2 q0 nxt4 q1 y0 y1 XG6 q2 y2 scan0 bit2 scan0b scan1 scan1b q3 y4 bit4 tt0 y3 and0 ce cvt0 scan2 scan2b scan3 tt1 vcopy0 and1 tt2 cvt1 and2 cvt2 cg rej7 BG3 t1 vcopy2 t2 e1 t3 k1 list k2 rej dl e3 k3 BG7 BSeven m20 m21 XSeven BSodd XSodd zm22 outb', 's': 'ca XG0 XG2 cc XG3 XG7 XG5 cd unph q4 s2 BG5 BG0 abs0 s4 sign0 BG1 abs1 vcopy1 sign1 abs2 sign2 BG2 NL BG4 BG6 mendc0 mendc1 nxt0 nxt2 out zmendc2', 't': 'BX2 BX2b BX2c BX2d E0 mend2 E1 X0 w X0b E2 pen0 X1 pen0b E4 pen1 X1b pen1b E3 back0 back1 X2 X3 pen2 X2b pen2b d0 vn0 pen3 back2 h47 back3 n7 d1 vn1 h4 d2 vn2 Aa A h37 n BX0 BX0b BX0c BX1 BX1b BX0d BX1c BX1d mend1 mend0 zBX2 zBX2b zBX2c zBX2d zmend2', 'g': 'cf late sendC SL sendV7 sendL', 'y': 'cpB stx stc'}
 
 F32, B16, I32, U16, H16 = "float32", "bfloat16", "int32", "uint16", "float16"
 SCRATCH = {}
 for _n, _w, _d in (
-        ("X", XW, B16), ("B", BW, F32), ("pki", 1024, I32), ("tlo", 1024, I32), ("thi", 1024, I32), ("cbi", L, I32), ("wti", 8, I32),
-        ("C0", L, U16), ("C1", L, U16), ("CF0", L, H16), ("CF1", L, H16), ("G", 16 * L, H16), ("GB", 16 * L, H16), ("SO", 3584, F32),
-        ("QI", L, I32), ("Y", L, B16), ("BT", L, I32), ("S", L, B16), ("TI", L, I32), ("A8", L, I32), ("VK", L, H16),
-        ("V0", L, B16), ("V1", L, B16), ("AB", L, B16), ("SG", L, B16), ("M2", L, H16), ("YC", L, F32), ("SUMS", 8, F32), ("SA", 8, F32),
-        ("rej", 32, F32), ("t1", 32, I32), ("t2", 32, I32), ("t3", 32, F32), ("n5", 32, I32), ("n6", 32, I32), ("n7", 32, F32),
-        ("dl", 32, F32), ("LS0", 32, U16), ("LS1", 32, U16), ("NL", 32, U16),
-        ("II", 8, I32), ("FF", 8, F32), ("CC", 16, F32), ("WI", 8, I32), ("W2", 8, H16), ("COL", 160, F32), ("GC", 128, F32),
+        ("X", XW, B16), ("B0", BW, I32), ("B1", BW, I32), ("pki", 1024, I32), ("cbi", L, I32), ("wti", 8, I32),
+        ("C0", L, U16), ("C1", L, U16), ("CF0", L, H16), ("CF1", L, H16), ("G", 16 * L, B16), ("GB", 16 * L, H16), ("SO", 4096, F32),
+        ("QI", L, I32), ("Y", L, B16), ("BT", L, I32), ("S", L, B16), ("TI", L, I32), ("A8", L, I32), ("VK", L, B16),
+        ("V0", L, B16), ("V1", L, B16), ("AB", L, B16), ("SG", L, B16), ("M2", L, H16), ("YC", L, F32),
+        ("SUMS", 8, F32), ("SA", 8, F32), ("SJ", 8, F32), ("rej", 32, F32), ("dl", 32, F32), ("t1", 64, I32), ("t2", 64, I32),
+        ("t3", 64, F32), ("LS0", 16, U16), ("LS1", 16, U16), ("NL", 48, U16),
+        ("II", 8, I32), ("FF", 8, F32), ("CC", 16, F32), ("WI", 8, I32), ("W2", 8, H16), ("COL", 144, F32), ("GC", 128, F32),
         ("DZ", 512, F32), ("IB0", 32, F32), ("IB", 32, H16), ("MC0", 32, F32), ("MC", 32, F32), ("RM", 16, F32),
-        ("EB", 144, H16), ("EL", 15 * 128, H16), ("XP", 64, H16), ("I64", 64, B16), ("PW", 512, B16), ("IDF", 128, F32),
-        ("PM", 128, H16), ("PK", 128, H16), ("SH", 128, H16), ("DF", 128, H16), ("F", 144, B16), ("FK", 144, H16), ("F4", 144, H16),
-        ("F37", 144, H16), ("OB", 128, F32), ("ID16", 128, H16), ("CR", L, B16), ("NI16", 128, H16), ("S16", 15 * 128, H16)):
+        ("ONE", 128, B16), ("ONF", 128, F32), ("EIG", 144, B16), ("EB", 144, B16), ("EL", 15 * 128, B16), ("XP0", 64, B16),
+        ("XP", 64, B16), ("I640", 64, B16), ("I64", 64, B16), ("PW", 512, B16), ("IDF", 128, F32), ("PM", 128, B16), ("DF", 128, B16),
+        ("F", 144, B16), ("FK", 144, B16), ("F4", 144, B16), ("F37", 144, H16), ("OB", 128, F32), ("ID", 128, B16), ("NI", 128, B16),
+        ("SL", 15 * 128, B16), ("IA", 128, B16), ("IB4", 128, B16), ("PD", 128, B16)):
     SCRATCH[_n] = ("sbuf", [128, _w], _d)
 for _t in range(NT):
     SCRATCH["rc%d" % _t] = ("sbuf", [128, HB], U16)
@@ -31,7 +32,7 @@ for _t in range(NT):
     SCRATCH["rl%d" % _t] = ("sbuf", [128, 16], U16)
 for _n in ("pE0", "pE1", "pU0", "pU1", "pU2", "pT", "pD", "pW"):
     SCRATCH[_n] = ("psum", [128, 512], F32)
-SEMAPHORES = (["qv", "qs", "qt", "qg", "dcb", "dx", "dpk", "dwt", "oyx", "oyc"]
+SEMAPHORES = (["qv", "qs", "qt", "qg", "dcb", "dx", "dpk", "dwt", "oyx", "oyc"] + ["dcp%d" % t for t in range(NT)]
               + [a + b + str(t) for a in "rl" for b in "CVL" for t in range(NT)])
 
 CY, TCY, GAM, SCA, LAT = 0.00083 * 1.1, 0.00042 * 1.1, 1.45, 3.5, 0.1
@@ -52,6 +53,14 @@ def val(T, s):
     return ap(T, s) if isinstance(s, tuple) else s
 
 
+def cuts(sizes):
+    out, a = [], 0
+    for n in sizes:
+        out.append((a, a + n))
+        a += n
+    return out
+
+
 def cost_of(el):
     kind, n = el
     return {"plain": 0.06 + max(64, n) * CY, "gat": 0.06 + n * GAM * CY, "sca": 0.06 + n * SCA * CY, "pe": 0.03 + n * TCY,
@@ -59,52 +68,63 @@ def cost_of(el):
 
 
 def build_ops(nsig):
-    ops, ck = [], [9]
+    ops, ck = [], [9, -1]
 
     def add(eng, fn, reads, writes, el, tok=None, name="", after=()):
-        ops.append(dict(eng=eng, fn=fn, reads=list(reads), writes=list(writes), el=el, cost=cost_of(el), tok=tok, name=name,
-                        after=list(after), ck=ck[0]))
+        ops.append(dict(eng=eng, fn=fn, reads=list(reads), writes=list(writes), el=el, tok=tok, name=name, after=list(after), ck=ck[0], rd=ck[1]))
         return len(ops) - 1
 
     def ne(a):
         return -((a[1] - a[2]) // a[3])
 
-    def cp(out, in_, cyc=1.0, name="copy"):
-        add("v", lambda g, T, X: g.vector.tensor_copy(ap(T, out), ap(T, in_)), [in_], [out], ("plain", ne(out) * cyc), name=name)
+    def half(*sides):
+        return 0.5 if all(SCRATCH[s[0]][2] in (B16, H16, U16) for s in sides) else 1.0
 
-    def ts(out, in0, s1, s2, op0, op1=None, cyc=1.0, name="ts"):
+    def both(out, reads, fv, fs, name, kind="plain"):
+        n = ne(out)
+        add("vs", {"v": fv, "s": fs}, reads, [out], {"v": (kind, n * (half(out, reads[0]) if kind == "plain" else 1)), "s": (kind, n)}, name=name)
+
+    def ts(out, in0, s1, s2, op0, op1=None, name="ts"):
         def fn(g, T, X):
             if op1 is None:
                 return g.vector.tensor_scalar(ap(T, out), ap(T, in0), val(T, s1), None, op0)
             return g.vector.tensor_scalar(ap(T, out), ap(T, in0), val(T, s1), val(T, s2), op0, op1)
-        add("v", fn, [in0] + [s for s in (s1, s2) if isinstance(s, tuple)], [out], ("plain", ne(out) * cyc), name=name)
+        add("v", fn, [in0] + [s for s in (s1, s2) if isinstance(s, tuple)], [out], ("plain", ne(out) * half(out, in0)), name=name)
 
-    def tt(out, a, b, op, cyc=2.0, name="tt"):
+    def tt(out, a, b, op, name="tt"):
+        cyc = 1.0 if SCRATCH[a[0]][0] == "psum" else 2.0
         add("v", lambda g, T, X: g.vector.tensor_tensor(ap(T, out), ap(T, a), ap(T, b), op), [a, b], [out], ("plain", ne(out) * cyc), name=name)
 
     def ms(out, x):
-        add("v", lambda g, T, X: g.vector.memset(ap(T, out), x), [], [out], ("plain", ne(out)), name="memset")
+        add("v", lambda g, T, X: g.vector.memset(ap(T, out), x), [], [out], ("plain", ne(out) * half(out)), name="memset")
 
-    def act(out, in_, func, bias=0.0, scale=1.0, accum=None, name="act"):
+    def act(out, in_, func, bias=0.0, accum=None, name="act"):
         def fn(g, T, X):
             if accum is None:
-                return g.scalar.activation(ap(T, out), ap(T, in_), func, bias=val(T, bias), scale=val(T, scale))
-            return g.scalar.activation(ap(T, out), ap(T, in_), func, bias=val(T, bias), scale=val(T, scale), accum_out=ap(T, accum))
-        add("s", fn, [in_] + [s for s in (bias, scale) if isinstance(s, tuple)], [out] + ([accum] if accum else []), ("plain", ne(out)), name=name)
+                return g.scalar.activation(ap(T, out), ap(T, in_), func, bias=val(T, bias))
+            return g.scalar.activation(ap(T, out), ap(T, in_), func, bias=val(T, bias), accum_out=ap(T, accum))
+        add("s", fn, [in_] + ([bias] if isinstance(bias, tuple) else []), [out] + ([accum] if accum else []), ("plain", ne(out)), name=name)
 
     def move(out, in_, name):
-        add("vs", {"v": lambda g, T, X: g.vector.tensor_copy(ap(T, out), ap(T, in_)),
-                   "s": lambda g, T, X: g.scalar.activation(ap(T, out), ap(T, in_), AF.Copy)}, [in_], [out], ("plain", ne(out)), name=name)
+        both(out, [in_], lambda g, T, X: g.vector.tensor_copy(ap(T, out), ap(T, in_)),
+             lambda g, T, X: g.scalar.activation(ap(T, out), ap(T, in_), AF.Copy), name)
+        if name in PLAN["pool"]:
+            ops[-1]["eng"] = "vsg"
+            ops[-1]["el"]["g"] = ("pool", ne(out))
+            ops[-1]["fn"]["g"] = lambda g, T, X: g.affine_select(ap(T, out), ap(T, in_), [[0, ne(out)]], OP.is_ge, 0.0, 0, 0)
 
-    def scaled(o, base, by, name):
-        add("vs", {"v": lambda g, T, X: g.vector.tensor_scalar(ap(T, o), ap(T, base), val(T, by), None, OP.mult),
-                   "s": lambda g, T, X: g.scalar.activation(ap(T, o), ap(T, base), AF.Copy, scale=val(T, by))},
-            [base] + ([by] if isinstance(by, tuple) else []), [o], ("plain", ne(o) * 0.75), name=name)
+    def affine(out, in_, scale, bias, name):
+        both(out, [in_], lambda g, T, X: g.vector.tensor_scalar(ap(T, out), ap(T, in_), scale, bias, OP.mult, OP.add),
+             lambda g, T, X: g.scalar.activation(ap(T, out), ap(T, in_), AF.Copy, bias=bias, scale=scale), name)
 
-    def gat(eng, out, win, off, name):
-        add(eng, {"v": lambda g, T, X: g.vector.tensor_copy(ap(T, out), ap(T, win).indirect(ap(T, off))),
-                  "s": lambda g, T, X: g.scalar.activation(ap(T, out), ap(T, win).indirect(ap(T, off)), AF.Copy)},
-            [win, off], [out], ("gat", ne(out)), name=name)
+    def scaled(out, base, by, name):
+        both(out, [base] + ([by] if isinstance(by, tuple) else []),
+             lambda g, T, X: g.vector.tensor_scalar(ap(T, out), ap(T, base), val(T, by), None, OP.mult),
+             lambda g, T, X: g.scalar.activation(ap(T, out), ap(T, base), AF.Copy, scale=val(T, by)), name)
+
+    def gat(out, win, off, name):
+        both(out, [win, off], lambda g, T, X: g.vector.tensor_copy(ap(T, out), ap(T, win).indirect(ap(T, off))),
+             lambda g, T, X: g.scalar.activation(ap(T, out), ap(T, win).indirect(ap(T, off)), AF.Copy), name, "gat")
 
     def sca(win, off, in_, name):
         add("v", lambda g, T, X: g.vector.tensor_copy(ap(T, win).indirect(ap(T, off)), ap(T, in_)), [in_, off], [win], ("sca", ne(in_)), name=name)
@@ -125,6 +145,10 @@ def build_ops(nsig):
             return g.iota(ap(T, out), pat, base, cm)
         add("g", fn, [], [out], ("pool", ne(out)), name="iota")
 
+    def where(out, in_, pat, base, fill=None, cm=1, name="where"):
+        op = OP.is_equal if fill is None else OP.not_equal
+        add("g", lambda g, T, X: g.affine_select(ap(T, out), ap(T, in_), pat, op, fill or 0.0, base, cm), [in_], [out], ("pool", ne(out)), name=name)
+
     def col(b, j=0):
         return R(b, j, j + 1)
 
@@ -135,77 +159,67 @@ def build_ops(nsig):
     add("sd", lambda g, T, X: g.scalar.dma_start(T.X[:, 0:W], T.x[:, :]), [], [R("X", 0, W)], ("fixed", 4.5), ("dx", 16), "ld x")
     add("y", lambda g, T, X: g.sync.dma_start(T.wti[:, 0:1], T.wt[:, :]), [], [col("wti")], ("fixed", 2.0), ("dwt", 16), "ld wt")
     add("y", lambda g, T, X: g.sync.dma_start(T.pki[:, :], T.pk[:, :]), [], [R("pki", 0, 1024)], ("fixed", 5.0), ("dpk", 16), "ld pk")
+    ms(whole("EIG"), 0.125)
+    ms(whole("ONE"), 1.0)
+    ms(whole("ONF"), 1.0)
     iota(col("II", 0), [[1, 1]], 0, 1, False)
-    iota(R("COL", 0, 152), [[1, 152]], -8, 0)
+    iota(whole("COL"), [[1, 144]], 0, 0)
+    where(R("EB", 0, 136), R("EIG", 0, 136), [[-1, 17], [-16, 8]], 1)
+    where(whole("XP0"), R("EIG", 0, 64), [[-16, 8], [-1, 8]], 0)
+    where(whole("XP"), whole("XP0"), [[-16, 8], [-1, 8]], -8, 32.0)
+    where(whole("I640"), R("ONE", 0, 64), [[-1, 64]], 0)
+    where(whole("I64"), whole("I640"), [[-1, 64]], -64, 1.0)
+    where(whole("IDF"), whole("ONF"), [[-1, 128]], 0)
+    where(whole("PM"), whole("ONE"), [[-1, 8], [-8, 16]], 0)
+    where(whole("DF"), whole("PM"), [[-1, 8], [-8, 16]], 8, -1.0)
+    where(whole("ID"), whole("ONE"), [[-1, 128]], 0)
     iota(whole("DZ"), [[0, 64], [16384, 8]], -8192, 0)
     iota(whole("GC"), [[1, 8], [0, 16]], 0, 0)
-    iota(R("IB0", 0, 14), [[32, 14]], 1, 0)
-    iota(R("IB0", 14, 28), [[32, 14]], 0, 0)
+    iota(R("IB0", 0, 28), [[-1, 2], [32, 14]], 1, 0)
     iota(R("MC0", 0, 28), [[16, 28]], MEND, 0)
-    for j, (s, op) in enumerate(((15, OP.bitwise_and), (4, OP.logical_shift_right), (7, OP.bitwise_and), (3, OP.logical_shift_right),
-                                 (63, OP.bitwise_and))):
+    for j, (s, op) in enumerate(((15, OP.bitwise_and), (4, OP.logical_shift_right), (7, OP.bitwise_and))):
         ts(col("II", j + 1), col("II", 0), s, None, op)
-    cp(R("FF", 0, 6), R("II", 0, 6))
-    pf, kf, gf, k8, k2, p64 = (col("FF", j) for j in range(6))
-
-    def cols(a, n):
-        return R("COL", 8 + a, 8 + a + n)
-    cp(R("C0", 0, HB), R("cbi", 1, L, 2), name="c16")
-    cp(R("C0", HB, L), R("cbi", 0, L, 2), name="c16")
-    ts(col("CC", 0), kf, 8.0, gf, OP.mult, OP.add)
-    ts(R("EB", 0, 136), cols(-8, 136), col("CC", 0), 0.125, OP.is_equal, OP.mult)
-    ts(R("RM", 0, 16), cols(0, 16), kf, None, OP.is_equal)
+    move(R("FF", 0, 3), R("II", 1, 4), "const")
+    kf, gf, k8 = (col("FF", j) for j in range(3))
+    move(R("C0", 0, HB), R("cbi", 1, L, 2), "c16")
+    move(R("C0", HB, L), R("cbi", 0, L, 2), "c16")
+    ts(R("RM", 0, 16), R("COL", 0, 16), kf, None, OP.is_equal)
     for k in range(15):
         scaled(R("EL", 128 * k, 128 * k + 128), R("EB", 0, 128), col("RM", k), "EL")
-    ts(col("CC", 1), gf, 8.0, k8, OP.mult, OP.add)
-    ts(col("CC", 2), kf, 7.5, 32.0, OP.is_gt, OP.mult)
-    ts(col("CC", 3), col("CC", 2), 0.125, None, OP.max)
-    ts(whole("XP"), cols(0, 64), col("CC", 1), col("CC", 3), OP.is_equal, OP.mult)
-    ts(whole("I64"), cols(0, 64), p64, None, OP.is_equal)
     for j in range(8):
         scaled(R("PW", j, 512, 8), whole("I64"), float(j * 2 ** 17), "PW")
     ms(R("DZ", 0, 512, 8), -float(2 ** 24))
-    ts(whole("IDF"), cols(0, 128), pf, None, OP.is_equal)
-    ts(col("CC", 4), k8, 16.0, k2, OP.mult, OP.add)
-    ts(col("CC", 5), k2, 0.5, None, OP.is_gt)
-    ts(col("CC", 6), k2, 14.5, None, OP.is_lt)
-    ts(whole("PM"), cols(0, 128), col("CC", 4), None, OP.is_equal)
-    ts(whole("PK"), cols(0, 128), col("CC", 4), col("CC", 5), OP.is_equal, OP.mult)
-    ts(whole("SH"), cols(-1, 128), col("CC", 4), col("CC", 6), OP.is_equal, OP.mult)
-    tt(whole("DF"), whole("PK"), whole("SH"), OP.subtract)
-    ms(col("CC", 7), -80.5)
-    ms(col("SUMS"), 448.0)
-    ts(col("CC", 8), gf, 16.0, 15.0, OP.mult, OP.add)
-    ts(whole("F"), cols(0, 144), col("CC", 8), None, OP.is_equal)
-    ts(col("CC", 9), k8, 16.0, 15.0, OP.mult, OP.add)
-    ts(whole("FK"), cols(0, 144), col("CC", 9), 8.0, OP.is_equal, OP.mult)
-    ts(col("WI", 0), col("wti"), 3, None, OP.bitwise_and)
-    ts(col("WI", 2), col("wti"), 37.0, None, OP.mult)
-    ts(col("WI", 1), col("WI", 2), W - 1, None, OP.bitwise_and)
-    cp(R("W2", 0, 2), R("WI", 0, 2))
+    ms(R("DF", 0, 128, 16), 0.0)
+    ms(col("CC", 0), -80.5)
+    affine(col("CC", 1), gf, 16.0, 15.0, "ca")
+    affine(col("CC", 2), k8, 16.0, 15.0, "ca")
+    affine(col("CC", 3), kf, 2.0, 0.0, "ca")
+    affine(col("WI", 2), col("wti"), 37.0, 0.0, "ca")
+    ts(col("WI", 0), col("wti"), 3, None, OP.bitwise_and, name="cb")
+    ts(col("WI", 1), col("WI", 2), W - 1, None, OP.bitwise_and, name="cb")
+    ts(whole("FK"), whole("COL"), col("CC", 2), 8.0, OP.is_equal, OP.mult, name="cb")
+    move(R("W2", 0, 2), R("WI", 0, 2), "cc")
     mm([(R("pW", 0, 2), R("EB", 8, 136), R("W2", 0, 2), True, True)], "w")
-    ts(whole("F4"), whole("FK"), col("pW", 0), None, OP.mult)
-    ts(whole("F37"), whole("FK"), col("pW", 1), None, OP.mult)
-    ts(whole("OB"), whole("GC"), gf, 0.5, OP.is_equal, OP.mult)
-    ts(col("CC", 10), kf, 2.0, None, OP.mult)
-    ts(R("IB", 0, 28), R("IB0", 0, 28), col("CC", 10), 1.0 / 512, OP.add, OP.mult)
-    ts(R("MC", 0, 28), R("MC0", 0, 28), kf, 1.0 / 2048, OP.add, OP.mult)
-    ts(whole("ID16"), cols(0, 128), pf, None, OP.is_equal)
-    scaled(whole("NI16"), whole("ID16"), -1.0, "NI")
+    move(R("CC", 4, 6), R("pW", 0, 2), "cd")
+    scaled(whole("F4"), whole("FK"), col("CC", 4), "cd")
+    scaled(whole("F37"), whole("FK"), col("CC", 5), "cd")
+    ts(whole("F"), whole("COL"), col("CC", 1), None, OP.is_equal, name="ce")
+    ts(R("IB", 0, 28), R("IB0", 0, 28), col("CC", 3), 1.0 / 512, OP.add, OP.mult, name="ce")
+    ts(whole("OB"), whole("GC"), gf, 0.5, OP.is_equal, OP.mult, name="cg")
+    ts(R("MC", 0, 28), R("MC0", 0, 28), kf, 1.0 / 2048, OP.add, OP.mult, name="cg")
+    for b, x in (("PD", 1.0 / 4096), ("NI", -1.0 / 4096), ("IA", -2048.0), ("IB4", 4096.0)):
+        where(whole(b), whole("ID"), [[-1, 128]], 0, x, name="late")
     for k in range(1, 16):
-        scaled(R("S16", 128 * k - 128, 128 * k), whole("ID16"), col("RM", k), "S16")
-    ts(whole("tlo"), whole("pki"), W - 1, None, OP.bitwise_and, name="unpk")
-    cp(R("B", 0, 1024), whole("tlo"), name="unpk")
-    ts(whole("thi"), whole("pki"), 11, None, OP.logical_shift_right, name="unpk")
-    cp(R("B", 1024, 2048), whole("thi"), name="unpk")
-    cp(whole("CF0"), whole("C0"), 0.5, name="cf")
+        where(R("SL", 128 * k - 128, 128 * k), whole("PD"), [[0, 8], [1, 16]], -k, cm=0, name="SL")
+    ts(R("B0", 0, 1024), whole("pki"), W - 1, None, OP.bitwise_and, name="unpk")
+    affine(R("B0", 1024, 2048), whole("pki"), 1.0 / W, -0.5 + 0.5 / W, "unph")
 
-    xw, bw = R("X", 0, W), R("B", 0, W)
+    xw = R("X", 0, W)
     ub = ["pU0", "pU1", "pU2"]
-    nc = len(CHUNKS)
 
     for t in range(NT):
         C, CF, V, LS = "C%d" % (t % 2), "CF%d" % (t % 2), "V%d" % (t % 2), "LS%d" % (t % 2)
+        Bo, Bn = "B%d" % (t % 2), "B%d" % ((t + 1) % 2)
         un, so = 0, 0
 
         def send(what, src, dst, t=t):
@@ -219,33 +233,35 @@ def build_ops(nsig):
             mm(list(first) + [(out, R(lh, 15 - b, 143 - b), R(src, 16 * a0 + b, 16 * a1, 16), b == 0 and not first, b == 15)
                               for b in range(16)], name)
 
-        def places(ph, a0, a1):
-            ts(R("t1", a0, a1), ph, col("pW", 64), 512.0, OP.add, OP.mult, name="t1")
-            ts(R("t2", a0, a1), R("t1", a0, a1), W - 1, None, OP.bitwise_and, name="t2")
-            tt(R("t3", a0, a1), R("t2", a0, a1), R("rej", a0, a1), OP.add, name="t3")
-            cp(R(LS, a0, a1), R("t3", a0, a1), name="list")
+        def sums(ph, pn, a0, a1):
+            wrap(ph, "F4", "VK", a0, a1, "h4", [(ph, whole("ID"), R("IB", a0, a1), True, False)])
+            wrap(pn, "F", "SG", a0, a1, "n")
+            ts(R("rej", a0, a1), pn, -5.0, 2048.0, OP.is_gt, OP.mult, name="rej")
 
-        def sums(ph, pn, a0, a1, what):
-            if what == "h":
-                wrap(ph, "F4", "VK", a0, a1, "h4", [(ph, whole("ID16"), R("IB", a0, a1), True, False)])
-            else:
-                wrap(pn, "F", "SG", a0, a1, "n")
-                ts(R("rej", a0, a1), pn, -5.0, 2048.0, OP.is_gt, OP.mult, name="rej")
-
+        ck[:] = [9, t]
         send("C", R(C, 0, HB), R("rc%d" % t, 0, HB))
-        for c, (i0, n) in enumerate(CHUNKS):
-            i1, g0, ck[0] = i0 + n, 16 * i0, c
-            for j in range(i0, i1, PLAN["xp"]):
-                e = min(j + PLAN["xp"], i1)
-                gat("vs", R("G", 16 * j, 16 * e), xw, R(C, j, e), "XG")
+        move(whole(CF), whole(C), "cf")
+        for c, (j, e) in enumerate(cuts(PLAN["xg"])):
+            ck[0] = c
+            gat(R("G", 16 * j, 16 * e), xw, R(C, j, e), "XG")
+        ck[0] = 9
+        add("y", lambda g, T, X, a=R(Bn, 0, W), b=R(Bo, 0, W): g.sync.dma_start(ap(T, a), ap(T, b)), [R(Bo, 0, W)], [R(Bn, 0, W)],
+            ("fixed", 6.0), ("dcp%d" % t, 16), "cp B")
+        for c, (i0, i1) in enumerate(cuts(PLAN["ec"])):
+            n, g0, ck[0] = i1 - i0, 16 * i0, c
             pe = R("pE%d" % (c % 2), 0, n)
-            el = [(pe, R("EL", 128 * k, 128 * k + 128), R("G", g0 + k, 16 * i1, 16), k == 0, k == 14) for k in range(15)]
-            mm(el, "E")
-            q, y, bt, s = (R(b, i0, i1) for b in ("QI", "Y", "BT", "S"))
-            ts(q, pe, 0.4375, None, OP.subtract, name="q")
-            tt(y, pe, q, OP.subtract, 1.0, name="y")
-            ts(bt, q, 1, None, OP.bitwise_and, name="bit")
-            ts(s, bt, -2040.0, 2048.0, OP.mult, OP.add, name="s")
+            mm([(pe, R("EL", 128 * k, 128 * k + 128), R("G", g0 + k, 16 * i1, 16), k == 0, k == 14) for k in range(15)], "E")
+            q, y = R("QI", i0, i1), R("Y", i0, i1)
+            affine(q, pe, 1.0, -0.4375, "q")
+            tt(y, pe, q, OP.subtract, name="y")
+            for a0, a1 in cuts(PLAN["sc"]):
+                if a1 == i1:
+                    ts(R("BT", a0, a1), R("QI", a0, a1), 1, None, OP.bitwise_and, name="bit")
+                    affine(R("S", a0, a1), R("BT", a0, a1), -2040.0, 2048.0, "s")
+        for c, (i0, i1) in enumerate(cuts(PLAN["ch"])):
+            n, g0, ck[0] = i1 - i0, 16 * i0, c
+            a0, a1 = [p for p in cuts(PLAN["pc"]) if p[0] <= i0 < p[1]][0]
+            o0 = i0 - a0
             pt = []
             for hs in ([(0,), (1,)] if n > 64 else [(0, 1)]):
                 u = ub[un % 3]
@@ -258,82 +274,93 @@ def build_ops(nsig):
                     ps.append((R(u, 0, 512, 1, p0, p0 + n), R("Y", i0, i1, 1, 64 * h, 64 * h + 64), R("PW", 0, 512, 1, 64 * h, 64 * h + 64),
                                False, True))
                     if len(hs) == 2:
-                        pt.append((R("pT", 0, n, 1, p0, p0 + 64), R("SO", so + 7, so + 512, 8, p0, p0 + n), R("IDF", p0, p0 + n, 1, p0, p0 + n), True, True))
+                        pt.append((R("pT", o0, o0 + n, 1, p0, p0 + 64), R("SO", so + 7, so + 512, 8, p0, p0 + n), R("IDF", p0, p0 + n, 1, p0, p0 + n), True, True))
                 mm(xs, "X")
                 mm(ps, "pen")
                 o, ui = R("SO", so, so + 512), R(u, 0, 512)
                 add("v", lambda g, T, X, o=o, ui=ui: g.vector.tensor_tensor_scan(ap(T, o), T.DZ[:, :], ap(T, ui), 0.0, OP.add, OP.max),
                     [ui, whole("DZ")], [o], ("plain", 512), name="scan")
                 so += 512
-            mm(pt or [(R("pT", 0, n), R("SO", so - 1017, so, 8), whole("IDF"), True, True)], "back", True)
+            mm(pt or [(R("pT", o0, o0 + n), R("SO", so - 1017, so, 8), whole("IDF"), True, True)], "back", True)
+            if i1 < a1:
+                continue
+            i0, n, c = a0, a1 - a0, cuts(PLAN["pc"]).index((a0, a1))
+            ck[0] = c
             ti, a8, vk = (R(b, i0, i1) for b in ("TI", "A8", "VK"))
-            tt(ti, R("pT", 0, n), s, OP.mult, 1.0, name="tt")
+            tt(ti, R("pT", 0, n), R("S", i0, i1), OP.mult, name="tt")
             ts(a8, ti, 8, 255, OP.logical_shift_right, OP.bitwise_and, name="and")
-            cp(vk, a8, name="cvt")
-            mm([(R("pD", 0, n), whole("DF"), vk, True, True), (R("pD", 128, 128 + n), whole("PM"), vk, True, True)], "d")
+            move(vk, a8, "cvt")
+            mm([(R("pD", 0, n), whole("DF"), vk, True, True)], "d")
+            mm([(R("pD", 256, 256 + n), whole("PM"), vk, True, True)], "vn")
             act(R("AB", i0, i1), R("pD", 0, n), AF.Abs, name="abs")
-            act(R("SG", i0, i1), R("AB", i0, i1), AF.Sign, bias=col("CC", 7), accum=col("SUMS", c + 1), name="sign")
-            act(R(V, i0, i1), R("pD", 128, 128 + n), AF.Copy, name="vcopy")
+            act(R("SG", i0, i1), R("AB", i0, i1), AF.Sign, bias=col("CC", 0), accum=col("SUMS", c), name="sign")
+            move(R(V, i0, i1), R("pD", 256, 256 + n), "vcopy")
             if i0 < HB <= i1:
+                ck[0] = 7
                 send("V", R(V, 0, HB), R("rv%d" % t, 0, HB))
-                sums(R("pW", 0, 14), None, 0, 14, "h")
-                sums(None, R("pW", 32, 46), 0, 14, "n")
+                sums(R("pW", 0, 14), R("pW", 32, 46), 0, 14)
         ck[0] = 9
-        sa, su, sl = col("SA"), R("SUMS", 0, nc), col("SUMS", nc)
-        add("v", lambda g, T, X, sa=sa, su=su: g.vector.tensor_reduce(ap(T, sa), ap(T, su), AxisListType.X, OP.add), [su], [sa], ("plain", 4), name="SA")
-        mm([(col("pW", 64), whole("OB"), sa, True, False), (col("pW", 64), whole("OB"), sl, False, True)], "A", True)
-        places(R("pW", 0, 14), 0, 14)
+        pa, nc = col("pW", 64), len(PLAN["pc"])
+        mm([(pa, whole("OB"), col("SUMS", c), c == 0, False) for c in range(nc - 1)], "Aa", True)
+        mm([(pa, whole("OB"), col("SUMS", nc - 1), False, True)], "A", True)
+        ts(R("t1", 48, 62), R("pW", 0, 14), pa, 512.0, OP.add, OP.mult, name="t1")
+        ts(R("t2", 48, 62), R("t1", 48, 62), W - 1, None, OP.bitwise_and, name="t2")
+        tt(R("t3", 48, 62), R("t2", 48, 62), R("rej", 0, 14), OP.add, name="t3")
+        move(R(LS, 0, 14), R("t3", 48, 62), "list")
         send("L", R(LS, 0, 14), R("rl%d" % t, 0, 14))
         ck[0] = 8
-        sums(R("pE1", 0, 14), None, 14, 28, "h")
-        sums(None, R("pT", 0, 14), 14, 28, "n")
-        places(R("pE1", 0, 14), 14, 28)
+        sums(R("pE1", 0, 14), R("pT", 0, 14), 14, 28)
         wrap(R("pE0", 0, 28), "F37", "VK", 0, 28, "h37")
-        ts(R("n5", 0, 28), R("pE0", 0, 28), col("pW", 64), None, OP.add, name="n5")
-        ts(R("n6", 0, 28), R("n5", 0, 28), W - 1, None, OP.bitwise_and, name="n6")
+        ts(R("t1", 0, 28), R("pE0", 0, 28), pa, 8.0 * L, OP.add, OP.add, name="k1")
+        ts(R("t1", 28, 42), R("pE1", 0, 14), pa, 512.0, OP.add, OP.mult, name="e1")
+        ts(R("t2", 0, 42), R("t1", 0, 42), W - 1, None, OP.bitwise_and, name="k2")
         tt(R("dl", 0, 28), R("rej", 0, 28), R("MC", 0, 28), OP.mult, name="dl")
-        tt(R("n7", 0, 28), R("n6", 0, 28), R("dl", 0, 28), OP.max, name="n7")
-        cp(R("NL", 0, 28), R("n7", 0, 28), name="NL")
-        for c, (i0, n) in enumerate(PLAN["bc"]):
-            i1, g0, ck[0], pb = i0 + n, 16 * i0, c, R(("pU1", "pU2", "pU0", "pD")[c], 0, n)
-            for j in range(i0, i1, PLAN["bp"]):
-                e = min(j + PLAN["bp"], i1)
-                gat("vs", R("GB", 16 * j, 16 * e), bw, R(C, j, e), "BG")
-            bl = ([(pb, whole("NI16"), R(CF, i0, i1), True, False)]
-                  + [(pb, R("S16", 128 * k - 128, 128 * k), R("GB", g0 + k, 16 * i1, 16), False, k == 15) for k in range(1, 16)])
+        tt(R("t3", 0, 28), R("t2", 0, 28), R("dl", 0, 28), OP.max, name="k3")
+        tt(R("t3", 28, 42), R("t2", 28, 42), R("rej", 14, 28), OP.add, name="e3")
+        move(R("NL", 0, 42), R("t3", 0, 42), "NL")
+        for c, (j, e) in enumerate(cuts(PLAN["bg"])):
+            ck[0] = c
+            gat(R("GB", 16 * j, 16 * e), R(Bo, 0, W), R(C, j, e), "BG")
+            if j >= PLAN["deferg"]:
+                ops[-1].update(dict(rd=t + 1) if t < NT - 1 else dict(name="zBG"))
+        for c, (i0, i1) in enumerate(cuts(PLAN["bc"])):
+            n, g0, ck[0], first = i1 - i0, 16 * i0, c, len(ops)
+            pb = R(PLAN["bb"][c], 0, n)
+            bl = ([(pb, whole("NI"), R(CF, i0, i1), True, False)]
+                  + [(pb, R("SL", 128 * k - 128, 128 * k), R("GB", g0 + k, 16 * i1, 16), False, k == 15) for k in range(1, 16)])
             for j in range(0, 16, 4):
                 mm(bl[j:j + 4], "BX")
-            cr, sg, pm = R("CR", i0, i1), R("SG", i0, i1), R(pb[0], 256, 256 + n)
-            add("vs", {"v": lambda g, T, X, cr=cr, sg=sg: g.vector.tensor_scalar(ap(T, cr), ap(T, sg), 0.0, None, OP.max),
-                       "s": lambda g, T, X, cr=cr, sg=sg: g.scalar.activation(ap(T, cr), ap(T, sg), AF.Relu)},
-                [sg], [cr], ("plain", n * 0.75), name="cr")
-            tt(R("M2", i0, i1), pb, cr, OP.mult, 1.0, name="m2")
-            mm([(pm, whole("ID16"), R(CF, i0, i1), True, False), (pm, whole("ID16"), R("M2", i0, i1), False, True)], "mend")
-            move(R("B", MEND + i0, MEND + i1), pm, "mendc")
+            sg, pm = R("SG", i0, i1), R(pb[0], 256, 256 + n)
+            tt(R("M2", i0, i1), pb, sg, OP.min, name="m2")
+            mm([(pm, whole("ID"), R(CF, i0, i1), True, False), (pm, whole("IA"), sg, False, False),
+                (pm, whole("IB4"), R("M2", i0, i1), False, True)], "mend")
+            affine(R(Bn, MEND + i0, MEND + i1), pm, 1.0, 2048.0, "mendc")
+            if i0 >= PLAN["defer"]:
+                for o in ops[first:]:
+                    o.update(dict(rd=t + 1) if t < NT - 1 else dict(name="z" + o["name"]))
         ck[0] = 9
-        xs, bs = R("X", 0, XW), R("B", 0, MEND)
-        ls, rl = R(LS, 14, 28), R("rl%d" % t, 0, 14)
+        xs, bs = R("X", 0, XW), R(Bn, 0, MEND)
+        ls, rl = R("NL", 28, 42), R("rl%d" % t, 0, 14)
         sca(xs, ls, R(V, HB, L), "XS even")
         sca(bs, ls, R(C, HB, L), "BS even")
-        last = t == NT - 1
-        rest = [(xs, R("rv%d" % t, 0, HB), "XS odd"), (bs, R("rc%d" % t, 0, HB), "BS odd")]
-        for w, s, nm in (rest if last else rest[::-1]):
-            sca(w, rl, s, nm)
-        bn = whole("B")
-        if last:
+        sca(xs, rl, R("rv%d" % t, 0, HB), "XS odd")
+        sca(bs, rl, R("rc%d" % t, 0, HB), "BS odd")
+        if t == NT - 1:
             add("y", lambda g, T, X: g.sync.dma_start(T.yx[:, :], T.X[:, 0:W]), [R("X", 0, W)], [], ("fixed", 4.0), ("oyx", 16), "st x")
-            gat("v", R("YC", 1, L, 2), bn, R("NL", 0, 14), "nxt")
-            gat("s", R("YC", 0, L, 2), bn, R("NL", 14, 28), "nxt")
+            gat(R("YC", 1, L, 2), R(Bn, 0, MEND + HB), R("NL", 0, 14), "out")
+            gat(R("YC", 0, L, 2), whole(Bn), R("NL", 14, 28), "out")
             add("y", lambda g, T, X: g.sync.dma_start(T.yc[:, :], T.YC[:, :]), [R("YC", 0, L)], [], ("fixed", 2.5), ("oyc", 16), "st c")
         else:
-            D, DF_ = "C%d" % ((t + 1) % 2), "CF%d" % ((t + 1) % 2)
-            for i0, i1 in PLAN["nx"]:
-                gat("v", R(D, i0, i1), R("B", 0, MEND + i1), R("NL", i0 // 16, i1 // 16), "nxt")
-            cp(whole(DF_), whole(D), 0.5, name="cf")
+            D = "C%d" % ((t + 1) % 2)
+            for i0, i1 in cuts(PLAN["nx"]):
+                ck[:] = [i0 // 64, t + (i0 >= PLAN["defer"])]
+                gat(R(D, i0, i1), R(Bn, 0, MEND + i1), R("NL", i0 // 16, i1 // 16), "nxt")
     return ops
 
 
 def hit(a, b):
+    if a[3] == b[3] > 1 and (a[1] - b[1]) % a[3]:
+        return False
     return a[0] == b[0] and a[1] < b[2] and b[1] < a[2] and a[4] < b[5] and b[4] < a[5]
 
 
@@ -365,70 +392,59 @@ def depend(ops):
     return deps
 
 
-def force(ops):
-    f, k = {}, {z: 0 for z in PLAN["eng"]}
-    tot = {z: max(1, sum(o["name"] == z for o in ops) // NT) for z in k}
-    for i, o in enumerate(ops):
-        z = o["name"]
-        if z in k:
-            p = PLAN["eng"][z]
-            f[i] = p[(k[z] % tot[z]) % len(p)]
-            k[z] += 1
-    return {i: ("vs" if v == "x" else v) for i, v in f.items()}
+def tags_of(ops):
+    seen, out = {}, []
+    for o in ops:
+        z = o["name"].replace(" ", "") + (str(o["ck"]) if o["ck"] < 8 else "")
+        k = seen.get((z, o["rd"]), 0)
+        seen[(z, o["rd"])] = k + 1
+        out.append(z + ("bcdefghijklmnopqrstuvwxyz"[k - 1] if k and o["rd"] >= 0 else ""))
+    return out
 
 
 def schedule(ops, deps):
     n = len(ops)
-    fc, adj, dl, wf = force(ops), PLAN["adj"], PLAN["delta"], PLAN["wf"]
     succ = [[] for _ in range(n)]
     for i in range(n):
         for j in deps[i]:
             succ[j].append(i)
-    pri = [0.0] * n
+    path = [0.0] * n
     for i in range(n - 1, -1, -1):
-        pri[i] = ops[i]["cost"] + max([pri[s] + LAT for s in succ[i]] or [0.0])
-    pa = [pri[i] + adj.get(ops[i]["name"], 0.0) + adj.get("%s@%d" % (ops[i]["name"], ops[i]["ck"]), 0.0) for i in range(n)]
-    left = [len(d) for d in deps]
-    ready = {i: 0.0 for i in range(n) if left[i] == 0}
-    free = {"v": 0.0, "s": 0.0, "t": 0.0, "g": 0.0, "y": 0.0}
-    fin, order = [0.0] * n, []
-    while ready:
-        best, heads = None, {}
-        for i, r in ready.items():
-            e = ops[i]["eng"]
-            if e == "x":
-                best = (r, "x", i)
-                break
-            if e == "vs":
-                e = fc.get(i, "vs")
-            for q in ("v", "s") if e == "vs" else (("s",) if e == "sd" else (e,)):
-                heads.setdefault(q, []).append((max(free[q], r), i))
-        if best is None:
-            for q, c in heads.items():
-                t0 = min(c)[0]
-                if best is not None and t0 >= best[0]:
-                    continue
-                a = max((pa[i], -i) for st, i in c if st <= t0 + dl)
-                lim = t0 + max(dl, wf * ops[-a[1]]["cost"])
-                a = max((pa[i], -i, st) for st, i in c if st <= lim)
-                if best is None or a[2] < best[0]:
-                    best = (a[2], q, -a[1])
-        st, q, i = best
-        del ready[i]
+        el = ops[i]["el"]
+        path[i] = max([path[s] + LAT for s in succ[i]] or [0.0]) + cost_of(el["s"] if isinstance(el, dict) else el)
+    tags, named = tags_of(ops), {z for v in ORDER.values() for z in v.split()}
+    first = [i for i in range(n) if tags[i] not in named and ops[i]["eng"] != "x"]
+    busy = {q: [] for q in ORDER}
+    fin = {}
+    while len(fin) < len(first):
+        i = min((x for x in first if x not in fin and all(j in fin for j in deps[x])), key=lambda x: (-path[x], x))
         o = ops[i]
-        if q == "x":
-            fin[i] = st + o["cost"]
-        elif o["eng"] in ("y", "sd"):
-            free[q] = st + 0.1
-            fin[i] = st + o["cost"]
-        else:
-            free[q] = fin[i] = st + o["cost"]
-        order.append((i, q))
-        for s in succ[i]:
-            left[s] -= 1
-            if left[s] == 0:
-                ready[s] = max(fin[j] + (LAT if w else 0.0) for j, w in deps[s].items())
-    return order, max(fin)
+        t0 = max([fin[j] + (LAT if w else 0.0) for j, w in deps[i].items()] or [0.0])
+        best = None
+        for q in {"sd": "s"}.get(o["eng"], o["eng"]):
+            c = cost_of(o["el"][q] if isinstance(o["el"], dict) else o["el"])
+            hold = 0.1 if o["eng"] in ("y", "sd") else c
+            a, at = t0, 0
+            for at, (b0, b1, _j) in enumerate(busy[q] + [(math.inf, math.inf, 0)]):
+                if a + hold <= b0 + 1e-9:
+                    break
+                a = max(a, b1)
+            if best is None or a + c < best[0]:
+                best = (a + c, q, at, a, hold)
+        fin[i] = best[0]
+        busy[best[1]].insert(best[2], (best[3], best[3] + best[4], i))
+    seq = {q: [b[2] for b in busy[q]] + [i for t in range(NT) for z in ORDER[q].split() for i in range(n)
+                                          if tags[i] == z and max(ops[i]["rd"], 0) == t] for q in ORDER}
+    seq.update({i: [i] for i in range(n) if ops[i]["eng"] == "x"})
+    done, order = set(), []
+    while len(order) < n:
+        before = len(order)
+        for q, v in seq.items():
+            while v and all(j in done for j in deps[v[0]]):
+                done.add(v[0])
+                order.append((v.pop(0), q if q in ORDER else "x"))
+        assert len(order) > before
+    return order, 0.0
 
 
 _plan = {}

@@ -1,14 +1,21 @@
-import math
-from concourse.mybir import AluOpType as OP, AxisListType, ActivationFunctionType as AF
+from concourse.mybir import AluOpType as OP, ActivationFunctionType as AF
 
 N, NT = 4, 4
 L, HB, W = 448, 224, 2048
 MEND = 4096
 BW, XW = MEND + L, 4096
-PLAN = {'ch': [128, 128, 128, 64], 'xg': [32, 32] + [64] * 6, 'bg': [64, 64, 64, 64, 64, 48, 48, 32], 'bc': [128, 128, 192], 'nx': [128, 128, 192],
-        'pc': [256, 128, 64], 'sc': [256, 192], 'pool': ["cvt", "cf"], 'defer': 256, 'deferg': 448, 'ec': [64, 64, 128, 128, 64],
-        'bb': ["pU1", "pU2", "pD"]}
-ORDER = {'v': 'cb XG1 m22 XG4 unpk mendc2 q0 nxt4 q1 y0 y1 XG6 q2 y2 scan0 bit2 scan0b scan1 scan1b q3 y4 bit4 tt0 y3 and0 ce cvt0 scan2 scan2b scan3 tt1 vcopy0 and1 tt2 cvt1 and2 cvt2 cg rej7 BG3 t1 vcopy2 t2 e1 t3 k1 list k2 rej dl e3 k3 BG7 BSeven m20 m21 XSeven BSodd XSodd zm22 outb', 's': 'ca XG0 XG2 cc XG3 XG7 XG5 cd unph q4 s2 BG5 BG0 abs0 s4 sign0 BG1 abs1 vcopy1 sign1 abs2 sign2 BG2 NL BG4 BG6 mendc0 mendc1 nxt0 nxt2 out zmendc2', 't': 'BX2 BX2b BX2c BX2d E0 mend2 E1 X0 w X0b E2 pen0 X1 pen0b E4 pen1 X1b pen1b E3 back0 back1 X2 X3 pen2 X2b pen2b d0 vn0 pen3 back2 h47 back3 n7 d1 vn1 h4 d2 vn2 Aa A h37 n BX0 BX0b BX0c BX1 BX1b BX0d BX1c BX1d mend1 mend0 zBX2 zBX2b zBX2c zBX2d zmend2', 'g': 'cf late sendC SL sendV7 sendL', 'y': 'cpB stx stc'}
+PLAN = {"xg": [64, 64, 56, 72, 64, 64, 64], "bg": [64, 64, 56, 72, 72, 72, 48], "ec": [128, 128, 128, 64], "qc": [128, 128, 128, 64],
+        "sc": [256, 192], "ch": [128, 128, 128, 64], "pc": [256, 192], "bc": [128, 128, 192], "bb": ["pU1", "pU2", "pD"],
+        "nx": [128, 128, 192], "defer": 256, "pool": ["cvt", "cf"]}
+ORDER = {
+    "v": "ms ki PWa kf mo mz ce cb cv cg md m22 XG0 mendc2 XG3 unpk q0 cc y0 BG6 q1 y1 scan0 scan0b scan1 scan1b bit1 cd s1 q2 tt0 y2 q3 "
+         "and0 y3 scan2 scan2b bit3 scan3 s3 vcopy0 tt1 and1 cvt1 rej7 BG3 t1 t2 t3 rej vcopy1 e3 dl k1 XSeven k2 m20 BSeven m21 k3 "
+         "zXSodd zm22 zBSodd BSodd XSodd outb",
+    "s": "ldx ca co PWb XG1 XG2 unph nxt4 XG5 XG4 XG6 BG0 BG1 abs0 sign0 BG2 abs1 sign1 BG4 BG5 mendc1 mendc0 zmendc2 nxt0 out nxt2",
+    "t": "BX2 BX2b BX2c BX2d mend2 X0 E0 X0b E1 pen0 X1 pen0b w pen1 X1b pen1b back0 E2 back1 X2 E3 X2b pen2 pen2b X3 pen3 d0 vn0 "
+         "back2 back3 BX0 n7 BX0b d1 vn1 h4 Aa A n h37 BX0c BX1 BX0d BX1b BX1c BX1d mend0 zBX2 zBX2b zBX2c zBX2d mend1 zmend2",
+    "g": "ii ib i64 gc dz col id xp el eb cf pm idf SL sendC cvt0 late sendV7 sendL",
+    "y": "ldwt ldcb ldpk cpB stx stc"}
 
 F32, B16, I32, U16, H16 = "float32", "bfloat16", "int32", "uint16", "float16"
 SCRATCH = {}
@@ -17,14 +24,14 @@ for _n, _w, _d in (
         ("C0", L, U16), ("C1", L, U16), ("CF0", L, H16), ("CF1", L, H16), ("G", 16 * L, B16), ("GB", 16 * L, H16), ("SO", 4096, F32),
         ("QI", L, I32), ("Y", L, B16), ("BT", L, I32), ("S", L, B16), ("TI", L, I32), ("A8", L, I32), ("VK", L, B16),
         ("V0", L, B16), ("V1", L, B16), ("AB", L, B16), ("SG", L, B16), ("M2", L, H16), ("YC", L, F32),
-        ("SUMS", 8, F32), ("SA", 8, F32), ("SJ", 8, F32), ("rej", 32, F32), ("dl", 32, F32), ("t1", 64, I32), ("t2", 64, I32),
-        ("t3", 64, F32), ("LS0", 16, U16), ("LS1", 16, U16), ("NL", 48, U16),
+        ("SUMS", 8, F32), ("rej", 32, F32), ("dl", 32, F32), ("t1", 64, I32), ("t2", 64, I32),
+        ("LS0", 16, U16), ("LS1", 16, U16), ("NL", 48, U16),
         ("II", 8, I32), ("FF", 8, F32), ("CC", 16, F32), ("WI", 8, I32), ("W2", 8, H16), ("COL", 144, F32), ("GC", 128, F32),
-        ("DZ", 512, F32), ("IB0", 32, F32), ("IB", 32, H16), ("MC0", 32, F32), ("MC", 32, F32), ("RM", 16, F32),
-        ("ONE", 128, B16), ("ONF", 128, F32), ("EIG", 144, B16), ("EB", 144, B16), ("EL", 15 * 128, B16), ("XP0", 64, B16),
+        ("DZ", 512, F32), ("IB0", 32, F32), ("IB", 32, H16), ("MC0", 32, F32), ("MC", 32, F32),
+        ("ONE", 128, B16), ("ONF", 128, F32), ("EIG", 144, B16), ("EB", 144, B16), ("EL", 512, B16), ("E0", 128, B16), ("XP0", 64, B16),
         ("XP", 64, B16), ("I640", 64, B16), ("I64", 64, B16), ("PW", 512, B16), ("IDF", 128, F32), ("PM", 128, B16), ("DF", 128, B16),
-        ("F", 144, B16), ("FK", 144, B16), ("F4", 144, B16), ("F37", 144, H16), ("OB", 128, F32), ("ID", 128, B16), ("NI", 128, B16),
-        ("SL", 15 * 128, B16), ("IA", 128, B16), ("IB4", 128, B16), ("PD", 128, B16)):
+        ("FK", 144, B16), ("F4", 144, B16), ("F37", 144, H16), ("OB", 128, F32), ("ID", 128, B16), ("NI", 128, B16),
+        ("SL", 512, B16), ("IA", 128, B16), ("IB4", 128, B16), ("TIN", 128, B16)):
     SCRATCH[_n] = ("sbuf", [128, _w], _d)
 for _t in range(NT):
     SCRATCH["rc%d" % _t] = ("sbuf", [128, HB], U16)
@@ -34,8 +41,6 @@ for _n in ("pE0", "pE1", "pU0", "pU1", "pU2", "pT", "pD", "pW"):
     SCRATCH[_n] = ("psum", [128, 512], F32)
 SEMAPHORES = (["qv", "qs", "qt", "qg", "dcb", "dx", "dpk", "dwt", "oyx", "oyc"] + ["dcp%d" % t for t in range(NT)]
               + [a + b + str(t) for a in "rl" for b in "CVL" for t in range(NT)])
-
-CY, TCY, GAM, SCA, LAT = 0.00083 * 1.1, 0.00042 * 1.1, 1.45, 3.5, 0.1
 
 
 def R(buf, c0, c1, step=1, p0=0, p1=128):
@@ -59,12 +64,6 @@ def cuts(sizes):
         out.append((a, a + n))
         a += n
     return out
-
-
-def cost_of(el):
-    kind, n = el
-    return {"plain": 0.06 + max(64, n) * CY, "gat": 0.06 + n * GAM * CY, "sca": 0.06 + n * SCA * CY, "pe": 0.03 + n * TCY,
-            "pool": 0.15 + 2 * n * CY, "fixed": n}[kind]
 
 
 def build_ops(nsig):
@@ -95,8 +94,8 @@ def build_ops(nsig):
         cyc = 1.0 if SCRATCH[a[0]][0] == "psum" else 2.0
         add("v", lambda g, T, X: g.vector.tensor_tensor(ap(T, out), ap(T, a), ap(T, b), op), [a, b], [out], ("plain", ne(out) * cyc), name=name)
 
-    def ms(out, x):
-        add("v", lambda g, T, X: g.vector.memset(ap(T, out), x), [], [out], ("plain", ne(out) * half(out)), name="memset")
+    def ms(out, x, name):
+        add("v", lambda g, T, X: g.vector.memset(ap(T, out), x), [], [out], ("plain", ne(out) * half(out)), name=name)
 
     def act(out, in_, func, bias=0.0, accum=None, name="act"):
         def fn(g, T, X):
@@ -129,21 +128,21 @@ def build_ops(nsig):
     def sca(win, off, in_, name):
         add("v", lambda g, T, X: g.vector.tensor_copy(ap(T, win).indirect(ap(T, off)), ap(T, in_)), [in_, off], [win], ("sca", ne(in_)), name=name)
 
-    def mm(lst, name, f32=False):
+    def mm(lst, name):
         def fn(g, T, X):
             i = None
             for o, l, r, a, b in lst:
                 i = g.tensor.matmul(ap(T, o), ap(T, l), ap(T, r), a, b)
             return i
-        cyc = sum(max(min(64, ne(l)), ne(r)) for _o, l, r, _a, _b in lst) * (4 if f32 else 1)
+        cyc = sum(max(min(64, ne(l)), ne(r)) * (4 if SCRATCH[l[0]][2] == F32 else 1) for _o, l, r, _a, _b in lst)
         add("t", fn, [x for m in lst for x in (m[1], m[2])], [m[0] for m in lst], ("pe", cyc), name=name)
 
-    def iota(out, pat, base, cm, f32=True):
+    def iota(out, pat, base, cm, name, f32=True):
         def fn(g, T, X):
             if f32:
                 return g.iota(ap(T, out), pat, base, cm, allow_small_or_imprecise_dtypes=True)
             return g.iota(ap(T, out), pat, base, cm)
-        add("g", fn, [], [out], ("pool", ne(out)), name="iota")
+        add("g", fn, [], [out], ("pool", ne(out)), name=name)
 
     def where(out, in_, pat, base, fill=None, cm=1, name="where"):
         op = OP.is_equal if fill is None else OP.not_equal
@@ -159,39 +158,40 @@ def build_ops(nsig):
     add("sd", lambda g, T, X: g.scalar.dma_start(T.X[:, 0:W], T.x[:, :]), [], [R("X", 0, W)], ("fixed", 4.5), ("dx", 16), "ld x")
     add("y", lambda g, T, X: g.sync.dma_start(T.wti[:, 0:1], T.wt[:, :]), [], [col("wti")], ("fixed", 2.0), ("dwt", 16), "ld wt")
     add("y", lambda g, T, X: g.sync.dma_start(T.pki[:, :], T.pk[:, :]), [], [R("pki", 0, 1024)], ("fixed", 5.0), ("dpk", 16), "ld pk")
-    ms(whole("EIG"), 0.125)
-    ms(whole("ONE"), 1.0)
-    ms(whole("ONF"), 1.0)
-    iota(col("II", 0), [[1, 1]], 0, 1, False)
-    iota(whole("COL"), [[1, 144]], 0, 0)
-    where(R("EB", 0, 136), R("EIG", 0, 136), [[-1, 17], [-16, 8]], 1)
-    where(whole("XP0"), R("EIG", 0, 64), [[-16, 8], [-1, 8]], 0)
-    where(whole("XP"), whole("XP0"), [[-16, 8], [-1, 8]], -8, 32.0)
-    where(whole("I640"), R("ONE", 0, 64), [[-1, 64]], 0)
-    where(whole("I64"), whole("I640"), [[-1, 64]], -64, 1.0)
-    where(whole("IDF"), whole("ONF"), [[-1, 128]], 0)
-    where(whole("PM"), whole("ONE"), [[-1, 8], [-8, 16]], 0)
-    where(whole("DF"), whole("PM"), [[-1, 8], [-8, 16]], 8, -1.0)
-    where(whole("ID"), whole("ONE"), [[-1, 128]], 0)
-    iota(whole("DZ"), [[0, 64], [16384, 8]], -8192, 0)
-    iota(whole("GC"), [[1, 8], [0, 16]], 0, 0)
-    iota(R("IB0", 0, 28), [[-1, 2], [32, 14]], 1, 0)
-    iota(R("MC0", 0, 28), [[16, 28]], MEND, 0)
-    for j, (s, op) in enumerate(((15, OP.bitwise_and), (4, OP.logical_shift_right), (7, OP.bitwise_and))):
-        ts(col("II", j + 1), col("II", 0), s, None, op)
-    move(R("FF", 0, 3), R("II", 1, 4), "const")
-    kf, gf, k8 = (col("FF", j) for j in range(3))
-    move(R("C0", 0, HB), R("cbi", 1, L, 2), "c16")
-    move(R("C0", HB, L), R("cbi", 0, L, 2), "c16")
-    ts(R("RM", 0, 16), R("COL", 0, 16), kf, None, OP.is_equal)
-    for k in range(15):
-        scaled(R("EL", 128 * k, 128 * k + 128), R("EB", 0, 128), col("RM", k), "EL")
+    ms(whole("EIG"), 0.125, "ms")
+    ms(whole("ONE"), 1.0, "ms")
+    ms(whole("ONF"), 1.0, "mo")
+    iota(col("II", 0), [[1, 1]], 0, 1, "ii", False)
+    iota(whole("COL"), [[1, 144]], 0, 0, "col")
+    where(R("EB", 0, 128), R("EIG", 0, 128), [[-1, 16], [-16, 8]], 0, name="eb")
+    for q in range(4):
+        where(R("EL", 128 * q, 128 * q + 128), R("EIG", 0, 128), [[-129, 4], [128, 4], [-16, 8]], 1 - 4 * q, name="el")
+    where(whole("E0"), R("EIG", 0, 128), [[128, 16], [-16, 8]], 0, name="idf")
+    for c in range(3):
+        ms(R("SO", 1024 * c, 1024 * c + 64), 0.0, "mz")
+    where(whole("XP0"), R("EIG", 0, 64), [[-16, 8], [-1, 8]], 0, name="xp")
+    where(whole("XP"), whole("XP0"), [[-16, 8], [-1, 8]], -8, 32.0, name="xp")
+    where(whole("I640"), R("ONE", 0, 64), [[-1, 64]], 0, name="i64")
+    where(whole("I64"), whole("I640"), [[-1, 64]], -64, 1.0, name="i64")
+    where(whole("IDF"), whole("ONF"), [[-1, 128]], 0, name="idf")
+    where(whole("PM"), whole("ONE"), [[-1, 8], [-8, 16]], 0, name="pm")
+    where(whole("ID"), whole("ONE"), [[-1, 128]], 0, name="id")
+    where(whole("DF"), whole("ID"), [[-1, 128]], 8, -1.0, name="id")
+    iota(whole("DZ"), [[0, 64], [16384, 8]], -8192, 0, "dz")
+    iota(whole("GC"), [[1, 8], [0, 16]], 0, 0, "gc")
+    iota(R("IB0", 0, 28), [[-1, 2], [32, 14]], 1, 0, "ib")
+    iota(R("MC0", 0, 28), [[16, 28]], MEND, 0, "ib")
+    for j, s in enumerate((15, 7)):
+        ts(col("II", j + 1), col("II", 0), s, None, OP.bitwise_and, name="ki")
+    move(R("FF", 0, 2), R("II", 1, 3), "kf")
+    kf, k8 = col("FF", 0), col("FF", 1)
+    move(R("C0", 0, HB), R("cbi", 1, L, 2), "co")
+    move(R("C0", HB, L), R("cbi", 0, L, 2), "cv")
     for j in range(8):
-        scaled(R("PW", j, 512, 8), whole("I64"), float(j * 2 ** 17), "PW")
-    ms(R("DZ", 0, 512, 8), -float(2 ** 24))
-    ms(R("DF", 0, 128, 16), 0.0)
-    ms(col("CC", 0), -80.5)
-    affine(col("CC", 1), gf, 16.0, 15.0, "ca")
+        scaled(R("PW", j, 512, 8), whole("I64"), float(j * 2 ** 17), "PW" + "ab"[j % 2])
+    ms(R("DZ", 0, 512, 8), -float(2 ** 24), "mz")
+    ms(R("DF", 0, 8), 0.0, "md")
+    ms(col("CC", 0), -80.5, "mo")
     affine(col("CC", 2), k8, 16.0, 15.0, "ca")
     affine(col("CC", 3), kf, 2.0, 0.0, "ca")
     affine(col("WI", 2), col("wti"), 37.0, 0.0, "ca")
@@ -199,18 +199,19 @@ def build_ops(nsig):
     ts(col("WI", 1), col("WI", 2), W - 1, None, OP.bitwise_and, name="cb")
     ts(whole("FK"), whole("COL"), col("CC", 2), 8.0, OP.is_equal, OP.mult, name="cb")
     move(R("W2", 0, 2), R("WI", 0, 2), "cc")
-    mm([(R("pW", 0, 2), R("EB", 8, 136), R("W2", 0, 2), True, True)], "w")
+    mm([(R("pW", 0, 2), R("EB", 0, 128), R("W2", 0, 2), True, True)], "w")
     move(R("CC", 4, 6), R("pW", 0, 2), "cd")
     scaled(whole("F4"), whole("FK"), col("CC", 4), "cd")
     scaled(whole("F37"), whole("FK"), col("CC", 5), "cd")
-    ts(whole("F"), whole("COL"), col("CC", 1), None, OP.is_equal, name="ce")
     ts(R("IB", 0, 28), R("IB0", 0, 28), col("CC", 3), 1.0 / 512, OP.add, OP.mult, name="ce")
-    ts(whole("OB"), whole("GC"), gf, 0.5, OP.is_equal, OP.mult, name="cg")
+    ts(whole("OB"), whole("GC"), k8, 0.5, OP.is_equal, OP.mult, name="cg")
     ts(R("MC", 0, 28), R("MC0", 0, 28), kf, 1.0 / 2048, OP.add, OP.mult, name="cg")
-    for b, x in (("PD", 1.0 / 4096), ("NI", -1.0 / 4096), ("IA", -2048.0), ("IB4", 4096.0)):
-        where(whole(b), whole("ID"), [[-1, 128]], 0, x, name="late")
-    for k in range(1, 16):
-        where(R("SL", 128 * k - 128, 128 * k), whole("PD"), [[0, 8], [1, 16]], -k, cm=0, name="SL")
+    ms(whole("TIN"), 1.0 / 4096, "mo")
+    where(whole("NI"), R("EB", 0, 128), [[-1, 16], [-16, 8]], 0, -1.0 / 4096, name="late")
+    for b, x in (("IA", -2048.0), ("IB4", 4096.0)):
+        where(whole(b), whole("PM"), [[-1, 8], [-8, 16]], 0, x, name="late")
+    for q in range(4):
+        where(R("SL", 128 * q, 128 * q + 128), whole("TIN"), [[-129, 4], [128, 4], [-16, 8]], -4 * q, name="SL")
     ts(R("B0", 0, 1024), whole("pki"), W - 1, None, OP.bitwise_and, name="unpk")
     affine(R("B0", 1024, 2048), whole("pki"), 1.0 / W, -0.5 + 0.5 / W, "unph")
 
@@ -233,10 +234,9 @@ def build_ops(nsig):
             mm(list(first) + [(out, R(lh, 15 - b, 143 - b), R(src, 16 * a0 + b, 16 * a1, 16), b == 0 and not first, b == 15)
                               for b in range(16)], name)
 
-        def sums(ph, pn, a0, a1):
-            wrap(ph, "F4", "VK", a0, a1, "h4", [(ph, whole("ID"), R("IB", a0, a1), True, False)])
-            wrap(pn, "F", "SG", a0, a1, "n")
-            ts(R("rej", a0, a1), pn, -5.0, 2048.0, OP.is_gt, OP.mult, name="rej")
+        def rejected(pn, a0, a1):
+            wrap(pn, "FK", "SG", a0, a1, "n")
+            ts(R("rej", a0, a1), pn, -40.0, 2048.0, OP.is_gt, OP.mult, name="rej")
 
         ck[:] = [9, t]
         send("C", R(C, 0, HB), R("rc%d" % t, 0, HB))
@@ -249,9 +249,14 @@ def build_ops(nsig):
             ("fixed", 6.0), ("dcp%d" % t, 16), "cp B")
         for c, (i0, i1) in enumerate(cuts(PLAN["ec"])):
             n, g0, ck[0] = i1 - i0, 16 * i0, c
-            pe = R("pE%d" % (c % 2), 0, n)
-            mm([(pe, R("EL", 128 * k, 128 * k + 128), R("G", g0 + k, 16 * i1, 16), k == 0, k == 14) for k in range(15)], "E")
-            q, y = R("QI", i0, i1), R("Y", i0, i1)
+            c, (a0, a1) = [p for p in enumerate(cuts(PLAN["qc"])) if p[1][0] <= i0 < p[1][1]][0]
+            pe = R("pE%d" % (c % 2), 0, a1 - a0)
+            mm([(R(pe[0], i0 - a0, i1 - a0, 1, k // 4 * 32, k // 4 * 32 + 32), R("EL", 32 * k, 32 * k + 32), R("G", g0 + k - 1, 16 * i1, 16),
+                 k == 1 or k % 4 == 0, k % 4 == 3) for k in range(1, 16)], "E")
+            if i1 < a1:
+                continue
+            ck[0] = c
+            q, y = R("QI", a0, a1), R("Y", a0, a1)
             affine(q, pe, 1.0, -0.4375, "q")
             tt(y, pe, q, OP.subtract, name="y")
             for a0, a1 in cuts(PLAN["sc"]):
@@ -269,19 +274,21 @@ def build_ops(nsig):
                 xs, ps = [], []
                 for h in hs:
                     p0 = 64 * h if len(hs) == 2 else 0
-                    xs += [(R(u, 64 * k, 64 * k + 64, 1, p0, p0 + n), R("G", g0 + 8 * h + k, 16 * i1, 16), whole("XP"), k == 0, False)
-                           for k in range(8)]
-                    ps.append((R(u, 0, 512, 1, p0, p0 + n), R("Y", i0, i1, 1, 64 * h, 64 * h + 64), R("PW", 0, 512, 1, 64 * h, 64 * h + 64),
-                               False, True))
+                    k0 = int(hs == (0,))
+                    xs += [(R(u, 64 * k, 64 * k + 64, 1, p0, p0 + n), R("G", g0 + 8 * h + k, 16 * i1, 16), whole("XP"), k == k0, False)
+                           for k in range(k0, 8)]
+                    ps.append((R(u, 64 * k0, 512, 1, p0, p0 + n), R("Y", i0, i1, 1, 64 * h, 64 * h + 64),
+                               R("PW", 64 * k0, 512, 1, 64 * h, 64 * h + 64), False, True))
                     if len(hs) == 2:
                         pt.append((R("pT", o0, o0 + n, 1, p0, p0 + 64), R("SO", so + 7, so + 512, 8, p0, p0 + n), R("IDF", p0, p0 + n, 1, p0, p0 + n), True, True))
                 mm(xs, "X")
                 mm(ps, "pen")
-                o, ui = R("SO", so, so + 512), R(u, 0, 512)
-                add("v", lambda g, T, X, o=o, ui=ui: g.vector.tensor_tensor_scan(ap(T, o), T.DZ[:, :], ap(T, ui), 0.0, OP.add, OP.max),
-                    [ui, whole("DZ")], [o], ("plain", 512), name="scan")
+                o, ui, dz = R("SO", so + 64 * k0, so + 512), R(u, 64 * k0, 512), R("DZ", 64 * k0, 512)
+                add("v", lambda g, T, X, o=o, ui=ui, dz=dz: g.vector.tensor_tensor_scan(ap(T, o), ap(T, dz), ap(T, ui), 0.0, OP.add, OP.max),
+                    [ui, dz], [o], ("plain", ne(o)), name="scan")
                 so += 512
-            mm(pt or [(R("pT", o0, o0 + n), R("SO", so - 1017, so, 8), whole("IDF"), True, True)], "back", True)
+            mm(pt or [(R("pT", o0, o0 + n), whole("E0"), R("G", g0, 16 * i1, 16), True, False),
+                      (R("pT", o0, o0 + n), R("SO", so - 1017, so, 8), whole("IDF"), False, True)], "back")
             if i1 < a1:
                 continue
             i0, n, c = a0, a1 - a0, cuts(PLAN["pc"]).index((a0, a1))
@@ -298,36 +305,33 @@ def build_ops(nsig):
             if i0 < HB <= i1:
                 ck[0] = 7
                 send("V", R(V, 0, HB), R("rv%d" % t, 0, HB))
-                sums(R("pW", 0, 14), R("pW", 32, 46), 0, 14)
+                rejected(R("pW", 32, 46), 0, 14)
         ck[0] = 9
         pa, nc = col("pW", 64), len(PLAN["pc"])
-        mm([(pa, whole("OB"), col("SUMS", c), c == 0, False) for c in range(nc - 1)], "Aa", True)
-        mm([(pa, whole("OB"), col("SUMS", nc - 1), False, True)], "A", True)
-        ts(R("t1", 48, 62), R("pW", 0, 14), pa, 512.0, OP.add, OP.mult, name="t1")
-        ts(R("t2", 48, 62), R("t1", 48, 62), W - 1, None, OP.bitwise_and, name="t2")
-        tt(R("t3", 48, 62), R("t2", 48, 62), R("rej", 0, 14), OP.add, name="t3")
-        move(R(LS, 0, 14), R("t3", 48, 62), "list")
+        wrap(R("pW", 0, 28), "F4", "VK", 0, 28, "h4", [(R("pW", 0, 28), whole("ID"), R("IB", 0, 28), True, False)])
+        mm([(pa, whole("OB"), col("SUMS", c), c == 0, False) for c in range(nc - 1)], "Aa")
+        mm([(pa, whole("OB"), col("SUMS", nc - 1), False, True)], "A")
+        ts(R("t1", 32, 60), R("pW", 0, 28), pa, 512.0, OP.add, OP.mult, name="t1")
+        ts(R("t2", 32, 60), R("t1", 32, 60), W - 1, None, OP.bitwise_and, name="t2")
+        tt(R(LS, 0, 14), R("t2", 32, 46), R("rej", 0, 14), OP.add, name="t3")
         send("L", R(LS, 0, 14), R("rl%d" % t, 0, 14))
         ck[0] = 8
-        sums(R("pE1", 0, 14), R("pT", 0, 14), 14, 28)
+        rejected(R("pT", 0, 14), 14, 28)
         wrap(R("pE0", 0, 28), "F37", "VK", 0, 28, "h37")
         ts(R("t1", 0, 28), R("pE0", 0, 28), pa, 8.0 * L, OP.add, OP.add, name="k1")
-        ts(R("t1", 28, 42), R("pE1", 0, 14), pa, 512.0, OP.add, OP.mult, name="e1")
-        ts(R("t2", 0, 42), R("t1", 0, 42), W - 1, None, OP.bitwise_and, name="k2")
+        ts(R("t2", 0, 28), R("t1", 0, 28), W - 1, None, OP.bitwise_and, name="k2")
         tt(R("dl", 0, 28), R("rej", 0, 28), R("MC", 0, 28), OP.mult, name="dl")
-        tt(R("t3", 0, 28), R("t2", 0, 28), R("dl", 0, 28), OP.max, name="k3")
-        tt(R("t3", 28, 42), R("t2", 28, 42), R("rej", 14, 28), OP.add, name="e3")
-        move(R("NL", 0, 42), R("t3", 0, 42), "NL")
+        tt(R("NL", 0, 28), R("t2", 0, 28), R("dl", 0, 28), OP.max, name="k3")
+        tt(R("NL", 28, 42), R("t2", 46, 60), R("rej", 14, 28), OP.add, name="e3")
         for c, (j, e) in enumerate(cuts(PLAN["bg"])):
             ck[0] = c
             gat(R("GB", 16 * j, 16 * e), R(Bo, 0, W), R(C, j, e), "BG")
-            if j >= PLAN["deferg"]:
-                ops[-1].update(dict(rd=t + 1) if t < NT - 1 else dict(name="zBG"))
         for c, (i0, i1) in enumerate(cuts(PLAN["bc"])):
             n, g0, ck[0], first = i1 - i0, 16 * i0, c, len(ops)
             pb = R(PLAN["bb"][c], 0, n)
             bl = ([(pb, whole("NI"), R(CF, i0, i1), True, False)]
-                  + [(pb, R("SL", 128 * k - 128, 128 * k), R("GB", g0 + k, 16 * i1, 16), False, k == 15) for k in range(1, 16)])
+                  + [(R(pb[0], 0, n, 1, k // 4 * 32, k // 4 * 32 + 32), R("SL", 32 * k, 32 * k + 32), R("GB", g0 + k, 16 * i1, 16), False, k % 4 == 3)
+                     for k in range(1, 16)])
             for j in range(0, 16, 4):
                 mm(bl[j:j + 4], "BX")
             sg, pm = R("SG", i0, i1), R(pb[0], 256, 256 + n)
@@ -343,8 +347,9 @@ def build_ops(nsig):
         ls, rl = R("NL", 28, 42), R("rl%d" % t, 0, 14)
         sca(xs, ls, R(V, HB, L), "XS even")
         sca(bs, ls, R(C, HB, L), "BS even")
-        sca(xs, rl, R("rv%d" % t, 0, HB), "XS odd")
-        sca(bs, rl, R("rc%d" % t, 0, HB), "BS odd")
+        z = "z" * (t == NT - 1)
+        sca(xs, rl, R("rv%d" % t, 0, HB), z + "XS odd")
+        sca(bs, rl, R("rc%d" % t, 0, HB), z + "BS odd")
         if t == NT - 1:
             add("y", lambda g, T, X: g.sync.dma_start(T.yx[:, :], T.X[:, 0:W]), [R("X", 0, W)], [], ("fixed", 4.0), ("oyx", 16), "st x")
             gat(R("YC", 1, L, 2), R(Bn, 0, MEND + HB), R("NL", 0, 14), "out")
@@ -403,38 +408,9 @@ def tags_of(ops):
 
 
 def schedule(ops, deps):
-    n = len(ops)
-    succ = [[] for _ in range(n)]
-    for i in range(n):
-        for j in deps[i]:
-            succ[j].append(i)
-    path = [0.0] * n
-    for i in range(n - 1, -1, -1):
-        el = ops[i]["el"]
-        path[i] = max([path[s] + LAT for s in succ[i]] or [0.0]) + cost_of(el["s"] if isinstance(el, dict) else el)
-    tags, named = tags_of(ops), {z for v in ORDER.values() for z in v.split()}
-    first = [i for i in range(n) if tags[i] not in named and ops[i]["eng"] != "x"]
-    busy = {q: [] for q in ORDER}
-    fin = {}
-    while len(fin) < len(first):
-        i = min((x for x in first if x not in fin and all(j in fin for j in deps[x])), key=lambda x: (-path[x], x))
-        o = ops[i]
-        t0 = max([fin[j] + (LAT if w else 0.0) for j, w in deps[i].items()] or [0.0])
-        best = None
-        for q in {"sd": "s"}.get(o["eng"], o["eng"]):
-            c = cost_of(o["el"][q] if isinstance(o["el"], dict) else o["el"])
-            hold = 0.1 if o["eng"] in ("y", "sd") else c
-            a, at = t0, 0
-            for at, (b0, b1, _j) in enumerate(busy[q] + [(math.inf, math.inf, 0)]):
-                if a + hold <= b0 + 1e-9:
-                    break
-                a = max(a, b1)
-            if best is None or a + c < best[0]:
-                best = (a + c, q, at, a, hold)
-        fin[i] = best[0]
-        busy[best[1]].insert(best[2], (best[3], best[3] + best[4], i))
-    seq = {q: [b[2] for b in busy[q]] + [i for t in range(NT) for z in ORDER[q].split() for i in range(n)
-                                          if tags[i] == z and max(ops[i]["rd"], 0) == t] for q in ORDER}
+    n, tags = len(ops), tags_of(ops)
+    seq = {q: [i for t in range(NT) for z in ORDER[q].split() for i in range(n) if tags[i] == z and max(ops[i]["rd"], 0) == t]
+           for q in ORDER}
     seq.update({i: [i] for i in range(n) if ops[i]["eng"] == "x"})
     done, order = set(), []
     while len(order) < n:
@@ -444,7 +420,7 @@ def schedule(ops, deps):
                 done.add(v[0])
                 order.append((v.pop(0), q if q in ORDER else "x"))
         assert len(order) > before
-    return order, 0.0
+    return order
 
 
 _plan = {}
@@ -455,7 +431,7 @@ def plan(nsig):
         return _plan[nsig]
     ops = build_ops(nsig)
     deps = depend(ops)
-    order, span = schedule(ops, deps)
+    order = schedule(ops, deps)
     sem = {"v": "qv", "s": "qs", "t": "qt", "g": "qg"}
     cnt, known, tok, snap, out = {}, {q: {} for q in "vstgy"}, {}, {}, []
     for i, q in order:
@@ -483,7 +459,7 @@ def plan(nsig):
         snap[i] = dict(kn)
         snap[i][tok[i][0]] = tok[i][1]
         out.append((q, o, sorted(top.items()), tok[i]))
-    _plan[nsig] = (out, cnt, span)
+    _plan[nsig] = (out, cnt)
     return _plan[nsig]
 
 
@@ -496,7 +472,7 @@ def rank_program(g, core, T, topo):
         d = T.cores[(rank + 1 + t % (N - 1)) % N]
         rid, pid = topo.addr(d, core)
         X.append((rid, pid, topo.mask(core, d)))
-    out, cnt, _span = plan(len(topo.engines(core, T.cores[(rank + 1) % N])))
+    out, cnt = plan(len(topo.engines(core, T.cores[(rank + 1) % N])))
     queue = {"v": g.vector, "s": g.scalar, "t": g.tensor, "g": g, "y": g.sync}
     for q, o, waits, tk in out:
         for s, v in waits:

@@ -4,42 +4,44 @@ N, NT = 4, 4
 L, HB, W = 448, 224, 2048
 MEND = 4096
 BW, XW = MEND + L, 4096
-PLAN = {"xg": [64, 64, 56, 72, 64, 64, 64], "bg": [64, 64, 56, 72, 72, 72, 48], "ec": [128, 128, 128, 64], "qc": [128, 128, 128, 64],
-        "sc": [256, 192], "ch": [128, 128, 128, 64], "pc": [256, 192], "bc": [128, 128, 192], "bb": ["pU1", "pU2", "pD"],
-        "nx": [128, 128, 192], "defer": 256, "pool": ["cvt", "cf"]}
+PLAN = {"xg": [52, 76, 52, 76, 52, 76, 64], "bg": [0, 100, 28, 8, 20, 100, 8, 40, 144], "ch": [128, 128, 128, 64],
+        "sc": [256, 192], "pc": [256, 192], "perm": ["pe", "g"], "bc": [128, 128, 192], "nx": [128, 128, 192], "defer": 256,
+        "pool": ["cvt", "s", "cf", "cBa", "cBb", "cBc", "cBd"], "bb": ["pU2", "pU1", "pU0"], "tb": ["pT"] * 4,
+        "db": ["pD", "pU1", "pD", "pD"], "vb": ["pE0", "pD", "pD", "pD"], "nb": ["pE1", "pT", "pE0"]}
 ORDER = {
-    "v": "ms ki PWa kf mo mz ce cb cv cg md m22 XG0 mendc2 XG3 unpk q0 cc y0 BG6 q1 y1 scan0 scan0b scan1 scan1b bit1 cd s1 q2 tt0 y2 q3 "
-         "and0 y3 scan2 scan2b bit3 scan3 s3 vcopy0 tt1 and1 cvt1 rej7 BG3 t1 t2 t3 rej vcopy1 e3 dl k1 XSeven k2 m20 BSeven m21 k3 "
-         "zXSodd zm22 zBSodd BSodd XSodd outb",
-    "s": "ldx ca co PWb XG1 XG2 unph nxt4 XG5 XG4 XG6 BG0 BG1 abs0 sign0 BG2 abs1 sign1 BG4 BG5 mendc1 mendc0 zmendc2 nxt0 out nxt2",
-    "t": "BX2 BX2b BX2c BX2d mend2 X0 E0 X0b E1 pen0 X1 pen0b w pen1 X1b pen1b back0 E2 back1 X2 E3 X2b pen2 pen2b X3 pen3 d0 vn0 "
-         "back2 back3 BX0 n7 BX0b d1 vn1 h4 Aa A n h37 BX0c BX1 BX0d BX1b BX1c BX1d mend0 zBX2 zBX2b zBX2c zBX2d mend1 zmend2",
-    "g": "ii ib i64 gc dz col id xp el eb cf pm idf SL sendC cvt0 late sendV7 sendL",
+    "v": "ms ki mv ca sa pl cg ce mz SLc m22 md SLb XG1 XG3 y0 XG4 unpk scan0 cb y1 bit1 scan0b scan1b scan1 y2 tt0 bit3 y3 and0 "
+         "scan2 scan2b scan3 tt1 ni and1 cd cvt2 BG5 t1 vcopy1 t2 rej7 BG6 t3 BG7 e1 rej e2 m20 e3 k1 dl k2 XSeven k3 zXSodd XSodd "
+         "m21 zm22 yc ycb",
+    "s": "ldx kf JIb JIa BSl co cv cw SLa XG0 XG2 e0 nxt2 q0 XG5 q1 XG6 unph q2 cc BG2 q3 BG1 BG4 vcopy0 cvt3 BG3 abs0 abs1 sign0 "
+         "sign1 BG8 BSeven BSodd nxt0 nxt1 zBSodd out outb",
+    "t": "BX2 BX2b BX2c BX2d mend2 E0 X0b X0 E1 pen0 pen0b X1 E2 X1b pen1b pen1 E3 Sc0 X2b X2 pen2 pen2b X3 pen3 Sc1 vn0 vn0b BX0 "
+         "BX0b d0 d1 BX0c BX0d vn1 h47 Aa vn1b A n7 n h4 mend0 h37 BX1 BX1b BX1c BX1d mend1 zBX2 zBX2b zBX2c zBX2d zmend2",
+    "g": "ii id col gc ib dz eb i64 xp df cf sendC cfb s1 cBa s3 cvt0 cvt1 cBc sendV7 cBd late cBb sendL",
     "y": "ldwt ldcb ldpk cpB stx stc"}
 
 F32, B16, I32, U16, H16 = "float32", "bfloat16", "int32", "uint16", "float16"
 SCRATCH = {}
 for _n, _w, _d in (
-        ("X", XW, B16), ("B0", BW, I32), ("B1", BW, I32), ("pki", 1024, I32), ("cbi", L, I32), ("wti", 8, I32),
-        ("C0", L, U16), ("C1", L, U16), ("CF0", L, H16), ("CF1", L, H16), ("G", 16 * L, B16), ("GB", 16 * L, H16), ("SO", 4096, F32),
-        ("QI", L, I32), ("Y", L, B16), ("BT", L, I32), ("S", L, B16), ("TI", L, I32), ("A8", L, I32), ("VK", L, B16),
-        ("V0", L, B16), ("V1", L, B16), ("AB", L, B16), ("SG", L, B16), ("M2", L, H16), ("YC", L, F32),
+        ("X", XW, B16), ("BI", W, I32), ("B0", BW, F32), ("B1", BW, F32), ("pki", 1024, I32), ("cbi", L, I32), ("wti", 8, I32),
+        ("C0", L, U16), ("C1", L, U16), ("CF0", L, F32), ("CF1", L, F32), ("G", 16 * L, B16), ("GB", 16 * L, H16), ("SO", 4096, F32),
+        ("QI", L, I32), ("Y", L, B16), ("BT", L, I32), ("S", L, B16), ("TI", L, I32), ("A8", 512, I32), ("VT", 1408, B16),
+        ("V0", L, B16), ("V1", L, B16), ("AB", L, B16), ("SG", L, B16), ("YC", L, F32),
         ("SUMS", 8, F32), ("rej", 32, F32), ("dl", 32, F32), ("t1", 64, I32), ("t2", 64, I32),
-        ("LS0", 16, U16), ("LS1", 16, U16), ("NL", 48, U16),
-        ("II", 8, I32), ("FF", 8, F32), ("CC", 16, F32), ("WI", 8, I32), ("W2", 8, H16), ("COL", 144, F32), ("GC", 128, F32),
+        ("LS0", 16, U16), ("LS1", 16, U16), ("NL", 48, U16), ("PL", 16, U16), ("PF", 16, F32),
+        ("II", 8, I32), ("FF", 8, F32), ("CC", 16, F32), ("WI", 8, I32), ("COL", 144, F32), ("GC", 128, F32),
         ("DZ", 512, F32), ("IB0", 32, F32), ("IB", 32, H16), ("MC0", 32, F32), ("MC", 32, F32),
-        ("ONE", 128, B16), ("ONF", 128, F32), ("EIG", 144, B16), ("EB", 144, B16), ("EL", 512, B16), ("E0", 128, B16), ("XP0", 64, B16),
-        ("XP", 64, B16), ("I640", 64, B16), ("I64", 64, B16), ("PW", 512, B16), ("IDF", 128, F32), ("PM", 128, B16), ("DF", 128, B16),
-        ("FK", 144, B16), ("F4", 144, B16), ("F37", 144, H16), ("OB", 128, F32), ("ID", 128, B16), ("NI", 128, B16),
-        ("SL", 512, B16), ("IA", 128, B16), ("IB4", 128, B16), ("TIN", 128, B16)):
+        ("ONE", 256, B16), ("SA", 128, B16), ("SB", 128, B16), ("DF", 128, B16), ("EIG", 144, B16), ("EB", 144, B16), ("E0", 8, B16),
+        ("XP0", 64, B16), ("XP", 64, B16), ("I640", 64, B16), ("I64", 64, B16), ("N64", 64, B16), ("JI", 1024, B16), ("NI", 128, B16),
+        ("FK", 144, B16), ("F4", 144, B16), ("F37", 144, H16), ("OB", 128, F32), ("ID", 128, B16),
+        ("SL", 2048, B16), ("IA0", 128, B16), ("IA", 128, B16), ("KM", 16, F32)):
     SCRATCH[_n] = ("sbuf", [128, _w], _d)
 for _t in range(NT):
-    SCRATCH["rc%d" % _t] = ("sbuf", [128, HB], U16)
+    SCRATCH["rc%d" % _t] = ("sbuf", [128, HB], F32)
     SCRATCH["rv%d" % _t] = ("sbuf", [128, HB], B16)
     SCRATCH["rl%d" % _t] = ("sbuf", [128, 16], U16)
 for _n in ("pE0", "pE1", "pU0", "pU1", "pU2", "pT", "pD", "pW"):
     SCRATCH[_n] = ("psum", [128, 512], F32)
-SEMAPHORES = (["qv", "qs", "qt", "qg", "dcb", "dx", "dpk", "dwt", "oyx", "oyc"] + ["dcp%d" % t for t in range(NT)]
+SEMAPHORES = (["qv", "qs", "qt", "qg", "dcb", "dx", "dpk", "dwt", "oyx", "oyc"] + ["dcp%d" % t for t in range(1, NT)]
               + [a + b + str(t) for a in "rl" for b in "CVL" for t in range(NT)])
 
 
@@ -67,7 +69,7 @@ def cuts(sizes):
 
 
 def build_ops(nsig):
-    ops, ck = [], [9, -1]
+    ops, ck = [], [-1, -1]
 
     def add(eng, fn, reads, writes, el, tok=None, name="", after=()):
         ops.append(dict(eng=eng, fn=fn, reads=list(reads), writes=list(writes), el=el, tok=tok, name=name, after=list(after), ck=ck[0], rd=ck[1]))
@@ -91,7 +93,7 @@ def build_ops(nsig):
         add("v", fn, [in0] + [s for s in (s1, s2) if isinstance(s, tuple)], [out], ("plain", ne(out) * half(out, in0)), name=name)
 
     def tt(out, a, b, op, name="tt"):
-        cyc = 1.0 if SCRATCH[a[0]][0] == "psum" else 2.0
+        cyc = 1.0 if "psum" in (SCRATCH[a[0]][0], SCRATCH[b[0]][0]) else 2.0
         add("v", lambda g, T, X: g.vector.tensor_tensor(ap(T, out), ap(T, a), ap(T, b), op), [a, b], [out], ("plain", ne(out) * cyc), name=name)
 
     def ms(out, x, name):
@@ -126,7 +128,12 @@ def build_ops(nsig):
              lambda g, T, X: g.scalar.activation(ap(T, out), ap(T, win).indirect(ap(T, off)), AF.Copy), name, "gat")
 
     def sca(win, off, in_, name):
-        add("v", lambda g, T, X: g.vector.tensor_copy(ap(T, win).indirect(ap(T, off)), ap(T, in_)), [in_, off], [win], ("sca", ne(in_)), name=name)
+        fn = {"v": lambda g, T, X: g.vector.tensor_copy(ap(T, win).indirect(ap(T, off)), ap(T, in_)),
+              "s": lambda g, T, X: g.scalar.activation(ap(T, win).indirect(ap(T, off)), ap(T, in_), AF.Silu)}
+        add("vs" if SCRATCH[win[0]][2] == F32 else "v", fn, [in_, off], [win], {q: ("sca", ne(in_)) for q in "vs"}, name=name)
+
+    def nxt(out, win, off, name):
+        add("s", lambda g, T, X: g.scalar.activation(ap(T, out), ap(T, win).indirect(ap(T, off)), AF.Abs), [win, off], [out], ("gat", ne(out)), name=name)
 
     def mm(lst, name):
         def fn(g, T, X):
@@ -160,68 +167,82 @@ def build_ops(nsig):
     add("y", lambda g, T, X: g.sync.dma_start(T.pki[:, :], T.pk[:, :]), [], [R("pki", 0, 1024)], ("fixed", 5.0), ("dpk", 16), "ld pk")
     ms(whole("EIG"), 0.125, "ms")
     ms(whole("ONE"), 1.0, "ms")
-    ms(whole("ONF"), 1.0, "mo")
     iota(col("II", 0), [[1, 1]], 0, 1, "ii", False)
     iota(whole("COL"), [[1, 144]], 0, 0, "col")
-    where(R("EB", 0, 128), R("EIG", 0, 128), [[-1, 16], [-16, 8]], 0, name="eb")
-    for q in range(4):
-        where(R("EL", 128 * q, 128 * q + 128), R("EIG", 0, 128), [[-129, 4], [128, 4], [-16, 8]], 1 - 4 * q, name="el")
-    where(whole("E0"), R("EIG", 0, 128), [[128, 16], [-16, 8]], 0, name="idf")
-    for c in range(3):
-        ms(R("SO", 1024 * c, 1024 * c + 64), 0.0, "mz")
+    where(R("EB", 0, 136), R("EIG", 0, 136), [[-1, 17], [-16, 8]], 1, name="eb")
+    ms(R("EB", 0, 8), 0.0, "md")
+    scaled(whole("E0"), R("EB", 8, 16), 32768.0, "e0")
+    so = 0
+    for n in PLAN["ch"]:
+        if n > 64:
+            ms(R("SO", so, so + 64), 1.0 / 16, "mz")
+        so += 8 * n
+    ms(R("VT", 0, 256 * len(PLAN["ch"])), 0.0, "mv")
     where(whole("XP0"), R("EIG", 0, 64), [[-16, 8], [-1, 8]], 0, name="xp")
     where(whole("XP"), whole("XP0"), [[-16, 8], [-1, 8]], -8, 32.0, name="xp")
     where(whole("I640"), R("ONE", 0, 64), [[-1, 64]], 0, name="i64")
     where(whole("I64"), whole("I640"), [[-1, 64]], -64, 1.0, name="i64")
-    where(whole("IDF"), whole("ONF"), [[-1, 128]], 0, name="idf")
-    where(whole("PM"), whole("ONE"), [[-1, 8], [-8, 16]], 0, name="pm")
-    where(whole("ID"), whole("ONE"), [[-1, 128]], 0, name="id")
-    where(whole("DF"), whole("ID"), [[-1, 128]], 8, -1.0, name="id")
+    where(whole("ID"), R("ONE", 0, 128), [[-1, 128]], 0, name="id")
+    scaled(whole("NI"), whole("ID"), -1.0, "ni")
+    scaled(whole("N64"), whole("I64"), -1.0, "ni")
+    scaled(whole("SA"), whole("ID"), 2048.0, "sa")
+    scaled(whole("SB"), whole("ID"), -2040.0, "sa")
+    where(whole("DF"), whole("ID"), [[-1, 128]], 1, -1.0, name="df")
     iota(whole("DZ"), [[0, 64], [16384, 8]], -8192, 0, "dz")
     iota(whole("GC"), [[1, 8], [0, 16]], 0, 0, "gc")
     iota(R("IB0", 0, 28), [[-1, 2], [32, 14]], 1, 0, "ib")
     iota(R("MC0", 0, 28), [[16, 28]], MEND, 0, "ib")
-    for j, s in enumerate((15, 7)):
-        ts(col("II", j + 1), col("II", 0), s, None, OP.bitwise_and, name="ki")
-    move(R("FF", 0, 2), R("II", 1, 3), "kf")
-    kf, k8 = col("FF", 0), col("FF", 1)
+    ts(col("II", 1), col("II", 0), 15, None, OP.bitwise_and, name="ki")
+    ts(col("II", 2), col("II", 0), 4, None, OP.logical_shift_right, name="ki")
+    move(R("FF", 0, 3), R("II", 0, 3), "kf")
+    pf, kf, gf = (col("FF", j) for j in range(3))
     move(R("C0", 0, HB), R("cbi", 1, L, 2), "co")
     move(R("C0", HB, L), R("cbi", 0, L, 2), "cv")
-    for j in range(8):
-        scaled(R("PW", j, 512, 8), whole("I64"), float(j * 2 ** 17), "PW" + "ab"[j % 2])
+    for j in range(1, 8):
+        scaled(R("JI", 128 * j, 128 * j + 128), whole("ID"), float(j * 2 ** 17), "JI" + "ab"[j % 2])
     ms(R("DZ", 0, 512, 8), -float(2 ** 24), "mz")
-    ms(R("DF", 0, 8), 0.0, "md")
-    ms(col("CC", 0), -80.5, "mo")
-    affine(col("CC", 2), k8, 16.0, 15.0, "ca")
+    ts(col("CC", 6), kf, 0.5, -1024.0, OP.is_lt, OP.mult, name="ca")
+    affine(col("CC", 0), col("CC", 6), 1.0, -80.5, "ca")
+    affine(col("CC", 1), gf, 16.0, 15.0, "ca")
     affine(col("CC", 3), kf, 2.0, 0.0, "ca")
-    affine(col("WI", 2), col("wti"), 37.0, 0.0, "ca")
+    affine(col("CC", 7), col("CC", 6), 2.0, 0.0, "ca")
+    affine(col("CC", 8), kf, 8.0, 0.0, "ca")
+    affine(col("WI", 2), col("wti"), 37.0, 0.0, "cw")
     ts(col("WI", 0), col("wti"), 3, None, OP.bitwise_and, name="cb")
     ts(col("WI", 1), col("WI", 2), W - 1, None, OP.bitwise_and, name="cb")
-    ts(whole("FK"), whole("COL"), col("CC", 2), 8.0, OP.is_equal, OP.mult, name="cb")
-    move(R("W2", 0, 2), R("WI", 0, 2), "cc")
-    mm([(R("pW", 0, 2), R("EB", 0, 128), R("W2", 0, 2), True, True)], "w")
-    move(R("CC", 4, 6), R("pW", 0, 2), "cd")
-    scaled(whole("F4"), whole("FK"), col("CC", 4), "cd")
-    scaled(whole("F37"), whole("FK"), col("CC", 5), "cd")
+    ts(whole("FK"), whole("COL"), col("CC", 1), 8.0, OP.is_equal, OP.mult, name="ce")
+    move(R("CC", 4, 6), R("WI", 0, 2), "cc")
+    ts(whole("F4"), whole("COL"), col("CC", 1), col("CC", 4), OP.is_equal, OP.mult, name="cd")
+    ts(whole("F37"), whole("COL"), col("CC", 1), col("CC", 5), OP.is_equal, OP.mult, name="cd")
     ts(R("IB", 0, 28), R("IB0", 0, 28), col("CC", 3), 1.0 / 512, OP.add, OP.mult, name="ce")
-    ts(whole("OB"), whole("GC"), k8, 0.5, OP.is_equal, OP.mult, name="cg")
+    ts(whole("OB"), whole("GC"), gf, 0.5, OP.is_equal, OP.mult, name="cg")
     ts(R("MC", 0, 28), R("MC0", 0, 28), kf, 1.0 / 2048, OP.add, OP.mult, name="cg")
-    ms(whole("TIN"), 1.0 / 4096, "mo")
-    where(whole("NI"), R("EB", 0, 128), [[-1, 16], [-16, 8]], 0, -1.0 / 4096, name="late")
-    for b, x in (("IA", -2048.0), ("IB4", 4096.0)):
-        where(whole(b), whole("PM"), [[-1, 8], [-8, 16]], 0, x, name="late")
-    for q in range(4):
-        where(R("SL", 128 * q, 128 * q + 128), whole("TIN"), [[-129, 4], [128, 4], [-16, 8]], -4 * q, name="SL")
-    ts(R("B0", 0, 1024), whole("pki"), W - 1, None, OP.bitwise_and, name="unpk")
-    affine(R("B0", 1024, 2048), whole("pki"), 1.0 / W, -0.5 + 0.5 / W, "unph")
+    ts(whole("IA0"), whole("GC"), gf, col("CC", 7), OP.is_equal, OP.mult, name="cg")
+    where(whole("IA"), whole("IA0"), [[-1, 128]], 0, -2048.0, name="late")
+    ms(R("A8", L, L + 8), 0, "mv")
+    ts(R("PF", 0, 8), R("COL", 0, 8), col("CC", 8), None, OP.add, name="pl")
+    ts(col("CC", 9), pf, 63.5, -64.0, OP.is_gt, OP.mult, name="pl")
+    ts(R("PF", 8, 16), R("PF", 0, 8), col("CC", 9), 64.0, OP.add, OP.min, name="pl")
+    ts(R("PF", 0, 8), R("PF", 8, 16), 0.0, 1000.0, OP.is_lt, OP.mult, name="pl")
+    tt(R("PF", 8, 16), R("PF", 8, 16), R("PF", 0, 8), OP.add, name="pl")
+    ts(R("PL", 8, 16), R("PF", 8, 16), 64.0, None, OP.min, name="pl")
+    act(R("PL", 0, 8), R("COL", 0, 8), AF.Silu, bias=col("CC", 8), name="BSl")
+    ts(whole("KM"), R("COL", 0, 16), kf, -1.0, OP.is_equal, OP.mult, name="cg")
+    for k in range(1, 16):
+        scaled(R("SL", 128 * k, 128 * k + 128), whole("ID"), col("KM", k), "SL" + "abc"[k % 3])
+    ts(R("BI", 0, 1024), whole("pki"), W - 1, None, OP.bitwise_and, name="unpk")
+    affine(R("BI", 1024, 2048), whole("pki"), 1.0 / W, -0.5 + 0.5 / W, "unph")
+    for j in range(4):
+        move(R("B1", 512 * j, 512 * j + 512), R("BI", 512 * j, 512 * j + 512), "cB" + "abcd"[j])
 
     xw = R("X", 0, W)
     ub = ["pU0", "pU1", "pU2"]
+    chunks = cuts(PLAN["ch"])
 
     for t in range(NT):
         C, CF, V, LS = "C%d" % (t % 2), "CF%d" % (t % 2), "V%d" % (t % 2), "LS%d" % (t % 2)
-        Bo, Bn = "B%d" % (t % 2), "B%d" % ((t + 1) % 2)
-        un, so = 0, 0
+        Bo, Bn = "B%d" % (t % 2) if t else "BI", "B%d" % ((t + 1) % 2)
+        un = 0
 
         def send(what, src, dst, t=t):
             def fn(g, T, X):
@@ -238,128 +259,148 @@ def build_ops(nsig):
             wrap(pn, "FK", "SG", a0, a1, "n")
             ts(R("rej", a0, a1), pn, -40.0, 2048.0, OP.is_gt, OP.mult, name="rej")
 
-        ck[:] = [9, t]
-        send("C", R(C, 0, HB), R("rc%d" % t, 0, HB))
-        move(whole(CF), whole(C), "cf")
+        def places(a0, a1):
+            wrap(R("pW", a0, a1), "F4", V, a0, a1, "h4", [(R("pW", a0, a1), whole("ID"), R("IB", a0, a1), True, False)])
+
+        ck[:] = [-1, t]
+        move(R(CF, 0, HB), R(C, 0, HB), "cf")
+        move(R(CF, HB, L), R(C, HB, L), "cf")
+        send("C", R(CF, 0, HB), R("rc%d" % t, 0, HB))
         for c, (j, e) in enumerate(cuts(PLAN["xg"])):
             ck[0] = c
-            gat(R("G", 16 * j, 16 * e), xw, R(C, j, e), "XG")
-        ck[0] = 9
-        add("y", lambda g, T, X, a=R(Bn, 0, W), b=R(Bo, 0, W): g.sync.dma_start(ap(T, a), ap(T, b)), [R(Bo, 0, W)], [R(Bn, 0, W)],
-            ("fixed", 6.0), ("dcp%d" % t, 16), "cp B")
-        for c, (i0, i1) in enumerate(cuts(PLAN["ec"])):
-            n, g0, ck[0] = i1 - i0, 16 * i0, c
-            c, (a0, a1) = [p for p in enumerate(cuts(PLAN["qc"])) if p[1][0] <= i0 < p[1][1]][0]
-            pe = R("pE%d" % (c % 2), 0, a1 - a0)
-            mm([(R(pe[0], i0 - a0, i1 - a0, 1, k // 4 * 32, k // 4 * 32 + 32), R("EL", 32 * k, 32 * k + 32), R("G", g0 + k - 1, 16 * i1, 16),
-                 k == 1 or k % 4 == 0, k % 4 == 3) for k in range(1, 16)], "E")
-            if i1 < a1:
-                continue
-            ck[0] = c
-            q, y = R("QI", a0, a1), R("Y", a0, a1)
-            affine(q, pe, 1.0, -0.4375, "q")
-            tt(y, pe, q, OP.subtract, name="y")
+            if e > j:
+                gat(R("G", 16 * j, 16 * e), xw, R(C, j, e), "XG")
+        ck[0] = -1
+        if t:
+            add("y", lambda g, T, X, a=R(Bn, 0, W), b=R(Bo, 0, W): g.sync.dma_start(ap(T, a), ap(T, b)), [R(Bo, 0, W)], [R(Bn, 0, W)],
+                ("fixed", 6.0), ("dcp%d" % t, 16), "cp B")
+        for c, (i0, i1) in enumerate(chunks):
+            n, ck[0], pe = i1 - i0, c, "pE%d" % (c % 2)
+            es = []
+            for k in range(1, 16):
+                p0, c0 = (64 * (k // 8), 8 * (k % 8)) if n == 64 else (0, 8 * k)
+                z = 8 * (k == 1)
+                es.append((R(pe, c0 - z, c0 + 8, 1, p0, p0 + n), R("G", 16 * i0 + k - 1, 16 * i1, 16), R("EB", 8 * k - z, 8 * k + 8), True, True))
+            mm(es, "E")
+            q, y = R("QI", i0, i1), R("Y", i0, i1)
+            affine(q, R(pe, 0, n), 1.0, -0.4375, "q")
+            tt(y, R(pe, 0, n), q, OP.subtract, name="y")
             for a0, a1 in cuts(PLAN["sc"]):
                 if a1 == i1:
                     ts(R("BT", a0, a1), R("QI", a0, a1), 1, None, OP.bitwise_and, name="bit")
-                    affine(R("S", a0, a1), R("BT", a0, a1), -2040.0, 2048.0, "s")
-        for c, (i0, i1) in enumerate(cuts(PLAN["ch"])):
+                    move(R("S", a0, a1), R("BT", a0, a1), "s")
+        for c, (i0, i1) in enumerate(chunks):
             n, g0, ck[0] = i1 - i0, 16 * i0, c
-            a0, a1 = [p for p in cuts(PLAN["pc"]) if p[0] <= i0 < p[1]][0]
-            o0 = i0 - a0
-            pt = []
             for hs in ([(0,), (1,)] if n > 64 else [(0, 1)]):
                 u = ub[un % 3]
                 un += 1
-                xs, ps = [], []
+                k0 = int(hs == (0,))
+                xs = []
                 for h in hs:
                     p0 = 64 * h if len(hs) == 2 else 0
-                    k0 = int(hs == (0,))
                     xs += [(R(u, 64 * k, 64 * k + 64, 1, p0, p0 + n), R("G", g0 + 8 * h + k, 16 * i1, 16), whole("XP"), k == k0, False)
                            for k in range(k0, 8)]
-                    ps.append((R(u, 64 * k0, 512, 1, p0, p0 + n), R("Y", i0, i1, 1, 64 * h, 64 * h + 64),
-                               R("PW", 64 * k0, 512, 1, 64 * h, 64 * h + 64), False, True))
-                    if len(hs) == 2:
-                        pt.append((R("pT", o0, o0 + n, 1, p0, p0 + 64), R("SO", so + 7, so + 512, 8, p0, p0 + n), R("IDF", p0, p0 + n, 1, p0, p0 + n), True, True))
                 mm(xs, "X")
-                mm(ps, "pen")
-                o, ui, dz = R("SO", so + 64 * k0, so + 512), R(u, 64 * k0, 512), R("DZ", 64 * k0, 512)
+                y0 = i0 + 64 * hs[0]
+                mm([(R(u, 64 * k0 + j, 512, 8), R("JI", 128 * j, 128 * j + 128), R("Y", y0 + 8 * k0, y0 + 64), False, j == 7) for j in range(1, 8)], "pen")
+                o, ui, dz = R("SO", 8 * y0 + 64 * k0, 8 * y0 + 512), R(u, 64 * k0, 512), R("DZ", 64 * k0, 512)
                 add("v", lambda g, T, X, o=o, ui=ui, dz=dz: g.vector.tensor_tensor_scan(ap(T, o), ap(T, dz), ap(T, ui), 0.0, OP.add, OP.max),
                     [ui, dz], [o], ("plain", ne(o)), name="scan")
-                so += 512
-            mm(pt or [(R("pT", o0, o0 + n), whole("E0"), R("G", g0, 16 * i1, 16), True, False),
-                      (R("pT", o0, o0 + n), R("SO", so - 1017, so, 8), whole("IDF"), False, True)], "back")
-            if i1 < a1:
+            if i1 not in [e for _j, e in cuts(PLAN["pc"])]:
                 continue
-            i0, n, c = a0, a1 - a0, cuts(PLAN["pc"]).index((a0, a1))
+            c, (a0, a1) = [p for p in enumerate(cuts(PLAN["pc"])) if p[1][1] == i1][0]
+            mine = [(x, j, e) for x, (j, e) in enumerate(chunks) if a0 <= j < a1]
+            n, ck[0], gp = a1 - a0, c, PLAN["perm"][c] == "g"
+            pT, pd, pv = PLAN["tb"][c], PLAN["db"][c], PLAN["vb"][c]
+            sl = [(R(pT, 0, n), whole("SA"), R("ONE", 0, n), True, False), (R(pT, 0, n), whole("SB"), R("S", a0, a1), False, False)]
+            sl += [(R(pT, j - a0, j - a0 + 8), R("G", 16 * j, 16 * e, 16), whole("E0"), False, False) for x, j, e in mine if e - j > 64]
+            sl[-1] = sl[-1][:4] + (True,)
+            mm(sl, "Sc")
+            tt(R("TI", a0, a1), R("SO", 8 * a0 + 7, 8 * a1, 8), R(pT, 0, n), OP.mult, name="tt")
+            ts(R("A8", a0, a1), R("TI", a0, a1), 8, 255, OP.logical_shift_right, OP.bitwise_and, name="and")
+            ds, vs = [], []
+            for x, j, e in mine:
+                ck[0], m, d0 = x, e - j, 128 + 256 * x
+                eye, neg = (whole("ID"), whole("NI")) if m > 64 else (whole("I64"), whole("N64"))
+                if gp:
+                    gat(R("VT", d0, d0 + 128), R("A8", j, j + 128) if m > 64 else R("A8", j, j + 72), R("PL", 0, 8) if m > 64 else R("PL", 8, 16), "cvt")
+                    o = R(pd, j - a0, e - a0)
+                    ds += [(o, R("VT", d0, d0 + 128), eye, True, False), (o, R("VT", d0 - 1, d0 + 127), neg, False, True)]
+                    vs.append([(R(pv, 256 + j - a0, 256 + e - a0), R("VT", d0, d0 + 128), eye, True, True)])
+                else:
+                    move(R("VT", d0, d0 + 128), R("A8", j, e), "cvt")
+                    vs.append([(R(pv, 256 + j - a0, 256 + e - a0, 1, g // 2 * 32, g // 2 * 32 + 32),
+                                R("VT", d0 + g - 128 * (g % 2), d0 + g - 128 * (g % 2) + 249, 8), eye, g % 2 == 0, g % 2 == 1) for g in range(8)])
             ck[0] = c
-            ti, a8, vk = (R(b, i0, i1) for b in ("TI", "A8", "VK"))
-            tt(ti, R("pT", 0, n), R("S", i0, i1), OP.mult, name="tt")
-            ts(a8, ti, 8, 255, OP.logical_shift_right, OP.bitwise_and, name="and")
-            move(vk, a8, "cvt")
-            mm([(R("pD", 0, n), whole("DF"), vk, True, True)], "d")
-            mm([(R("pD", 256, 256 + n), whole("PM"), vk, True, True)], "vn")
-            act(R("AB", i0, i1), R("pD", 0, n), AF.Abs, name="abs")
-            act(R("SG", i0, i1), R("AB", i0, i1), AF.Sign, bias=col("CC", 0), accum=col("SUMS", c), name="sign")
-            move(R(V, i0, i1), R("pD", 256, 256 + n), "vcopy")
-            if i0 < HB <= i1:
+            if gp:
+                mm(ds, "d")
+            for v in vs:
+                mm(v, "vn")
+            if not gp:
+                move(R(V, a0, a1), R(pv, 256, 256 + n), "vcopy")
+                mm([(R(pd, 0, n), whole("DF"), R(V, a0, a1), True, True)], "d")
+            act(R("AB", a0, a1), R(pd, 0, n), AF.Abs, name="abs")
+            act(R("SG", a0, a1), R("AB", a0, a1), AF.Sign, bias=col("CC", 0), accum=col("SUMS", c), name="sign")
+            if gp:
+                move(R(V, a0, a1), R(pv, 256, 256 + n), "vcopy")
+            if a0 < HB <= a1:
                 ck[0] = 7
                 send("V", R(V, 0, HB), R("rv%d" % t, 0, HB))
-                rejected(R("pW", 32, 46), 0, 14)
-        ck[0] = 9
+                rejected(R(PLAN["nb"][0], 32, 46), 0, 14)
+                places(0, 14)
+        ck[0] = -1
         pa, nc = col("pW", 64), len(PLAN["pc"])
-        wrap(R("pW", 0, 28), "F4", "VK", 0, 28, "h4", [(R("pW", 0, 28), whole("ID"), R("IB", 0, 28), True, False)])
         mm([(pa, whole("OB"), col("SUMS", c), c == 0, False) for c in range(nc - 1)], "Aa")
         mm([(pa, whole("OB"), col("SUMS", nc - 1), False, True)], "A")
-        ts(R("t1", 32, 60), R("pW", 0, 28), pa, 512.0, OP.add, OP.mult, name="t1")
-        ts(R("t2", 32, 60), R("t1", 32, 60), W - 1, None, OP.bitwise_and, name="t2")
-        tt(R(LS, 0, 14), R("t2", 32, 46), R("rej", 0, 14), OP.add, name="t3")
+        ts(R("t1", 48, 62), R("pW", 0, 14), pa, 512.0, OP.add, OP.mult, name="t1")
+        ts(R("t2", 48, 62), R("t1", 48, 62), W - 1, None, OP.bitwise_and, name="t2")
+        tt(R(LS, 0, 14), R("t2", 48, 62), R("rej", 0, 14), OP.add, name="t3")
         send("L", R(LS, 0, 14), R("rl%d" % t, 0, 14))
-        ck[0] = 8
-        rejected(R("pT", 0, 14), 14, 28)
-        wrap(R("pE0", 0, 28), "F37", "VK", 0, 28, "h37")
-        ts(R("t1", 0, 28), R("pE0", 0, 28), pa, 8.0 * L, OP.add, OP.add, name="k1")
+        places(14, 28)
+        rejected(R(PLAN["nb"][1], 96, 110), 14, 28)
+        ph = R(PLAN["nb"][2], 128, 156)
+        wrap(ph, "F37", V, 0, 28, "h37")
+        ts(R("t1", 28, 42), R("pW", 14, 28), pa, 512.0, OP.add, OP.mult, name="e1")
+        ts(R("t2", 28, 42), R("t1", 28, 42), W - 1, None, OP.bitwise_and, name="e2")
+        tt(R("NL", 28, 42), R("t2", 28, 42), R("rej", 14, 28), OP.add, name="e3")
+        ts(R("t1", 0, 28), ph, pa, 8.0 * L, OP.add, OP.add, name="k1")
         ts(R("t2", 0, 28), R("t1", 0, 28), W - 1, None, OP.bitwise_and, name="k2")
         tt(R("dl", 0, 28), R("rej", 0, 28), R("MC", 0, 28), OP.mult, name="dl")
         tt(R("NL", 0, 28), R("t2", 0, 28), R("dl", 0, 28), OP.max, name="k3")
-        tt(R("NL", 28, 42), R("t2", 46, 60), R("rej", 14, 28), OP.add, name="e3")
         for c, (j, e) in enumerate(cuts(PLAN["bg"])):
             ck[0] = c
-            gat(R("GB", 16 * j, 16 * e), R(Bo, 0, W), R(C, j, e), "BG")
+            if e > j:
+                gat(R("GB", 16 * j, 16 * e), R(Bo, 0, W), R(C, j, e), "BG")
         for c, (i0, i1) in enumerate(cuts(PLAN["bc"])):
             n, g0, ck[0], first = i1 - i0, 16 * i0, c, len(ops)
             pb = R(PLAN["bb"][c], 0, n)
-            bl = ([(pb, whole("NI"), R(CF, i0, i1), True, False)]
-                  + [(R(pb[0], 0, n, 1, k // 4 * 32, k // 4 * 32 + 32), R("SL", 32 * k, 32 * k + 32), R("GB", g0 + k, 16 * i1, 16), False, k % 4 == 3)
-                     for k in range(1, 16)])
-            for j in range(0, 16, 4):
+            bl = [(pb, R("SL", 128 * k, 128 * k + 128), R("GB", g0 + k, 16 * i1, 16), k == 1, False) for k in range(1, 16)]
+            for j in range(0, 15, 4):
                 mm(bl[j:j + 4], "BX")
-            sg, pm = R("SG", i0, i1), R(pb[0], 256, 256 + n)
-            tt(R("M2", i0, i1), pb, sg, OP.min, name="m2")
-            mm([(pm, whole("ID"), R(CF, i0, i1), True, False), (pm, whole("IA"), sg, False, False),
-                (pm, whole("IB4"), R("M2", i0, i1), False, True)], "mend")
-            affine(R(Bn, MEND + i0, MEND + i1), pm, 1.0, 2048.0, "mendc")
+            mm([(pb, whole("IA"), R("SG", i0, i1), False, True)], "mend")
+            tt(R(Bn, MEND + i0, MEND + i1), pb, R(CF, i0, i1), OP.min, name="m2")
             if i0 >= PLAN["defer"]:
                 for o in ops[first:]:
                     o.update(dict(rd=t + 1) if t < NT - 1 else dict(name="z" + o["name"]))
-        ck[0] = 9
+        ck[0] = -1
         xs, bs = R("X", 0, XW), R(Bn, 0, MEND)
         ls, rl = R("NL", 28, 42), R("rl%d" % t, 0, 14)
         sca(xs, ls, R(V, HB, L), "XS even")
-        sca(bs, ls, R(C, HB, L), "BS even")
+        sca(bs, ls, R(CF, HB, L), "BS even")
         z = "z" * (t == NT - 1)
         sca(xs, rl, R("rv%d" % t, 0, HB), z + "XS odd")
         sca(bs, rl, R("rc%d" % t, 0, HB), z + "BS odd")
+        D = "C%d" % ((t + 1) % 2)
         if t == NT - 1:
             add("y", lambda g, T, X: g.sync.dma_start(T.yx[:, :], T.X[:, 0:W]), [R("X", 0, W)], [], ("fixed", 4.0), ("oyx", 16), "st x")
-            gat(R("YC", 1, L, 2), R(Bn, 0, MEND + HB), R("NL", 0, 14), "out")
-            gat(R("YC", 0, L, 2), whole(Bn), R("NL", 14, 28), "out")
+            for h in range(2):
+                nxt(R(D, HB * h, HB * h + HB), R(Bn, 0, MEND + HB * h + HB), R("NL", 14 * h, 14 * h + 14), "out")
+                move(R("YC", 1 - h, L, 2), R(D, HB * h, HB * h + HB), "yc")
             add("y", lambda g, T, X: g.sync.dma_start(T.yc[:, :], T.YC[:, :]), [R("YC", 0, L)], [], ("fixed", 2.5), ("oyc", 16), "st c")
         else:
-            D = "C%d" % ((t + 1) % 2)
-            for i0, i1 in cuts(PLAN["nx"]):
-                ck[:] = [i0 // 64, t + (i0 >= PLAN["defer"])]
-                gat(R(D, i0, i1), R(Bn, 0, MEND + i1), R("NL", i0 // 16, i1 // 16), "nxt")
+            for c, (i0, i1) in enumerate(cuts(PLAN["nx"])):
+                ck[:] = [c, t + (i0 >= PLAN["defer"])]
+                nxt(R(D, i0, i1), R(Bn, 0, MEND + i1), R("NL", i0 // 16, i1 // 16), "nxt")
     return ops
 
 
@@ -400,7 +441,7 @@ def depend(ops):
 def tags_of(ops):
     seen, out = {}, []
     for o in ops:
-        z = o["name"].replace(" ", "") + (str(o["ck"]) if o["ck"] < 8 else "")
+        z = o["name"].replace(" ", "") + (str(o["ck"]) if o["ck"] >= 0 else "")
         k = seen.get((z, o["rd"]), 0)
         seen[(z, o["rd"])] = k + 1
         out.append(z + ("bcdefghijklmnopqrstuvwxyz"[k - 1] if k and o["rd"] >= 0 else ""))

from concourse.mybir import AluOpType as OP, ActivationFunctionType as AF

N, NT = 4, 4
L, HB, W = 448, 224, 2048
MEND = 4096
BW, XW = MEND + L, 4096
PLAN = {"xg": [52, 76, 52, 76, 52, 76, 64], "bg": [0, 100, 28, 8, 20, 100, 8, 40, 144], "ch": [128, 128, 128, 64],
        "sc": [256, 192], "pc": [256, 192], "perm": ["pe", "g"], "bc": [128, 128, 192], "nx": [128, 128, 192], "defer": 256,
        "pool": ["cvt", "s", "cf", "cBa", "cBb", "cBc", "cBd"], "bb": ["pU2", "pU1", "pU0"], "tb": ["pT"] * 4,
        "db": ["pD", "pU1", "pD", "pD"], "vb": ["pE0", "pD", "pD", "pD"], "nb": ["pE1", "pT", "pE0"]}
ORDER = {
    "v": "ms ki mv ca sa pl cg ce mz SLc m22 md SLb XG1 XG3 y0 XG4 unpk scan0 cb y1 bit1 scan0b scan1b scan1 y2 tt0 bit3 y3 and0 "
         "scan2 scan2b scan3 tt1 ni and1 cd cvt2 BG5 t1 vcopy1 t2 rej7 BG6 t3 BG7 e1 rej e2 m20 e3 k1 dl k2 XSeven k3 zXSodd XSodd "
         "m21 zm22 yc ycb",
    "s": "ldx kf JIb JIa BSl co cv cw SLa XG0 XG2 e0 nxt2 q0 XG5 q1 XG6 unph q2 cc BG2 q3 BG1 BG4 vcopy0 cvt3 BG3 abs0 abs1 sign0 "
         "sign1 BG8 BSeven BSodd nxt0 nxt1 zBSodd out outb",
    "t": "BX2 BX2b BX2c BX2d mend2 E0 X0b X0 E1 pen0 pen0b X1 E2 X1b pen1b pen1 E3 Sc0 X2b X2 pen2 pen2b X3 pen3 Sc1 vn0 vn0b BX0 "
         "BX0b d0 d1 BX0c BX0d vn1 h47 Aa vn1b A n7 n h4 mend0 h37 BX1 BX1b BX1c BX1d mend1 zBX2 zBX2b zBX2c zBX2d zmend2",
    "g": "ii id col gc ib dz eb i64 xp df cf sendC cfb s1 cBa s3 cvt0 cvt1 cBc sendV7 cBd late cBb sendL",
    "y": "ldwt ldcb ldpk cpB stx stc"}

F32, B16, I32, U16, H16 = "float32", "bfloat16", "int32", "uint16", "float16"
SCRATCH = {}
for _n, _w, _d in (
        ("X", XW, B16), ("BI", W, I32), ("B0", BW, F32), ("B1", BW, F32), ("pki", 1024, I32), ("cbi", L, I32), ("wti", 8, I32),
        ("C0", L, U16), ("C1", L, U16), ("CF0", L, F32), ("CF1", L, F32), ("G", 16 * L, B16), ("GB", 16 * L, H16), ("SO", 4096, F32),
        ("QI", L, I32), ("Y", L, B16), ("BT", L, I32), ("S", L, B16), ("TI", L, I32), ("A8", 512, I32), ("VT", 1408, B16),
        ("V0", L, B16), ("V1", L, B16), ("AB", L, B16), ("SG", L, B16), ("YC", L, F32),
        ("SUMS", 8, F32), ("rej", 32, F32), ("dl", 32, F32), ("t1", 64, I32), ("t2", 64, I32),
        ("LS0", 16, U16), ("LS1", 16, U16), ("NL", 48, U16), ("PL", 16, U16), ("PF", 16, F32),
        ("II", 8, I32), ("FF", 8, F32), ("CC", 16, F32), ("WI", 8, I32), ("COL", 144, F32), ("GC", 128, F32),
        ("DZ", 512, F32), ("IB0", 32, F32), ("IB", 32, H16), ("MC0", 32, F32), ("MC", 32, F32),
        ("ONE", 256, B16), ("SA", 128, B16), ("SB", 128, B16), ("DF", 128, B16), ("EIG", 144, B16), ("EB", 144, B16), ("E0", 8, B16),
        ("XP0", 64, B16), ("XP", 64, B16), ("I640", 64, B16), ("I64", 64, B16), ("N64", 64, B16), ("JI", 1024, B16), ("NI", 128, B16),
        ("FK", 144, B16), ("F4", 144, B16), ("F37", 144, H16), ("OB", 128, F32), ("ID", 128, B16),
        ("SL", 2048, B16), ("IA0", 128, B16), ("IA", 128, B16), ("KM", 16, F32)):
    SCRATCH[_n] = ("sbuf", [128, _w], _d)
for _t in range(NT):
    SCRATCH["rc%d" % _t] = ("sbuf", [128, HB], F32)
    SCRATCH["rv%d" % _t] = ("sbuf", [128, HB], B16)
    SCRATCH["rl%d" % _t] = ("sbuf", [128, 16], U16)
for _n in ("pE0", "pE1", "pU0", "pU1", "pU2", "pT", "pD", "pW"):
    SCRATCH[_n] = ("psum", [128, 512], F32)
SEMAPHORES = (["qv", "qs", "qt", "qg", "dcb", "dx", "dpk", "dwt", "oyx", "oyc"] + ["dcp%d" % t for t in range(1, NT)]
              + [a + b + str(t) for a in "rl" for b in "CVL" for t in range(NT)])


def R(buf, c0, c1, step=1, p0=0, p1=128):
    return (buf, c0, c1, step, p0, p1)


def ap(T, a):
    buf, c0, c1, step, p0, p1 = a
    if step == 1:
        return T[buf][p0:p1, c0:c1]
    return T[buf][p0:p1, c0:c1:step]


def val(T, s):
    return ap(T, s) if isinstance(s, tuple) else s


def cuts(sizes):
    out, a = [], 0
    for n in sizes:
        out.append((a, a + n))
        a += n
    return out


def build_ops(nsig):
    ops, ck = [], [-1, -1]

    def add(eng, fn, reads, writes, el, tok=None, name="", after=()):
        ops.append(dict(eng=eng, fn=fn, reads=list(reads), writes=list(writes), el=el, tok=tok, name=name, after=list(after), ck=ck[0], rd=ck[1]))
        return len(ops) - 1

    def ne(a):
        return -((a[1] - a[2]) // a[3])

    def half(*sides):
        return 0.5 if all(SCRATCH[s[0]][2] in (B16, H16, U16) for s in sides) else 1.0

    def both(out, reads, fv, fs, name, kind="plain"):
        n = ne(out)
        add("vs", {"v": fv, "s": fs}, reads, [out], {"v": (kind, n * (half(out, reads[0]) if kind == "plain" else 1)), "s": (kind, n)}, name=name)

    def ts(out, in0, s1, s2, op0, op1=None, name="ts"):
        def fn(g, T, X):
            if op1 is None:
                return g.vector.tensor_scalar(ap(T, out), ap(T, in0), val(T, s1), None, op0)
            return g.vector.tensor_scalar(ap(T, out), ap(T, in0), val(T, s1), val(T, s2), op0, op1)
        add("v", fn, [in0] + [s for s in (s1, s2) if isinstance(s, tuple)], [out], ("plain", ne(out) * half(out, in0)), name=name)

    def tt(out, a, b, op, name="tt"):
        cyc = 1.0 if "psum" in (SCRATCH[a[0]][0], SCRATCH[b[0]][0]) else 2.0
        add("v", lambda g, T, X: g.vector.tensor_tensor(ap(T, out), ap(T, a), ap(T, b), op), [a, b], [out], ("plain", ne(out) * cyc), name=name)

    def ms(out, x, name):
        add("v", lambda g, T, X: g.vector.memset(ap(T, out), x), [], [out], ("plain", ne(out) * half(out)), name=name)

    def act(out, in_, func, bias=0.0, accum=None, name="act"):
        def fn(g, T, X):
            if accum is None:
                return g.scalar.activation(ap(T, out), ap(T, in_), func, bias=val(T, bias))
            return g.scalar.activation(ap(T, out), ap(T, in_), func, bias=val(T, bias), accum_out=ap(T, accum))
        add("s", fn, [in_] + ([bias] if isinstance(bias, tuple) else []), [out] + ([accum] if accum else []), ("plain", ne(out)), name=name)

    def move(out, in_, name):
        both(out, [in_], lambda g, T, X: g.vector.tensor_copy(ap(T, out), ap(T, in_)),
             lambda g, T, X: g.scalar.activation(ap(T, out), ap(T, in_), AF.Copy), name)
        if name in PLAN["pool"]:
            ops[-1]["eng"] = "vsg"
            ops[-1]["el"]["g"] = ("pool", ne(out))
            ops[-1]["fn"]["g"] = lambda g, T, X: g.affine_select(ap(T, out), ap(T, in_), [[0, ne(out)]], OP.is_ge, 0.0, 0, 0)

    def affine(out, in_, scale, bias, name):
        both(out, [in_], lambda g, T, X: g.vector.tensor_scalar(ap(T, out), ap(T, in_), scale, bias, OP.mult, OP.add),
             lambda g, T, X: g.scalar.activation(ap(T, out), ap(T, in_), AF.Copy, bias=bias, scale=scale), name)

    def scaled(out, base, by, name):
        both(out, [base] + ([by] if isinstance(by, tuple) else []),
             lambda g, T, X: g.vector.tensor_scalar(ap(T, out), ap(T, base), val(T, by), None, OP.mult),
             lambda g, T, X: g.scalar.activation(ap(T, out), ap(T, base), AF.Copy, scale=val(T, by)), name)

    def gat(out, win, off, name):
        both(out, [win, off], lambda g, T, X: g.vector.tensor_copy(ap(T, out), ap(T, win).indirect(ap(T, off))),
             lambda g, T, X: g.scalar.activation(ap(T, out), ap(T, win).indirect(ap(T, off)), AF.Copy), name, "gat")

    def sca(win, off, in_, name):
        fn = {"v": lambda g, T, X: g.vector.tensor_copy(ap(T, win).indirect(ap(T, off)), ap(T, in_)),
              "s": lambda g, T, X: g.scalar.activation(ap(T, win).indirect(ap(T, off)), ap(T, in_), AF.Silu)}
        add("vs" if SCRATCH[win[0]][2] == F32 else "v", fn, [in_, off], [win], {q: ("sca", ne(in_)) for q in "vs"}, name=name)

    def nxt(out, win, off, name):
        add("s", lambda g, T, X: g.scalar.activation(ap(T, out), ap(T, win).indirect(ap(T, off)), AF.Abs), [win, off], [out], ("gat", ne(out)), name=name)

    def mm(lst, name):
        def fn(g, T, X):
            i = None
            for o, l, r, a, b in lst:
                i = g.tensor.matmul(ap(T, o), ap(T, l), ap(T, r), a, b)
            return i
        cyc = sum(max(min(64, ne(l)), ne(r)) * (4 if SCRATCH[l[0]][2] == F32 else 1) for _o, l, r, _a, _b in lst)
        add("t", fn, [x for m in lst for x in (m[1], m[2])], [m[0] for m in lst], ("pe", cyc), name=name)

    def iota(out, pat, base, cm, name, f32=True):
        def fn(g, T, X):
            if f32:
                return g.iota(ap(T, out), pat, base, cm, allow_small_or_imprecise_dtypes=True)
            return g.iota(ap(T, out), pat, base, cm)
        add("g", fn, [], [out], ("pool", ne(out)), name=name)

    def where(out, in_, pat, base, fill=None, cm=1, name="where"):
        op = OP.is_equal if fill is None else OP.not_equal
        add("g", lambda g, T, X: g.affine_select(ap(T, out), ap(T, in_), pat, op, fill or 0.0, base, cm), [in_], [out], ("pool", ne(out)), name=name)

    def col(b, j=0):
        return R(b, j, j + 1)

    def whole(b):
        return R(b, 0, SCRATCH[b][1][1])

    add("y", lambda g, T, X: g.sync.dma_start(T.cbi[:, :], T.cb[:, :]), [], [R("cbi", 0, L)], ("fixed", 2.5), ("dcb", 16), "ld cb")
    add("sd", lambda g, T, X: g.scalar.dma_start(T.X[:, 0:W], T.x[:, :]), [], [R("X", 0, W)], ("fixed", 4.5), ("dx", 16), "ld x")
    add("y", lambda g, T, X: g.sync.dma_start(T.wti[:, 0:1], T.wt[:, :]), [], [col("wti")], ("fixed", 2.0), ("dwt", 16), "ld wt")
    add("y", lambda g, T, X: g.sync.dma_start(T.pki[:, :], T.pk[:, :]), [], [R("pki", 0, 1024)], ("fixed", 5.0), ("dpk", 16), "ld pk")
    ms(whole("EIG"), 0.125, "ms")
    ms(whole("ONE"), 1.0, "ms")
    iota(col("II", 0), [[1, 1]], 0, 1, "ii", False)
    iota(whole("COL"), [[1, 144]], 0, 0, "col")
    where(R("EB", 0, 136), R("EIG", 0, 136), [[-1, 17], [-16, 8]], 1, name="eb")
    ms(R("EB", 0, 8), 0.0, "md")
    scaled(whole("E0"), R("EB", 8, 16), 32768.0, "e0")
    so = 0
    for n in PLAN["ch"]:
        if n > 64:
            ms(R("SO", so, so + 64), 1.0 / 16, "mz")
        so += 8 * n
    ms(R("VT", 0, 256 * len(PLAN["ch"])), 0.0, "mv")
    where(whole("XP0"), R("EIG", 0, 64), [[-16, 8], [-1, 8]], 0, name="xp")
    where(whole("XP"), whole("XP0"), [[-16, 8], [-1, 8]], -8, 32.0, name="xp")
    where(whole("I640"), R("ONE", 0, 64), [[-1, 64]], 0, name="i64")
    where(whole("I64"), whole("I640"), [[-1, 64]], -64, 1.0, name="i64")
    where(whole("ID"), R("ONE", 0, 128), [[-1, 128]], 0, name="id")
    scaled(whole("NI"), whole("ID"), -1.0, "ni")
    scaled(whole("N64"), whole("I64"), -1.0, "ni")
    scaled(whole("SA"), whole("ID"), 2048.0, "sa")
    scaled(whole("SB"), whole("ID"), -2040.0, "sa")
    where(whole("DF"), whole("ID"), [[-1, 128]], 1, -1.0, name="df")
    iota(whole("DZ"), [[0, 64], [16384, 8]], -8192, 0, "dz")
    iota(whole("GC"), [[1, 8], [0, 16]], 0, 0, "gc")
    iota(R("IB0", 0, 28), [[-1, 2], [32, 14]], 1, 0, "ib")
    iota(R("MC0", 0, 28), [[16, 28]], MEND, 0, "ib")
    ts(col("II", 1), col("II", 0), 15, None, OP.bitwise_and, name="ki")
    ts(col("II", 2), col("II", 0), 4, None, OP.logical_shift_right, name="ki")
    move(R("FF", 0, 3), R("II", 0, 3), "kf")
    pf, kf, gf = (col("FF", j) for j in range(3))
    move(R("C0", 0, HB), R("cbi", 1, L, 2), "co")
    move(R("C0", HB, L), R("cbi", 0, L, 2), "cv")
    for j in range(1, 8):
        scaled(R("JI", 128 * j, 128 * j + 128), whole("ID"), float(j * 2 ** 17), "JI" + "ab"[j % 2])
    ms(R("DZ", 0, 512, 8), -float(2 ** 24), "mz")
    ts(col("CC", 6), kf, 0.5, -1024.0, OP.is_lt, OP.mult, name="ca")
    affine(col("CC", 0), col("CC", 6), 1.0, -80.5, "ca")
    affine(col("CC", 1), gf, 16.0, 15.0, "ca")
    affine(col("CC", 3), kf, 2.0, 0.0, "ca")
    affine(col("CC", 7), col("CC", 6), 2.0, 0.0, "ca")
    affine(col("CC", 8), kf, 8.0, 0.0, "ca")
    affine(col("WI", 2), col("wti"), 37.0, 0.0, "cw")
    ts(col("WI", 0), col("wti"), 3, None, OP.bitwise_and, name="cb")
    ts(col("WI", 1), col("WI", 2), W - 1, None, OP.bitwise_and, name="cb")
    ts(whole("FK"), whole("COL"), col("CC", 1), 8.0, OP.is_equal, OP.mult, name="ce")
    move(R("CC", 4, 6), R("WI", 0, 2), "cc")
    ts(whole("F4"), whole("COL"), col("CC", 1), col("CC", 4), OP.is_equal, OP.mult, name="cd")
    ts(whole("F37"), whole("COL"), col("CC", 1), col("CC", 5), OP.is_equal, OP.mult, name="cd")
    ts(R("IB", 0, 28), R("IB0", 0, 28), col("CC", 3), 1.0 / 512, OP.add, OP.mult, name="ce")
    ts(whole("OB"), whole("GC"), gf, 0.5, OP.is_equal, OP.mult, name="cg")
    ts(R("MC", 0, 28), R("MC0", 0, 28), kf, 1.0 / 2048, OP.add, OP.mult, name="cg")
    ts(whole("IA0"), whole("GC"), gf, col("CC", 7), OP.is_equal, OP.mult, name="cg")
    where(whole("IA"), whole("IA0"), [[-1, 128]], 0, -2048.0, name="late")
    ms(R("A8", L, L + 8), 0, "mv")
    ts(R("PF", 0, 8), R("COL", 0, 8), col("CC", 8), None, OP.add, name="pl")
    ts(col("CC", 9), pf, 63.5, -64.0, OP.is_gt, OP.mult, name="pl")
    ts(R("PF", 8, 16), R("PF", 0, 8), col("CC", 9), 64.0, OP.add, OP.min, name="pl")
    ts(R("PF", 0, 8), R("PF", 8, 16), 0.0, 1000.0, OP.is_lt, OP.mult, name="pl")
    tt(R("PF", 8, 16), R("PF", 8, 16), R("PF", 0, 8), OP.add, name="pl")
    ts(R("PL", 8, 16), R("PF", 8, 16), 64.0, None, OP.min, name="pl")
    act(R("PL", 0, 8), R("COL", 0, 8), AF.Silu, bias=col("CC", 8), name="BSl")
    ts(whole("KM"), R("COL", 0, 16), kf, -1.0, OP.is_equal, OP.mult, name="cg")
    for k in range(1, 16):
        scaled(R("SL", 128 * k, 128 * k + 128), whole("ID"), col("KM", k), "SL" + "abc"[k % 3])
    ts(R("BI", 0, 1024), whole("pki"), W - 1, None, OP.bitwise_and, name="unpk")
    affine(R("BI", 1024, 2048), whole("pki"), 1.0 / W, -0.5 + 0.5 / W, "unph")
    for j in range(4):
        move(R("B1", 512 * j, 512 * j + 512), R("BI", 512 * j, 512 * j + 512), "cB" + "abcd"[j])

    xw = R("X", 0, W)
    ub = ["pU0", "pU1", "pU2"]
    chunks = cuts(PLAN["ch"])

    for t in range(NT):
        C, CF, V, LS = "C%d" % (t % 2), "CF%d" % (t % 2), "V%d" % (t % 2), "LS%d" % (t % 2)
        Bo, Bn = "B%d" % (t % 2) if t else "BI", "B%d" % ((t + 1) % 2)
        un = 0

        def send(what, src, dst, t=t):
            def fn(g, T, X):
                rid, pid, m = X[t]
                return g.remote_dma(ap(T, dst), ap(T, src), T.sem["r%s%d" % (what, t)], T.sem["l%s%d" % (what, t)], pid, rid, m)
            i = add("g", fn, [src], [], ("fixed", 0.6), ("l%s%d" % (what, t), nsig), "send " + what)
            add("x", None, [], [dst], ("fixed", 2.2), ("r%s%d" % (what, t), nsig), "recv " + what, [i])

        def wrap(out, lh, src, a0, a1, name, first=()):
            mm(list(first) + [(out, R(lh, 15 - b, 143 - b), R(src, 16 * a0 + b, 16 * a1, 16), b == 0 and not first, b == 15)
                              for b in range(16)], name)

        def rejected(pn, a0, a1):
            wrap(pn, "FK", "SG", a0, a1, "n")
            ts(R("rej", a0, a1), pn, -40.0, 2048.0, OP.is_gt, OP.mult, name="rej")

        def places(a0, a1):
            wrap(R("pW", a0, a1), "F4", V, a0, a1, "h4", [(R("pW", a0, a1), whole("ID"), R("IB", a0, a1), True, False)])

        ck[:] = [-1, t]
        move(R(CF, 0, HB), R(C, 0, HB), "cf")
        move(R(CF, HB, L), R(C, HB, L), "cf")
        send("C", R(CF, 0, HB), R("rc%d" % t, 0, HB))
        for c, (j, e) in enumerate(cuts(PLAN["xg"])):
            ck[0] = c
            if e > j:
                gat(R("G", 16 * j, 16 * e), xw, R(C, j, e), "XG")
        ck[0] = -1
        if t:
            add("y", lambda g, T, X, a=R(Bn, 0, W), b=R(Bo, 0, W): g.sync.dma_start(ap(T, a), ap(T, b)), [R(Bo, 0, W)], [R(Bn, 0, W)],
                ("fixed", 6.0), ("dcp%d" % t, 16), "cp B")
        for c, (i0, i1) in enumerate(chunks):
            n, ck[0], pe = i1 - i0, c, "pE%d" % (c % 2)
            es = []
            for k in range(1, 16):
                p0, c0 = (64 * (k // 8), 8 * (k % 8)) if n == 64 else (0, 8 * k)
                z = 8 * (k == 1)
                es.append((R(pe, c0 - z, c0 + 8, 1, p0, p0 + n), R("G", 16 * i0 + k - 1, 16 * i1, 16), R("EB", 8 * k - z, 8 * k + 8), True, True))
            mm(es, "E")
            q, y = R("QI", i0, i1), R("Y", i0, i1)
            affine(q, R(pe, 0, n), 1.0, -0.4375, "q")
            tt(y, R(pe, 0, n), q, OP.subtract, name="y")
            for a0, a1 in cuts(PLAN["sc"]):
                if a1 == i1:
                    ts(R("BT", a0, a1), R("QI", a0, a1), 1, None, OP.bitwise_and, name="bit")
                    move(R("S", a0, a1), R("BT", a0, a1), "s")
        for c, (i0, i1) in enumerate(chunks):
            n, g0, ck[0] = i1 - i0, 16 * i0, c
            for hs in ([(0,), (1,)] if n > 64 else [(0, 1)]):
                u = ub[un % 3]
                un += 1
                k0 = int(hs == (0,))
                xs = []
                for h in hs:
                    p0 = 64 * h if len(hs) == 2 else 0
                    xs += [(R(u, 64 * k, 64 * k + 64, 1, p0, p0 + n), R("G", g0 + 8 * h + k, 16 * i1, 16), whole("XP"), k == k0, False)
                           for k in range(k0, 8)]
                mm(xs, "X")
                y0 = i0 + 64 * hs[0]
                mm([(R(u, 64 * k0 + j, 512, 8), R("JI", 128 * j, 128 * j + 128), R("Y", y0 + 8 * k0, y0 + 64), False, j == 7) for j in range(1, 8)], "pen")
                o, ui, dz = R("SO", 8 * y0 + 64 * k0, 8 * y0 + 512), R(u, 64 * k0, 512), R("DZ", 64 * k0, 512)
                add("v", lambda g, T, X, o=o, ui=ui, dz=dz: g.vector.tensor_tensor_scan(ap(T, o), ap(T, dz), ap(T, ui), 0.0, OP.add, OP.max),
                    [ui, dz], [o], ("plain", ne(o)), name="scan")
            if i1 not in [e for _j, e in cuts(PLAN["pc"])]:
                continue
            c, (a0, a1) = [p for p in enumerate(cuts(PLAN["pc"])) if p[1][1] == i1][0]
            mine = [(x, j, e) for x, (j, e) in enumerate(chunks) if a0 <= j < a1]
            n, ck[0], gp = a1 - a0, c, PLAN["perm"][c] == "g"
            pT, pd, pv = PLAN["tb"][c], PLAN["db"][c], PLAN["vb"][c]
            sl = [(R(pT, 0, n), whole("SA"), R("ONE", 0, n), True, False), (R(pT, 0, n), whole("SB"), R("S", a0, a1), False, False)]
            sl += [(R(pT, j - a0, j - a0 + 8), R("G", 16 * j, 16 * e, 16), whole("E0"), False, False) for x, j, e in mine if e - j > 64]
            sl[-1] = sl[-1][:4] + (True,)
            mm(sl, "Sc")
            tt(R("TI", a0, a1), R("SO", 8 * a0 + 7, 8 * a1, 8), R(pT, 0, n), OP.mult, name="tt")
            ts(R("A8", a0, a1), R("TI", a0, a1), 8, 255, OP.logical_shift_right, OP.bitwise_and, name="and")
            ds, vs = [], []
            for x, j, e in mine:
                ck[0], m, d0 = x, e - j, 128 + 256 * x
                eye, neg = (whole("ID"), whole("NI")) if m > 64 else (whole("I64"), whole("N64"))
                if gp:
                    gat(R("VT", d0, d0 + 128), R("A8", j, j + 128) if m > 64 else R("A8", j, j + 72), R("PL", 0, 8) if m > 64 else R("PL", 8, 16), "cvt")
                    o = R(pd, j - a0, e - a0)
                    ds += [(o, R("VT", d0, d0 + 128), eye, True, False), (o, R("VT", d0 - 1, d0 + 127), neg, False, True)]
                    vs.append([(R(pv, 256 + j - a0, 256 + e - a0), R("VT", d0, d0 + 128), eye, True, True)])
                else:
                    move(R("VT", d0, d0 + 128), R("A8", j, e), "cvt")
                    vs.append([(R(pv, 256 + j - a0, 256 + e - a0, 1, g // 2 * 32, g // 2 * 32 + 32),
                                R("VT", d0 + g - 128 * (g % 2), d0 + g - 128 * (g % 2) + 249, 8), eye, g % 2 == 0, g % 2 == 1) for g in range(8)])
            ck[0] = c
            if gp:
                mm(ds, "d")
            for v in vs:
                mm(v, "vn")
            if not gp:
                move(R(V, a0, a1), R(pv, 256, 256 + n), "vcopy")
                mm([(R(pd, 0, n), whole("DF"), R(V, a0, a1), True, True)], "d")
            act(R("AB", a0, a1), R(pd, 0, n), AF.Abs, name="abs")
            act(R("SG", a0, a1), R("AB", a0, a1), AF.Sign, bias=col("CC", 0), accum=col("SUMS", c), name="sign")
            if gp:
                move(R(V, a0, a1), R(pv, 256, 256 + n), "vcopy")
            if a0 < HB <= a1:
                ck[0] = 7
                send("V", R(V, 0, HB), R("rv%d" % t, 0, HB))
                rejected(R(PLAN["nb"][0], 32, 46), 0, 14)
                places(0, 14)
        ck[0] = -1
        pa, nc = col("pW", 64), len(PLAN["pc"])
        mm([(pa, whole("OB"), col("SUMS", c), c == 0, False) for c in range(nc - 1)], "Aa")
        mm([(pa, whole("OB"), col("SUMS", nc - 1), False, True)], "A")
        ts(R("t1", 48, 62), R("pW", 0, 14), pa, 512.0, OP.add, OP.mult, name="t1")
        ts(R("t2", 48, 62), R("t1", 48, 62), W - 1, None, OP.bitwise_and, name="t2")
        tt(R(LS, 0, 14), R("t2", 48, 62), R("rej", 0, 14), OP.add, name="t3")
        send("L", R(LS, 0, 14), R("rl%d" % t, 0, 14))
        places(14, 28)
        rejected(R(PLAN["nb"][1], 96, 110), 14, 28)
        ph = R(PLAN["nb"][2], 128, 156)
        wrap(ph, "F37", V, 0, 28, "h37")
        ts(R("t1", 28, 42), R("pW", 14, 28), pa, 512.0, OP.add, OP.mult, name="e1")
        ts(R("t2", 28, 42), R("t1", 28, 42), W - 1, None, OP.bitwise_and, name="e2")
        tt(R("NL", 28, 42), R("t2", 28, 42), R("rej", 14, 28), OP.add, name="e3")
        ts(R("t1", 0, 28), ph, pa, 8.0 * L, OP.add, OP.add, name="k1")
        ts(R("t2", 0, 28), R("t1", 0, 28), W - 1, None, OP.bitwise_and, name="k2")
        tt(R("dl", 0, 28), R("rej", 0, 28), R("MC", 0, 28), OP.mult, name="dl")
        tt(R("NL", 0, 28), R("t2", 0, 28), R("dl", 0, 28), OP.max, name="k3")
        for c, (j, e) in enumerate(cuts(PLAN["bg"])):
            ck[0] = c
            if e > j:
                gat(R("GB", 16 * j, 16 * e), R(Bo, 0, W), R(C, j, e), "BG")
        for c, (i0, i1) in enumerate(cuts(PLAN["bc"])):
            n, g0, ck[0], first = i1 - i0, 16 * i0, c, len(ops)
            pb = R(PLAN["bb"][c], 0, n)
            bl = [(pb, R("SL", 128 * k, 128 * k + 128), R("GB", g0 + k, 16 * i1, 16), k == 1, False) for k in range(1, 16)]
            for j in range(0, 15, 4):
                mm(bl[j:j + 4], "BX")
            mm([(pb, whole("IA"), R("SG", i0, i1), False, True)], "mend")
            tt(R(Bn, MEND + i0, MEND + i1), pb, R(CF, i0, i1), OP.min, name="m2")
            if i0 >= PLAN["defer"]:
                for o in ops[first:]:
                    o.update(dict(rd=t + 1) if t < NT - 1 else dict(name="z" + o["name"]))
        ck[0] = -1
        xs, bs = R("X", 0, XW), R(Bn, 0, MEND)
        ls, rl = R("NL", 28, 42), R("rl%d" % t, 0, 14)
        sca(xs, ls, R(V, HB, L), "XS even")
        sca(bs, ls, R(CF, HB, L), "BS even")
        z = "z" * (t == NT - 1)
        sca(xs, rl, R("rv%d" % t, 0, HB), z + "XS odd")
        sca(bs, rl, R("rc%d" % t, 0, HB), z + "BS odd")
        D = "C%d" % ((t + 1) % 2)
        if t == NT - 1:
            add("y", lambda g, T, X: g.sync.dma_start(T.yx[:, :], T.X[:, 0:W]), [R("X", 0, W)], [], ("fixed", 4.0), ("oyx", 16), "st x")
            for h in range(2):
                nxt(R(D, HB * h, HB * h + HB), R(Bn, 0, MEND + HB * h + HB), R("NL", 14 * h, 14 * h + 14), "out")
                move(R("YC", 1 - h, L, 2), R(D, HB * h, HB * h + HB), "yc")
            add("y", lambda g, T, X: g.sync.dma_start(T.yc[:, :], T.YC[:, :]), [R("YC", 0, L)], [], ("fixed", 2.5), ("oyc", 16), "st c")
        else:
            for c, (i0, i1) in enumerate(cuts(PLAN["nx"])):
                ck[:] = [c, t + (i0 >= PLAN["defer"])]
                nxt(R(D, i0, i1), R(Bn, 0, MEND + i1), R("NL", i0 // 16, i1 // 16), "nxt")
    return ops


def hit(a, b):
    if a[3] == b[3] > 1 and (a[1] - b[1]) % a[3]:
        return False
    return a[0] == b[0] and a[1] < b[2] and b[1] < a[2] and a[4] < b[5] and b[4] < a[5]


def depend(ops):
    hist, deps = {}, []
    for i, o in enumerate(ops):
        d = {a: True for a in o["after"]}
        acc = [(r, False) for r in o["reads"]] + [(w, True) for w in o["writes"]]
        for r, wr in acc:
            ps = SCRATCH[r[0]][0] == "psum"
            for j, q, qw in hist.get(r[0], []):
                if j == i:
                    continue
                same = ops[j]["eng"] == o["eng"] and o["eng"] in ("t", "v", "s", "g")
                over = hit(r, q) and (wr or qw)
                if same and o["eng"] == "t":
                    if over or ps:
                        d[j] = d.get(j, False)
                elif over or (ps and not same):
                    d[j] = True
        deps.append(d)
        for r, wr in acc:
            h = hist.setdefault(r[0], [])
            if wr and SCRATCH[r[0]][0] != "psum" and r[3] == 1:
                h[:] = [e for e in h if e[0] == i or not (e[1][1] >= r[1] and e[1][2] <= r[2] and e[1][4] >= r[4] and e[1][5] <= r[5])]
            h.append((i, r, wr))
            if SCRATCH[r[0]][0] == "psum":
                del h[:-80]
    return deps


def tags_of(ops):
    seen, out = {}, []
    for o in ops:
        z = o["name"].replace(" ", "") + (str(o["ck"]) if o["ck"] >= 0 else "")
        k = seen.get((z, o["rd"]), 0)
        seen[(z, o["rd"])] = k + 1
        out.append(z + ("bcdefghijklmnopqrstuvwxyz"[k - 1] if k and o["rd"] >= 0 else ""))
    return out


def schedule(ops, deps):
    n, tags = len(ops), tags_of(ops)
    seq = {q: [i for t in range(NT) for z in ORDER[q].split() for i in range(n) if tags[i] == z and max(ops[i]["rd"], 0) == t]
           for q in ORDER}
    seq.update({i: [i] for i in range(n) if ops[i]["eng"] == "x"})
    done, order = set(), []
    while len(order) < n:
        before = len(order)
        for q, v in seq.items():
            while v and all(j in done for j in deps[v[0]]):
                done.add(v[0])
                order.append((v.pop(0), q if q in ORDER else "x"))
        assert len(order) > before
    return order


_plan = {}


def plan(nsig):
    if nsig in _plan:
        return _plan[nsig]
    ops = build_ops(nsig)
    deps = depend(ops)
    order = schedule(ops, deps)
    sem = {"v": "qv", "s": "qs", "t": "qt", "g": "qg"}
    cnt, known, tok, snap, out = {}, {q: {} for q in "vstgy"}, {}, {}, []
    for i, q in order:
        o = ops[i]
        if q == "x":
            tok[i] = o["tok"]
            cnt[o["tok"][0]] = o["tok"][1]
            snap[i] = {o["tok"][0]: o["tok"][1]}
            continue
        kn, top = known[q], {}
        for j in sorted((j for j, w in deps[i].items() if w), reverse=True):
            s, v = tok[j]
            if kn.get(s, 0) < v:
                top[s] = max(top.get(s, 0), v)
                for a, b in snap[j].items():
                    if kn.get(a, 0) < b:
                        kn[a] = b
        if o["tok"]:
            tok[i] = o["tok"]
            cnt[o["tok"][0]] = o["tok"][1]
        else:
            s = sem[q]
            cnt[s] = cnt.get(s, 0) + 1
            tok[i] = (s, cnt[s])
        snap[i] = dict(kn)
        snap[i][tok[i][0]] = tok[i][1]
        out.append((q, o, sorted(top.items()), tok[i]))
    _plan[nsig] = (out, cnt)
    return _plan[nsig]


def rank_program(g, core, T, topo):
    rank = T.rank_of(core)
    if rank is None:
        return
    X = []
    for t in range(NT):
        d = T.cores[(rank + 1 + t % (N - 1)) % N]
        rid, pid = topo.addr(d, core)
        X.append((rid, pid, topo.mask(core, d)))
    out, cnt = plan(len(topo.engines(core, T.cores[(rank + 1) % N])))
    queue = {"v": g.vector, "s": g.scalar, "t": g.tensor, "g": g, "y": g.sync}
    for q, o, waits, tk in out:
        for s, v in waits:
            queue[q].wait_ge(T.sem[s], v)
        fn = o["fn"][q] if isinstance(o["fn"], dict) else o["fn"]
        ins = fn(g, T, X)
        if o["tok"] is None:
            ins.then_inc(T.sem[tk[0]], 1)
        elif o["name"][:4] != "send":
            ins.then_inc(T.sem[tk[0]], tk[1])
    for s, v in sorted(cnt.items()):
        g.wait_ge(T.sem[s], v)
